import numpy as np, ml_dtypes
CORES = [16,18,20,22]
N = 4
import mx_ref
BF = ml_dtypes.bfloat16
def gcols(t, e):
    v = np.concatenate([t.reshape(8, 16, -1, 4), np.zeros((8, 16, 1, 4), BF)], axis=2)
    return np.ascontiguousarray(np.stack([v[g][:, e[g]] for g in range(8)])).reshape(128, -1)
def tile(rs):
    return np.stack(rs, axis=2).reshape(128, -1).astype(BF)
def pick(q, e):
    c = np.concatenate([q[0].reshape(128, -1, 4), np.zeros((128, 1, 4), np.uint8)], axis=1); s = np.concatenate([q[1], np.ones((16, 1), np.uint8)], axis=1)
    return (np.ascontiguousarray(c[:, e].reshape(128, -1)), np.ascontiguousarray(s[:, e]))
def join(*qs):
    return (np.concatenate([q[0] for q in qs], axis=1), np.concatenate([q[1] for q in qs], axis=1))
def put(q, e, v):
    c, s = q[0].reshape(128, -1, 4).copy(), q[1].copy(); c[:, e] = v[0].reshape(128, -1, 4); s[:, e] = v[1]
    return (c.reshape(128, -1), s)
def pk(c, s):
    return (np.ascontiguousarray(c), mx_ref.live(s))
def emit(q):
    return q[0], q[1]
def packed(v, rng):
    q = [mx_ref.quantize(np.ascontiguousarray(v[r])) for r in range(N)]
    return np.stack([a for a, b in q]), np.stack([mx_ref.plane(b, rng) for a, b in q])
def values_of_codes():
    e, c = np.zeros((128, 128, 4), np.float32), np.zeros((128, 2, 4), np.uint8)
    e[np.arange(128), np.arange(128), 0] = 1
    c[:127, :, 0] = np.arange(256).reshape(2, 128).T[:127]
    return mx_ref.matmul(mx_ref.quantize(e.reshape(128, 512).astype(BF)), (c.reshape(128, 8), np.full((16, 2), 127, np.uint8))).T.reshape(-1).astype(np.float64)
CODE_VALUE, SCALE_VALUE = values_of_codes(), 2.0 ** (np.arange(256) - 127.0)
def decode(q):
    return (CODE_VALUE[q[0]].reshape(16, 8, -1, 4) * SCALE_VALUE[q[1]][:, None, :, None] + 0.0).reshape(128, -1).astype(np.float32)
def f(rng, *shape):
    return mx_ref.flush((rng.standard_normal(shape, dtype=np.float32) * np.exp2(rng.integers(-2, 3, shape[:-1] + (1,)))).astype(BF))
def wide(rng, *shape, cols=0):
    v = rng.standard_normal(shape, dtype=np.float32) * np.exp2(rng.integers(-12, 13, shape)).astype(np.float32)
    if cols: v *= np.repeat(np.exp2(rng.integers(-cols, cols + 1, shape[:-2] + (1, shape[-1] // 4))) * (rng.random(shape[:-2] + (1, shape[-1] // 4)) > 0.0625), 4, axis=-1).astype(np.float32)
    return mx_ref.flush(v.astype(BF))
T, M, R, L = 512, 96, 3, 2
def clock(z):
    step = 1 + np.sum(z.reshape(8, 16, T) > 0, axis=1)
    c = np.cumsum(step, axis=1)
    s = c[:, -1:]
    first = np.argmax(M * c[:, None, :] > np.arange(M)[:, None] * s[:, :, None], axis=2)
    phase = M * (c - step) // s
    return c, first, phase
def big(v, k):
    v = v.astype(np.float32) * np.float32(k)
    v[np.abs(v) < np.float32(2.0 ** -16)] = 0
    return v.astype(BF)
def dense(rng):
    return np.array(f(rng, N, 128, 2048))
def weights(rng, w):
    c, p = packed(w, rng)
    return {"wc": c, "ws": p}
def setup_inputs(rng):
    return {"x": big(f(rng, N, 128, 4 * T), 1), "u": np.array(f(rng, N, 128, 512)), **weights(rng, dense(rng))}
def signals(rng, c):
    p = np.arange(128)
    x = big(f(rng, N, 128, 4 * T), 1).reshape(N, 128, T, 4)
    order = np.argsort(rng.random((8, 16)), axis=1)
    up = (order[:, :, None] < c[:, :, None] - 1).reshape(N, 128, T)
    size = (1 + rng.random((N, 128, T))) * 2.0 ** rng.integers(0, 2, (N, 128, T))
    x[..., 0] = (np.where(up, size, -size * (rng.random((N, 128, T)) > 0.25)) + 0.0).astype(np.float32).astype(BF)
    u = np.zeros((N, 128, 128, 4), BF)
    u[:, p, p, 0] = (2.0 ** rng.integers(-3, 4, (N, 128))).astype(np.float32).astype(BF)
    w = dense(rng).reshape(N, 128, 4, 128, 4)
    w[:, :, 0] = 0
    w[:, p, 0, p, 0] = 32
    return {"x": x.reshape(N, 128, 4 * T), "u": u.reshape(N, 128, 512), **weights(rng, w.reshape(N, 128, 2048))}
def setup_inputs_borders(rng):
    c = np.ones((8, 16), int)
    for i, g in enumerate(rng.permutation(8)):
        e = rng.permutation(16)
        n = 16 if i < 2 else int(rng.integers(4, 17))
        c[g, e[0]] += n
        for k in rng.integers(1, 16, 16 - n): c[g, e[k]] += 1
    return signals(rng, np.stack([np.repeat(c, T // 16, axis=1)] * N))
def setup_inputs_stretches(rng):
    c, j = np.ones((N, 8, T), int), np.arange(T)
    for r in range(N):
        for g, k in enumerate(rng.permutation(8)):
            n = int(rng.integers(T // 8, T // 2))
            s = int(rng.integers(1, T - n))
            mid = (j >= s) & (j < s + n)
            loud = [j >= 0, j < 0, j == 0, j == T - 1, j < n, j >= T - n, ~mid, mid][int(k)]
            c[r, g, loud] = 17
    return signals(rng, c)
def setup_inputs_sizes(rng):
    d = setup_inputs(rng)
    small = np.arange(N) >> (L - 1) == int(rng.integers(0, 2))
    k = np.where(small, 2.0 ** -18, 2.0 ** -8).astype(np.float32)
    d["x"] = np.array(mx_ref.flush((d["x"].astype(np.float32) * k[:, None, None]).astype(BF)))
    for r in np.flatnonzero(~small & (np.arange(N) % 2 == int(rng.integers(0, 2)))):
        d["x"][r, :8] = ((1 - 2 * rng.integers(0, 2, (8, 4 * T))) * (1 + rng.random((8, 4 * T))) * 2.0 ** -29).astype(np.float32).astype(BF)
    u = (1 - 2 * rng.integers(0, 2, (N, 128, 128, 4))) * (1 + rng.random((N, 128, 128, 4))) * 2.0 ** rng.integers(-29, 29, (N, 1, 128, 1))
    i = np.arange(32)
    u[:, :, ::4] = 0
    u[:, i // 4, 4 * i, i % 4] = 2.0 ** -30
    d["u"] = u.astype(np.float32).astype(BF).reshape(N, 128, 512)
    return d
def setup_inputs_rests(rng):
    d = setup_inputs(rng)
    x = d["x"].reshape(N, 128, T, 4)
    for r in range(N):
        k = rng.permutation(T) % 3
        e = int(np.flatnonzero(k == 2)[0])
        x[r][:, k == 0] = 0
        x[r][:, k == 1] = x[r][:, e:e + 1]
    x[int(rng.integers(0, N))] = 0
    d["x"] = x.reshape(N, 128, 4 * T)
    return d
def setup_inputs_spread(rng):
    d = setup_inputs(rng)
    d["x"] = big(wide(rng, N, 128, 4 * T, cols=6), 1)
    return d
def check_inputs(d):
    b = []
    for k in ("x", "u"):
        v = np.abs(d[k].astype(np.float32))
        if not (np.isfinite(v).all() and ((v == 0) | (v >= 2.0 ** -30) & (v <= 2.0 ** 30)).all()): b.append("a value of " + k)
    return b
def reference(x, u, wc, ws):
    qu = [mx_ref.quantize(np.ascontiguousarray(u[r])) for r in range(N)]
    w = [pk(wc[r], ws[r]) for r in range(N)]
    t = [np.ascontiguousarray(x[r]) for r in range(N)]
    a = [mx_ref.quantize(t[r]) for r in range(N)]
    for b in range(R):
        phase, v = [], []
        for r in range(N):
            c, first, p = clock(mx_ref.matmul(qu[r], a[r]))
            phase.append(p)
            v.append(mx_ref.quantize(gcols(t[r], first)))
        d = decode(join(*a, *v))
        da, dv = d[:, :4 * N * T].reshape(8, 16, N, T, 4), d[:, 4 * N * T:].reshape(8, 16, N, M, 4)
        for r in range(N):
            q = r ^ (1 << (b % L))
            got = np.stack([dv[g, :, q][:, phase[r][g]] for g in range(8)])
            h = ((da[:, :, r] + got) * np.float32(0.5)).reshape(128, 4 * T).astype(BF)
            h = mx_ref.quantize(np.ascontiguousarray(h))
            t[r] = tile([mx_ref.matmul(pick(w[r], np.arange(128 * i, 128 * i + 128)), h) * np.float32(0.03125) for i in range(4)])
            a[r] = mx_ref.quantize(t[r])
    y, cl = np.zeros((N, 128, T), np.float32), np.zeros((N, 8, T), np.float32)
    oc, osc = np.zeros((N, 128, 4 * T), np.uint8), np.zeros((N, 16, T), np.uint8)
    for r in range(N):
        y[r] = mx_ref.matmul(qu[r], a[r])
        c, first, p = clock(y[r])
        cl[r] = c
        oc[r], osc[r] = emit(a[r])
    return {"y": y, "cl": cl, "oc": oc, "osc": osc}

@@ -1,0 +1,422 @@
+from concourse.mybir import dt, AluOpType as ALU, ActivationFunctionType as ACT
+
+TC, M, R = 512, 96, 3
+CH = [(0, 128), (128, 256), (256, 384), (384, 512)]
+XC = [(0, 128), (128, 256), (256, 384), (384, 512)]
+EARLY = [[(1, 0, 128)], [(1, 0, 128)], [(1, 0, 128), (2, 128, 256)]]
+CV = 224
+F8, U8, BF, F32, I32, U16 = "float8_e4m3fn_x4", "uint8", "bfloat16", "float32", "int32", "uint16"
+
+
+def _sb(n, d):
+    return ("sbuf", [128, n], d)
+
+
+SCRATCH = {
+    "t0": _sb(2048, BF), "t1": _sb(2048, BF), "t2": _sb(2048, BF), "t3": _sb(2048, BF),
+    "aq": _sb(4 * TC, F8), "asc": _sb(4 * TC, U8),
+    "ut": _sb(512, BF), "uq": _sb(128, F8), "usc": _sb(128, U8),
+    "wq": _sb(512, F8), "wsc": _sb(512, U8),
+    "ht": _sb(2048, BF), "hq": _sb(R * TC, F8), "hsc": _sb(R * TC, U8),
+    "da": _sb(2048, BF), "dv": _sb(384, BF), "vt": _sb(512, BF),
+    "cvq": _sb(R * CV, F8), "cvs": _sb(R * CV, U8),
+    "sg": _sb(512, BF), "sq": _sb(R * 128 + 128, F8), "ssc": _sb(R * 128 + 128, U8),
+    "cmp": _sb(512, BF), "cq": _sb(R * 128, F8), "csc": _sb(R * 128, U8),
+    "half": _sb(528, BF), "eb": _sb(528, BF), "eq": _sb(512, F8), "esc": _sb(512, U8),
+    "nq": _sb(128, BF), "gt": _sb(1536, BF), "gf": _sb(1536, BF), "gq": _sb(768, F8), "gsc": _sb(768, U8),
+    "pi": _sb(4, I32), "ri": _sb(4, I32), "rf": _sb(4, F32), "col": _sb(8, F32), "tiny": _sb(4, F32),
+    "jq": _sb(128, F32), "iw": _sb(128, F32), "c36": _sb(128, F32), "rest": _sb(384, F32),
+    "k6": _sb(8, F32), "r6": _sb(8, F32), "w6": _sb(8, F32), "k96": _sb(96, F32), "m2": _sb(128, F32), "m3": _sb(96, F32),
+    "cw": _sb(128, F32), "ew": _sb(128, F32), "ed": _sb(128, F32), "th96": _sb(96, F32),
+    "junk": _sb(192, F32), "acc": _sb(8, F32), "brep": _sb(96, F32), "bsel": _sb(96, F32), "s24": _sb(24, F32),
+    "o2": _sb(8, U16), "ov": _sb(24, U16), "op": _sb(128, U16),
+    "sm": _sb(8, F32), "x4": _sb(128, F32), "y4": _sb(128, F32),
+    "ys": _sb(512, F32), "cs": _sb(512, F32),
+}
+for _b in range(8):
+    SCRATCH["p%d" % _b] = ("psum", [128, 512], F32)
+
+NC, ND = 60, 20
+SEMAPHORES = ["arr0", "arr1", "arr2", "left"] + ["c%d" % _i for _i in range(NC)] + ["d%d" % _i for _i in range(ND)]
+
+
+def is_bank(k):
+    return k[0] == "p" and k[1:].isdigit()
+
+
+def emit(ops, queues, T):
+    known = {e: 0 for e in queues}
+    for i, o in enumerate(ops):
+        o["by"] = []
+        if o["e"] == "x":
+            o["done"] = 1 << i
+            continue
+        o["waits"] = []
+        for j in range(i - 1, -1, -1):
+            if known[o["e"]] >> j & 1:
+                continue
+            p = ops[j]
+            hit = False
+            for (k, m) in o["r"]:
+                if p["W"].get(k, 0) & m or (is_bank(k) and k in p["R"] and p["e"] != o["e"]):
+                    hit = True
+            for (k, m) in o["w"]:
+                if (p["W"].get(k, 0) | p["R"].get(k, 0)) & m:
+                    hit = True
+            if hit:
+                o["waits"].append(j)
+                p["by"].append(i)
+                known[o["e"]] |= p["done"]
+        o["seen"] = known[o["e"]]
+        o["done"] = known[o["e"]] | 1 << i
+    groups = {}
+    for i, o in enumerate(ops):
+        if o["by"] and o["e"] != "x":
+            groups.setdefault((o["dma"], tuple(o["by"])), []).append(i)
+    pools = {"c": [], "d": []}
+    for i, o in enumerate(ops):
+        if o["e"] == "x":
+            continue
+        q = queues[o["e"]]
+        for sem in sorted(set(ops[j]["sem"] for j in o["waits"])):
+            q.wait_ge(T.sem[sem[0]], sem[1])
+        if o["f"] is None:
+            continue
+        ins = o["f"]()
+        if o["by"]:
+            kind = "d" if o["dma"] else "c"
+            step = 16 if o["dma"] else 1
+            if "sem" not in o:
+                members = groups[(o["dma"], tuple(o["by"]))]
+                mask = sum(1 << j for j in members)
+                pool = pools[kind]
+                free = [s for s in range(len(pool)) if all(ops[j]["seen"] & pool[s][0] == pool[s][0] for j in members)]
+                s = free[0] if free else len(pool)
+                if not free:
+                    pool.append((0, 0))
+                pool[s] = (mask, pool[s][1] + step * len(members))
+                for j in members:
+                    ops[j]["sem"] = ("%s%d" % (kind, s), pool[s][1])
+            ins.then_inc(T.sem[o["sem"][0]], step)
+
+
+def rank_program(g, core, T, topo):
+    rank = T.rank_of(core)
+    if rank is None:
+        return
+    ops = []
+    vec, act, pe, syn = g.vector, g.scalar, g.tensor, g.sync
+
+    def V(name, a, b, s=1):
+        m = 0
+        if is_bank(name):
+            m = 1
+        elif s == 1:
+            m = ((1 << (b - a)) - 1) << a
+        else:
+            for c in range(a, b, s):
+                m |= 1 << c
+        return (T[name][:, a:b] if s == 1 else T[name][:, a:b:s], [(name, m)])
+
+    def IND(win, off):
+        return (win[0].indirect(off[0]), win[1] + off[1])
+
+    def op(e, f, r, w, dma=False, sem=None):
+        rr = [a for v in r for a in v[1]]
+        ww = [a for v in w for a in v[1]]
+        o = {"e": e, "f": f, "r": rr, "w": ww, "R": {}, "W": {}, "dma": dma}
+        for (k, m) in rr:
+            o["R"][k] = o["R"].get(k, 0) | m
+        for (k, m) in ww:
+            o["W"][k] = o["W"].get(k, 0) | m
+        if sem:
+            o["sem"] = sem
+        ops.append(o)
+
+    def isv(a):
+        return isinstance(a, tuple)
+
+    def ap(a):
+        return a[0] if isv(a) else a
+
+    def ts(out, in0, s1, s2, o0, o1=None):
+        r = [in0] + [a for a in (s1, s2) if isv(a)]
+        if o1 is None:
+            op("v", lambda: vec.tensor_scalar(out[0], in0[0], ap(s1), None, o0), r, [out])
+        else:
+            op("v", lambda: vec.tensor_scalar(out[0], in0[0], ap(s1), ap(s2), o0, o1), r, [out])
+
+    def tt(out, a, b, o):
+        op("v", lambda: vec.tensor_tensor(out[0], a[0], b[0], o), [a, b], [out])
+
+    def cp(out, a):
+        op("v", lambda: vec.tensor_copy(out[0], a[0]), [a], [out])
+
+    def ms(out, c):
+        op("v", lambda: vec.memset(out[0], c), [], [out])
+
+    def rcp(out, a):
+        op("v", lambda: vec.reciprocal(out[0], a[0]), [a], [out])
+
+    def scan(out, d0, d1, init, o0, o1):
+        op("v", lambda: vec.tensor_tensor_scan(out[0], d0[0], d1[0], ap(init), o0, o1),
+           [d0, d1] + ([init] if isv(init) else []), [out])
+
+    def quant(q, s, a, b, src):
+        vq, vs = V(q, a, b), V(s, a, b)
+        op("v", lambda: vec.quantize_mx(vq[0], vs[0], src[0]), [src], [vq, vs])
+
+    def A(out, a, func, bias=0.0, scale=1.0, acc=None):
+        r = [a] + [c for c in (bias, scale) if isv(c)]
+        if acc is None:
+            op("s", lambda: act.activation(out[0], a[0], func, bias=ap(bias), scale=ap(scale)), r, [out])
+        else:
+            op("s", lambda: act.activation(out[0], a[0], func, bias=ap(bias), scale=ap(scale), accum_out=acc[0]), r, [out, acc])
+
+    def mm(bank, lq, ls, l0, rq, rs, a, b):
+        out = V("p%d" % bank, 0, b - a)
+        w, ws_, x, xs = V(lq, l0, l0 + 128), V(ls, l0, l0 + 128), V(rq, a, b), V(rs, a, b)
+        op("t", lambda: pe.matmul_mx(out[0], w[0], ws_[0], x[0], xs[0], True, True), [w, ws_, x, xs], [out])
+
+    def iota(out, pat, base, cm, flt=True):
+        if flt:
+            op("g", lambda: g.iota(out[0], pat, base, cm, allow_small_or_imprecise_dtypes=True), [], [out])
+        else:
+            op("g", lambda: g.iota(out[0], pat, base, cm), [], [out])
+
+    def sel(out, a, pat, cmp_, fill, base, cm):
+        op("g", lambda: g.affine_select(out[0], a[0], pat, cmp_, fill, base, cm), [a], [out])
+
+    def dma(e, out, a, r, w):
+        q = syn if e == "y" else act
+        op(e, lambda: q.dma_start(out, a), r, w, dma=True)
+
+    outs = []
+
+    def store(e, out, a, r):
+        tag = (None, [("out%d" % len(outs), 1)])
+        outs.append(tag)
+        dma(e, out, a, r, [tag])
+
+    def move(e, out, a, scale):
+        if e == "s":
+            A(out, a, ACT.Copy, scale=scale)
+        elif scale == 1.0:
+            cp(out, a)
+        else:
+            ts(out, a, scale, None, ALU.mult)
+
+    dma("y", T.ut[:], T.u[:], [], [V("ut", 0, 512)])
+    for c, (a, b) in enumerate(XC):
+        v = V("t0", 4 * a, 4 * b)
+        dma("s" if c % 2 == 0 else "y", v[0], T.x[:, 4 * a:4 * b], [], [v])
+    somex = V("t0", 4 * XC[1][0], 4 * XC[1][1])
+    dma("y", T.wq[:].bitcast(dt.uint8), T.wc[:], [somex], [V("wq", 0, 512)])
+    dma("y", T.wsc[:], T.ws[:], [somex], [V("wsc", 0, 512)])
+
+    rcol, qcol, tcol = V("rf", 0, 1), V("rf", 1, 2), V("rf", 2, 3)
+    cthr, ca4, ct52 = V("col", 0, 1), V("col", 1, 2), V("col", 2, 3)
+    tiny = V("tiny", 0, 1)
+    iota(V("pi", 0, 1), [[0, 1]], 0, 1, False)
+    iota(V("nq", 0, 128), [[0, 8], [1, 4], [0, 4]], 0, 0)
+    sel(V("nq", 0, 128), V("nq", 0, 128), [[-16, 8], [0, 16]], ALU.is_ge, 99.0, 0, 1)
+    sel(V("nq", 0, 128), V("nq", 0, 128), [[16, 8], [0, 16]], ALU.is_ge, 99.0, 15, -1)
+    iota(V("iw", 0, 128), [[1, 128]], 0, 0)
+    iota(V("jq", 0, 128), [[0, 32], [1, 4]], 0, 0)
+    ms(tiny, -2.0 ** -120)
+    ms(V("half", 0, 528), 0.5)
+    ms(V("cmp", 96, 512), 0.0)
+    ms(V("vt", 384, 512), 0.0)
+    ms(V("c36", 0, 128), 36.0)
+    sel(V("eb", 0, 528), V("half", 0, 528), [[-1, 528]], ALU.is_equal, 0.0, 3, 4)
+    ts(V("ri", 0, 1), V("pi", 0, 1), 15, None, ALU.bitwise_and)
+    ts(V("ri", 1, 2), V("pi", 0, 1), 2, 3, ALU.arith_shift_right, ALU.bitwise_and)
+    ts(V("ri", 2, 3), V("pi", 0, 1), 3, None, ALU.bitwise_and)
+    cp(V("rf", 0, 3), V("ri", 0, 3))
+    ts(cthr, qcol, -9.0, 36.0 + 0.5 / M, ALU.mult, ALU.add)
+    ts(ca4, qcol, 36.0 * M, 2.0 - 144.0 * M, ALU.mult, ALU.add)
+    ts(ct52, tcol, -52.0, None, ALU.add)
+    for s in (3, 2, 1, 0):
+        ts(V("gt", 512 + s, 1024, 4), V("nq", 0, 128), float(s), 0.5, ALU.is_le, ALU.mult)
+    for s in range(4):
+        A(V("gt", s, 512, 4), V("gt", 515, 1024, 4), ACT.Copy)
+    for s in range(4):
+        ts(V("gt", 1024 + s, 1536, 4), V("nq", 0, 128), float(s), 4.0, ALU.is_equal, ALU.mult)
+    ts(V("k6", 0, 6), V("iw", 0, 96, 16), rcol, 1.0e-4, ALU.add, ALU.max)
+    quant("gq", "gsc", 0, 256, V("gt", 0, 1024))
+    rcp(V("r6", 0, 6), V("k6", 0, 6))
+    A(V("k96", 0, 96), V("iw", 0, 96), ACT.Copy, scale=1.0 / M)
+    A(V("w6", 0, 6), V("r6", 0, 6), ACT.Copy, scale=-M * (1.0 - 5.0e-7))
+    ts(V("m2", 0, 128), V("jq", 0, 128), tcol, 1.0e6, ALU.is_equal, ALU.mult)
+    quant("uq", "usc", 0, 128, V("ut", 0, 512))
+
+    def q_state(b, a0, a1):
+        quant("aq", "asc", TC * b + a0, TC * b + a1, V("t%d" % b, 4 * a0, 4 * a1))
+
+    def z_mm(b, a0, a1, bank):
+        mm(bank, "uq", "usc", 0, "aq", "asc", TC * b + a0, TC * b + a1)
+
+    def z_sign(a0, a1, bank):
+        A(V("sg", a0, a1), V("p%d" % bank, 0, a1 - a0), ACT.Sign, bias=tiny)
+
+    def da_mm(b, e):
+        mm(4 + e, "eq", "esc", 128 * e, "aq", "asc", TC * b, TC * b + TC)
+
+    def da_cp(eng, e, h):
+        move(eng, V("da", 1024 * h + e, 1024 * h + 1024, 4), V("p%d" % (4 + e), 256 * h, 256 * h + 256), 1.0)
+
+    def exchange(b):
+        early = b > 0
+        S = V("cw", 127, 128)
+        if early:
+            da_mm(b, 0)
+        quant("sq", "ssc", 128 * b, 128 * b + 128, V("sg", 0, 512))
+        mm(2, "gq", "gsc", 0, "sq", "ssc", 128 * b, 128 * b + 128)
+        mm(3, "gq", "gsc", 128, "sq", "ssc", 128 * b, 128 * b + 128)
+        if early:
+            da_mm(b, 1)
+            da_cp("s", 0, 0)
+        scan(V("cw", 0, 128), V("p2", 0, 128), V("c36", 0, 128), 0.0, ALU.add, ALU.add)
+        for m in range(6):
+            A(V("junk", 32 * m, 32 * m + 32), V("cw", 3, 128, 4), ACT.Sign, bias=S, scale=V("w6", m, m + 1), acc=V("acc", m, m + 1))
+        tt(V("ew", 0, 128), V("cw", 0, 128), V("p3", 0, 128), ALU.subtract)
+        ts(V("th96", 0, 96), V("k96", 0, 96), S, cthr, ALU.mult, ALU.add)
+        scan(V("ed", 0, 128), V("m2", 0, 128), V("ew", 0, 128), 0.0, ALU.max, ALU.min)
+        ts(V("o2", 0, 6), V("acc", 0, 6), 2.0, 67.0, ALU.mult, ALU.add)
+        tt(V("cmp", 0, 96), IND(V("ed", 0, 128), V("o2", 0, 6)), V("th96", 0, 96), ALU.is_le)
+        A(V("brep", 0, 96), IND(V("iw", 0, 128), V("o2", 0, 6)), ACT.Copy, scale=16.0)
+        if early:
+            da_cp("s", 1, 0)
+        quant("cq", "csc", 128 * b, 128 * b + 128, V("cmp", 0, 512))
+        mm(0, "gq", "gsc", 256, "cq", "csc", 128 * b, 128 * b + 128)
+        if early:
+            da_mm(b, 2)
+            da_mm(b, 3)
+        scan(V("bsel", 0, 96), V("m3", 0, 96), V("brep", 0, 96), 0.0, ALU.max, ALU.min)
+        tt(V("s24", 0, 24), V("p0", 0, 24), V("bsel", 3, 96, 4), ALU.add)
+        ts(V("ov", 0, 24), V("s24", 0, 24), ct52, None, ALU.add)
+        st = V("t%d" % b, 0, 2048)
+        cp(V("vt", 0, 192), IND(st, V("ov", 0, 12)))
+        A(V("vt", 192, 384), IND(st, V("ov", 12, 24)), ACT.Copy)
+        own = CV * b + M
+        quant("cvq", "cvs", own, own + 128, V("vt", 0, 512))
+        peer = T.cores[rank ^ (1 << (b % 2))]
+        rid, pid, _ = topo.addr(peer)
+        mask = topo.mask(core, peer)
+        n = len(topo.engines(core, peer))
+        sq_, ss_, lq, ls = V("cvq", own, own + M), V("cvs", own, own + M), V("cvq", CV * b, own), V("cvs", CV * b, own)
+        arr = T.sem["arr%d" % b]
+        op("g", lambda: g.remote_dma(lq[0].bitcast(dt.uint8), sq_[0].bitcast(dt.uint8), arr, T.sem.left, pid, rid, mask), [sq_], [])
+        op("g", lambda: g.remote_dma(ls[0], ss_[0], arr, T.sem.left, pid, rid, mask), [ss_], [])
+        sent.append(2 * n)
+        if b == 0:
+            for t in range(3):
+                sel(V("gf", 512 * t, 512 * t + 512), V("gt", 0, 512), [[0, 128], [1, 4]], ALU.is_ge, 0.0, -t - 1, 0)
+            for e in range(4):
+                quant("eq", "esc", 128 * e, 128 * e + 128, V("eb", 3 - e, 515 - e))
+                da_mm(b, e)
+            da_cp("s", 0, 0)
+            da_cp("s", 1, 0)
+        da_cp("s", 2, 0)
+        da_cp("s", 3, 0)
+        big = 1.5 * 2.0 ** 25
+        rcp(V("sm", 0, 1), S)
+        ts(V("sm", 1, 2), S, -2.0, ca4, ALU.mult, ALU.add)
+        ts(V("x4", 0, 128), V("ew", 0, 128), 4.0 * M, V("sm", 1, 2), ALU.mult, ALU.add)
+        ts(V("y4", 0, 128), V("x4", 0, 128), V("sm", 0, 1), big, ALU.mult, ALU.add)
+        ts(V("op", 0, 128), V("y4", 0, 128), big, tcol, ALU.subtract, ALU.add)
+        da_cp("v", 0, 1)
+        da_cp("s", 1, 1)
+        da_cp("s", 2, 1)
+        da_cp("s", 3, 1)
+        if b == 1:
+            quant("gq", "gsc", 384, 768, V("gf", 0, 1536))
+        op("x", None, [], [lq, ls], sem=("arr%d" % b, 2 * n))
+        for e in (0, 2, 1, 3):
+            mm(e, "eq", "esc", 128 * e, "cvq", "cvs", CV * b, CV * b + 128)
+        for e in (0, 2, 1, 3):
+            move("v" if e < 2 else "s", V("dv", e, 384, 4), V("p%d" % e, 0, M), 1.0)
+
+    def h_make(b, c):
+        a0, a1 = CH[c]
+        tt(V("ht", 4 * a0, 4 * a1), IND(V("dv", 0, 384), V("op", a0 // 4, a1 // 4)), V("da", 4 * a0, 4 * a1), ALU.add)
+        quant("hq", "hsc", TC * b + a0, TC * b + a1, V("ht", 4 * a0, 4 * a1))
+        for i in range(4):
+            mm(4 + i, "wq", "wsc", 128 * i, "hq", "hsc", TC * b + a0, TC * b + a1)
+
+    def r_cp(b, c, i, eng):
+        a0, a1 = CH[c]
+        move(eng, V("t%d" % (b + 1), 4 * a0 + i, 4 * a1, 4), V("p%d" % (4 + i), 0, a1 - a0), 0.03125)
+
+    def y_cp(eng, a0, a1, bank):
+        move(eng, V("ys", a0, a1), V("p%d" % bank, 0, a1 - a0), 1.0)
+
+    def st_codes(a0, a1):
+        v = V("aq", TC * R + a0, TC * R + a1)
+        store("y", T.oc[:, 4 * a0:4 * a1], v[0].bitcast(dt.uint8), [v])
+
+    def st_y(e, a0, a1):
+        v = V("ys", a0, a1)
+        store(e, T.y[:, a0:a1], v[0], [v])
+
+    sent = []
+    n = len(CH)
+    for c, (a0, a1) in enumerate(XC):
+        q_state(0, a0, a1)
+        z_mm(0, a0, a1, c % 2)
+        z_sign(a0, a1, c % 2)
+    quant("gq", "gsc", 256, 384, V("gt", 1024, 1536))
+    ts(V("m3", 0, 96), V("jq", 0, 96), qcol, 1.0e6, ALU.is_equal, ALU.mult)
+    e1 = CH[-1][0]
+    for b in range(R):
+        exchange(b)
+        fin = b == R - 1
+        e0 = 0
+        for c in range(n):
+            h_make(b, c)
+            now = [(a0, a1) for (k, a0, a1) in EARLY[b] if k == c]
+            for (a0, a1) in now:
+                q_state(b + 1, a0, a1)
+                z_mm(b + 1, a0, a1, 0)
+                if fin:
+                    st_codes(a0, a1)
+                e0 = a1
+            if c < n - 1:
+                for i in range(4):
+                    r_cp(b, c, i, "s")
+            for (a0, a1) in now:
+                z_sign(a0, a1, 0)
+                if fin:
+                    y_cp("s", a0, a1, 0)
+                    st_y("y", a0, a1)
+        q_state(b + 1, e0, e1)
+        z_mm(b + 1, e0, e1, 1)
+        if fin:
+            st_codes(e0, e1)
+            z_mm(b + 1, e0, e1, 2)
+        for i in range(4):
+            r_cp(b, n - 1, i, "s" if i % 2 == 0 else "v")
+        z_sign(e0, e1, 1)
+        q_state(b + 1, e1, TC)
+        z_mm(b + 1, e1, TC, 0)
+        z_sign(e1, TC, 0)
+    st_codes(e1, TC)
+    y_cp("v", e0, e1, 2)
+    st_y("y", e0, e1)
+    for k in range(4):
+        store("y", T.osc[4 * k:4 * k + 4, :], T.asc[32 * k:32 * k + 4, TC * R:TC * R + TC], [V("asc", TC * R, TC * R + TC)])
+    y_cp("s", e1, TC, 0)
+    st_y("y", e1, TC)
+    quant("sq", "ssc", 128 * R, 128 * R + 128, V("sg", 0, 512))
+    mm(3, "gq", "gsc", 0, "sq", "ssc", 128 * R, 128 * R + 128)
+    for t in range(3):
+        mm(4 + t, "gq", "gsc", 384 + 128 * t, "sq", "ssc", 128 * R, 128 * R + 128)
+    scan(V("cs", 3, 512, 4), V("p3", 0, 128), V("c36", 0, 128), 0.0, ALU.add, ALU.add)
+    for t in range(3):
+        rest = V("rest", 128 * t, 128 * t + 128)
+        A(rest, V("p%d" % (4 + t), 0, 128), ACT.Identity, bias=9.0 * (3 - t))
+        scan(V("cs", t, 512, 4), V("cs", 3, 512, 4), rest, 0.0, ALU.max, ALU.subtract)
+    store("s", T.cl[:], T.cs[0:128:16, :], [V("cs", 0, 512)])
+    op("y", None, outs, [])
+    emit(ops, {"g": g, "v": vec, "s": act, "t": pe, "y": syn}, T)
+    g.wait_ge(T.sem.left, sum(sent))

@@ -1,9 +1,8 @@
 from concourse.mybir import dt, AluOpType as ALU, ActivationFunctionType as ACT
 
 TC, M, R = 512, 96, 3
-CH = [(0, 128), (128, 256), (256, 384), (384, 512)]
-XC = [(0, 128), (128, 256), (256, 384), (384, 512)]
-EARLY = [[(1, 0, 128)], [(1, 0, 128)], [(1, 0, 128), (2, 128, 256)]]
+CH = [(0, 288), (288, 512)]
+XC = [(0, 320), (320, 512)]
 CV = 224
 F8, U8, BF, F32, I32, U16 = "float8_e4m3fn_x4", "uint8", "bfloat16", "float32", "int32", "uint16"
 
@@ -20,12 +19,12 @@ SCRATCH = {
     "ht": _sb(2048, BF), "hq": _sb(R * TC, F8), "hsc": _sb(R * TC, U8),
     "da": _sb(2048, BF), "dv": _sb(384, BF), "vt": _sb(512, BF),
     "cvq": _sb(R * CV, F8), "cvs": _sb(R * CV, U8),
-    "sg": _sb(512, BF), "sq": _sb(R * 128 + 128, F8), "ssc": _sb(R * 128 + 128, U8),
+    "sg": _sb(512, BF), "sgf": _sb(2048, BF), "sq": _sb(R * 128 + TC, F8), "ssc": _sb(R * 128 + TC, U8),
     "cmp": _sb(512, BF), "cq": _sb(R * 128, F8), "csc": _sb(R * 128, U8),
     "half": _sb(528, BF), "eb": _sb(528, BF), "eq": _sb(512, F8), "esc": _sb(512, U8),
-    "nq": _sb(128, BF), "gt": _sb(1536, BF), "gf": _sb(1536, BF), "gq": _sb(768, F8), "gsc": _sb(768, U8),
+    "nq": _sb(128, BF), "gt": _sb(1536, BF), "gq": _sb(384, F8), "gsc": _sb(384, U8),
     "pi": _sb(4, I32), "ri": _sb(4, I32), "rf": _sb(4, F32), "col": _sb(8, F32), "tiny": _sb(4, F32),
-    "jq": _sb(128, F32), "iw": _sb(128, F32), "c36": _sb(128, F32), "rest": _sb(384, F32),
+    "jq": _sb(128, F32), "iw": _sb(128, F32), "c36": _sb(128, F32), "c9": _sb(512, F32),
     "k6": _sb(8, F32), "r6": _sb(8, F32), "w6": _sb(8, F32), "k96": _sb(96, F32), "m2": _sb(128, F32), "m3": _sb(96, F32),
     "cw": _sb(128, F32), "ew": _sb(128, F32), "ed": _sb(128, F32), "th96": _sb(96, F32),
     "junk": _sb(192, F32), "acc": _sb(8, F32), "brep": _sb(96, F32), "bsel": _sb(96, F32), "s24": _sb(24, F32),
@@ -210,7 +209,7 @@ def rank_program(g, core, T, topo):
     for c, (a, b) in enumerate(XC):
         v = V("t0", 4 * a, 4 * b)
         dma("s" if c % 2 == 0 else "y", v[0], T.x[:, 4 * a:4 * b], [], [v])
-    somex = V("t0", 4 * XC[1][0], 4 * XC[1][1])
+    somex = V("t0", 4 * XC[0][0], 4 * XC[0][1])
     dma("y", T.wq[:].bitcast(dt.uint8), T.wc[:], [somex], [V("wq", 0, 512)])
     dma("y", T.wsc[:], T.ws[:], [somex], [V("wsc", 0, 512)])
 
@@ -228,27 +227,25 @@ def rank_program(g, core, T, topo):
     ms(V("cmp", 96, 512), 0.0)
     ms(V("vt", 384, 512), 0.0)
     ms(V("c36", 0, 128), 36.0)
-    sel(V("eb", 0, 528), V("half", 0, 528), [[-1, 528]], ALU.is_equal, 0.0, 3, 4)
     ts(V("ri", 0, 1), V("pi", 0, 1), 15, None, ALU.bitwise_and)
     ts(V("ri", 1, 2), V("pi", 0, 1), 2, 3, ALU.arith_shift_right, ALU.bitwise_and)
     ts(V("ri", 2, 3), V("pi", 0, 1), 3, None, ALU.bitwise_and)
     cp(V("rf", 0, 3), V("ri", 0, 3))
-    ts(cthr, qcol, -9.0, 36.0 + 0.5 / M, ALU.mult, ALU.add)
-    ts(ca4, qcol, 36.0 * M, 2.0 - 144.0 * M, ALU.mult, ALU.add)
-    ts(ct52, tcol, -52.0, None, ALU.add)
+    A(cthr, qcol, ACT.Identity, bias=36.0 + 0.5 / M, scale=-9.0)
+    A(ca4, qcol, ACT.Identity, bias=2.0 - 144.0 * M, scale=36.0 * M)
+    A(ct52, tcol, ACT.Identity, bias=-52.0)
     for s in (3, 2, 1, 0):
         ts(V("gt", 512 + s, 1024, 4), V("nq", 0, 128), float(s), 0.5, ALU.is_le, ALU.mult)
-    for s in range(4):
+    for s in range(2):
         A(V("gt", s, 512, 4), V("gt", 515, 1024, 4), ACT.Copy)
+        ts(V("gt", 2 + s, 512, 4), V("nq", 0, 128), 3.0, 0.5, ALU.is_le, ALU.mult)
     for s in range(4):
-        ts(V("gt", 1024 + s, 1536, 4), V("nq", 0, 128), float(s), 4.0, ALU.is_equal, ALU.mult)
-    ts(V("k6", 0, 6), V("iw", 0, 96, 16), rcol, 1.0e-4, ALU.add, ALU.max)
+        sel(V("gt", 1024 + s, 1536, 4), V("gt", 515, 1024, 4), [[0, 8], [-1, 4], [0, 4]], ALU.is_equal, 0.0, s, 0)
+    sel(V("eb", 0, 528), V("half", 0, 528), [[-1, 528]], ALU.is_equal, 0.0, 3, 4)
     quant("gq", "gsc", 0, 256, V("gt", 0, 1024))
-    rcp(V("r6", 0, 6), V("k6", 0, 6))
-    A(V("k96", 0, 96), V("iw", 0, 96), ACT.Copy, scale=1.0 / M)
-    A(V("w6", 0, 6), V("r6", 0, 6), ACT.Copy, scale=-M * (1.0 - 5.0e-7))
-    ts(V("m2", 0, 128), V("jq", 0, 128), tcol, 1.0e6, ALU.is_equal, ALU.mult)
+    ts(V("k6", 0, 6), V("iw", 0, 96, 16), rcol, 1.0e-4, ALU.add, ALU.max)
     quant("uq", "usc", 0, 128, V("ut", 0, 512))
+    A(V("k96", 0, 96), V("iw", 0, 96), ACT.Copy, scale=1.0 / M)
 
     def q_state(b, a0, a1):
         quant("aq", "asc", TC * b + a0, TC * b + a1, V("t%d" % b, 4 * a0, 4 * a1))
@@ -256,14 +253,14 @@ def rank_program(g, core, T, topo):
     def z_mm(b, a0, a1, bank):
         mm(bank, "uq", "usc", 0, "aq", "asc", TC * b + a0, TC * b + a1)
 
-    def z_sign(a0, a1, bank):
-        A(V("sg", a0, a1), V("p%d" % bank, 0, a1 - a0), ACT.Sign, bias=tiny)
+    def z_sign(a0, a1, bank, fin=False):
+        A(V("sgf", 4 * a0, 4 * a1, 4) if fin else V("sg", a0, a1), V("p%d" % bank, 0, a1 - a0), ACT.Sign, bias=tiny)
 
     def da_mm(b, e):
         mm(4 + e, "eq", "esc", 128 * e, "aq", "asc", TC * b, TC * b + TC)
 
-    def da_cp(eng, e, h):
-        move(eng, V("da", 1024 * h + e, 1024 * h + 1024, 4), V("p%d" % (4 + e), 256 * h, 256 * h + 256), 1.0)
+    def da_cp(eng, e, h, k=1):
+        move(eng, V("da", 1024 * h + e, 1024 * (h + k), 4), V("p%d" % (4 + e), 256 * h, 256 * (h + k)), 1.0)
 
     def exchange(b):
         early = b > 0
@@ -276,15 +273,19 @@ def rank_program(g, core, T, topo):
         if early:
             da_mm(b, 1)
             da_cp("s", 0, 0)
+        else:
+            A(V("w6", 0, 6), V("r6", 0, 6), ACT.Copy, scale=-M * (1.0 - 5.0e-7))
         scan(V("cw", 0, 128), V("p2", 0, 128), V("c36", 0, 128), 0.0, ALU.add, ALU.add)
         for m in range(6):
             A(V("junk", 32 * m, 32 * m + 32), V("cw", 3, 128, 4), ACT.Sign, bias=S, scale=V("w6", m, m + 1), acc=V("acc", m, m + 1))
         tt(V("ew", 0, 128), V("cw", 0, 128), V("p3", 0, 128), ALU.subtract)
         ts(V("th96", 0, 96), V("k96", 0, 96), S, cthr, ALU.mult, ALU.add)
         scan(V("ed", 0, 128), V("m2", 0, 128), V("ew", 0, 128), 0.0, ALU.max, ALU.min)
+        if not early:
+            quant("gq", "gsc", 256, 384, V("gt", 1024, 1536))
         ts(V("o2", 0, 6), V("acc", 0, 6), 2.0, 67.0, ALU.mult, ALU.add)
         tt(V("cmp", 0, 96), IND(V("ed", 0, 128), V("o2", 0, 6)), V("th96", 0, 96), ALU.is_le)
-        A(V("brep", 0, 96), IND(V("iw", 0, 128), V("o2", 0, 6)), ACT.Copy, scale=16.0)
+        A(V("brep", 0, 96), IND(V("iw", 0, 128), V("o2", 0, 6)), ACT.Copy, scale=2.0)
         if early:
             da_cp("s", 1, 0)
         quant("cq", "csc", 128 * b, 128 * b + 128, V("cmp", 0, 512))
@@ -294,7 +295,7 @@ def rank_program(g, core, T, topo):
             da_mm(b, 3)
         scan(V("bsel", 0, 96), V("m3", 0, 96), V("brep", 0, 96), 0.0, ALU.max, ALU.min)
         tt(V("s24", 0, 24), V("p0", 0, 24), V("bsel", 3, 96, 4), ALU.add)
-        ts(V("ov", 0, 24), V("s24", 0, 24), ct52, None, ALU.add)
+        ts(V("ov", 0, 24), V("s24", 0, 24), 8.0, ct52, ALU.mult, ALU.add)
         st = V("t%d" % b, 0, 2048)
         cp(V("vt", 0, 192), IND(st, V("ov", 0, 12)))
         A(V("vt", 192, 384), IND(st, V("ov", 12, 24)), ACT.Copy)
@@ -310,27 +311,24 @@ def rank_program(g, core, T, topo):
         op("g", lambda: g.remote_dma(ls[0], ss_[0], arr, T.sem.left, pid, rid, mask), [ss_], [])
         sent.append(2 * n)
         if b == 0:
-            for t in range(3):
-                sel(V("gf", 512 * t, 512 * t + 512), V("gt", 0, 512), [[0, 128], [1, 4]], ALU.is_ge, 0.0, -t - 1, 0)
+            iota(V("c9", 0, 512), [[0, 512]], 9, 0)
+            iota(V("sgf", 0, 2048), [[0, 2048]], 0, 0)
             for e in range(4):
                 quant("eq", "esc", 128 * e, 128 * e + 128, V("eb", 3 - e, 515 - e))
                 da_mm(b, e)
             da_cp("s", 0, 0)
-            da_cp("s", 1, 0)
-        da_cp("s", 2, 0)
-        da_cp("s", 3, 0)
+            da_cp("s", 1, 0, 2)
+        da_cp("s", 2, 0, 2)
+        da_cp("s", 3, 0, 2)
         big = 1.5 * 2.0 ** 25
         rcp(V("sm", 0, 1), S)
         ts(V("sm", 1, 2), S, -2.0, ca4, ALU.mult, ALU.add)
         ts(V("x4", 0, 128), V("ew", 0, 128), 4.0 * M, V("sm", 1, 2), ALU.mult, ALU.add)
-        ts(V("y4", 0, 128), V("x4", 0, 128), V("sm", 0, 1), big, ALU.mult, ALU.add)
-        ts(V("op", 0, 128), V("y4", 0, 128), big, tcol, ALU.subtract, ALU.add)
         da_cp("v", 0, 1)
-        da_cp("s", 1, 1)
-        da_cp("s", 2, 1)
-        da_cp("s", 3, 1)
-        if b == 1:
-            quant("gq", "gsc", 384, 768, V("gf", 0, 1536))
+        ts(V("y4", 0, 128), V("x4", 0, 128), V("sm", 0, 1), big, ALU.mult, ALU.add)
+        if early:
+            da_cp("s", 1, 1)
+        ts(V("op", 0, 128), V("y4", 0, 128), big, tcol, ALU.subtract, ALU.add)
         op("x", None, [], [lq, ls], sem=("arr%d" % b, 2 * n))
         for e in (0, 2, 1, 3):
             mm(e, "eq", "esc", 128 * e, "cvq", "cvs", CV * b, CV * b + 128)
@@ -355,9 +353,18 @@ def rank_program(g, core, T, topo):
         v = V("aq", TC * R + a0, TC * R + a1)
         store("y", T.oc[:, 4 * a0:4 * a1], v[0].bitcast(dt.uint8), [v])
 
+    def st_scales(e, k):
+        store(e, T.osc[4 * k:4 * k + 4, :], T.asc[32 * k:32 * k + 4, TC * R:TC * R + TC], [V("asc", TC * R, TC * R + TC)])
+
     def st_y(e, a0, a1):
         v = V("ys", a0, a1)
         store(e, T.y[:, a0:a1], v[0], [v])
+
+    def last_clocks(a0, a1, bank):
+        o = 128 * R
+        quant("sq", "ssc", o + a0, o + a1, V("sgf", 4 * a0, 4 * a1))
+        mm(bank, "gq", "gsc", 0, "sq", "ssc", o + a0, o + a1)
+        scan(V("cs", a0, a1), V("p%d" % bank, 0, a1 - a0), V("c9", a0, a1), V("cs", a0 - 1, a0) if a0 else 0.0, ALU.add, ALU.add)
 
     sent = []
     n = len(CH)
@@ -365,57 +372,40 @@ def rank_program(g, core, T, topo):
         q_state(0, a0, a1)
         z_mm(0, a0, a1, c % 2)
         z_sign(a0, a1, c % 2)
-    quant("gq", "gsc", 256, 384, V("gt", 1024, 1536))
+    rcp(V("r6", 0, 6), V("k6", 0, 6))
+    ts(V("m2", 0, 128), V("jq", 0, 128), tcol, 1.0e6, ALU.is_equal, ALU.mult)
     ts(V("m3", 0, 96), V("jq", 0, 96), qcol, 1.0e6, ALU.is_equal, ALU.mult)
     e1 = CH[-1][0]
     for b in range(R):
         exchange(b)
         fin = b == R - 1
-        e0 = 0
         for c in range(n):
             h_make(b, c)
-            now = [(a0, a1) for (k, a0, a1) in EARLY[b] if k == c]
-            for (a0, a1) in now:
-                q_state(b + 1, a0, a1)
-                z_mm(b + 1, a0, a1, 0)
-                if fin:
-                    st_codes(a0, a1)
-                e0 = a1
             if c < n - 1:
                 for i in range(4):
                     r_cp(b, c, i, "s")
-            for (a0, a1) in now:
-                z_sign(a0, a1, 0)
-                if fin:
-                    y_cp("s", a0, a1, 0)
-                    st_y("y", a0, a1)
-        q_state(b + 1, e0, e1)
-        z_mm(b + 1, e0, e1, 1)
+        q_state(b + 1, 0, e1)
+        z_mm(b + 1, 0, e1, 1)
         if fin:
-            st_codes(e0, e1)
-            z_mm(b + 1, e0, e1, 2)
+            st_codes(0, e1)
         for i in range(4):
             r_cp(b, n - 1, i, "s" if i % 2 == 0 else "v")
-        z_sign(e0, e1, 1)
+        z_sign(0, e1, 1, fin)
         q_state(b + 1, e1, TC)
         z_mm(b + 1, e1, TC, 0)
-        z_sign(e1, TC, 0)
+        if fin:
+            y_cp("s", 0, e1, 1)
+            last_clocks(0, e1, 2)
+        z_sign(e1, TC, 0, fin)
     st_codes(e1, TC)
-    y_cp("v", e0, e1, 2)
-    st_y("y", e0, e1)
-    for k in range(4):
-        store("y", T.osc[4 * k:4 * k + 4, :], T.asc[32 * k:32 * k + 4, TC * R:TC * R + TC], [V("asc", TC * R, TC * R + TC)])
+    st_y("y", 0, e1)
     y_cp("s", e1, TC, 0)
+    st_scales("y", 0)
     st_y("y", e1, TC)
-    quant("sq", "ssc", 128 * R, 128 * R + 128, V("sg", 0, 512))
-    mm(3, "gq", "gsc", 0, "sq", "ssc", 128 * R, 128 * R + 128)
-    for t in range(3):
-        mm(4 + t, "gq", "gsc", 384 + 128 * t, "sq", "ssc", 128 * R, 128 * R + 128)
-    scan(V("cs", 3, 512, 4), V("p3", 0, 128), V("c36", 0, 128), 0.0, ALU.add, ALU.add)
-    for t in range(3):
-        rest = V("rest", 128 * t, 128 * t + 128)
-        A(rest, V("p%d" % (4 + t), 0, 128), ACT.Identity, bias=9.0 * (3 - t))
-        scan(V("cs", t, 512, 4), V("cs", 3, 512, 4), rest, 0.0, ALU.max, ALU.subtract)
+    st_scales("y", 1)
+    st_scales("y", 2)
+    st_scales("s", 3)
+    last_clocks(e1, TC, 3)
     store("s", T.cl[:], T.cs[0:128:16, :], [V("cs", 0, 512)])
     op("y", None, outs, [])
     emit(ops, {"g": g, "v": vec, "s": act, "t": pe, "y": syn}, T)

@@ -1,9 +1,14 @@
-from concourse.mybir import dt, AluOpType as ALU, ActivationFunctionType as ACT
+from concourse.bass import DstId, RemoteDMATransfer
+from concourse.mybir import dt, AluOpType as ALU, ActivationFunctionType as ACT, AxisListType as AX
 
 TC, M, R = 512, 96, 3
 CH = [(0, 288), (288, 512)]
 XC = [(0, 320), (320, 512)]
-CV = 224
+DA = CH[0][1]
+DB = (5, 6, 7, 1)
+CW = 128
+CQ, CS = CW + M, CW + 4 * M
+AS = 128 + TC
 F8, U8, BF, F32, I32, U16 = "float8_e4m3fn_x4", "uint8", "bfloat16", "float32", "int32", "uint16"
 
 
@@ -13,29 +18,29 @@ def _sb(n, d):
 
 SCRATCH = {
     "t0": _sb(2048, BF), "t1": _sb(2048, BF), "t2": _sb(2048, BF), "t3": _sb(2048, BF),
-    "aq": _sb(4 * TC, F8), "asc": _sb(4 * TC, U8),
+    "aq": _sb(4 * TC, F8), "asc": _sb(4 * AS, U8),
     "ut": _sb(512, BF), "uq": _sb(128, F8), "usc": _sb(128, U8),
     "wq": _sb(512, F8), "wsc": _sb(512, U8),
     "ht": _sb(2048, BF), "hq": _sb(R * TC, F8), "hsc": _sb(R * TC, U8),
-    "da": _sb(2048, BF), "dv": _sb(384, BF), "vt": _sb(512, BF),
-    "cvq": _sb(R * CV, F8), "cvs": _sb(R * CV, U8),
+    "da": _sb(2048, BF), "dg": _sb(2048, BF), "dv": _sb(384, BF), "vt": _sb(512, BF),
+    "vq": _sb(R * 128, F8),
     "sg": _sb(512, BF), "sgf": _sb(2048, BF), "sq": _sb(R * 128 + TC, F8), "ssc": _sb(R * 128 + TC, U8),
-    "cmp": _sb(512, BF), "cq": _sb(R * 128, F8), "csc": _sb(R * 128, U8),
-    "half": _sb(528, BF), "eb": _sb(528, BF), "eq": _sb(512, F8), "esc": _sb(512, U8),
+    "cmp": _sb(4 * CW, BF), "cq": _sb(R * CQ, F8), "csc": _sb(R * CS, U8),
+    "eb": _sb(528, BF), "eq": _sb(512, F8), "esc": _sb(512, U8),
     "nq": _sb(128, BF), "gt": _sb(1536, BF), "gq": _sb(384, F8), "gsc": _sb(384, U8),
     "pi": _sb(4, I32), "ri": _sb(4, I32), "rf": _sb(4, F32), "col": _sb(8, F32), "tiny": _sb(4, F32),
     "jq": _sb(128, F32), "iw": _sb(128, F32), "c36": _sb(128, F32), "c9": _sb(512, F32),
-    "k6": _sb(8, F32), "r6": _sb(8, F32), "w6": _sb(8, F32), "k96": _sb(96, F32), "m2": _sb(128, F32), "m3": _sb(96, F32),
+    "k6": _sb(8, F32), "r6": _sb(8, F32), "w6": _sb(8, F32), "k96": _sb(96, F32), "m2": _sb(128, F32),
     "cw": _sb(128, F32), "ew": _sb(128, F32), "ed": _sb(128, F32), "th96": _sb(96, F32),
     "junk": _sb(192, F32), "acc": _sb(8, F32), "brep": _sb(96, F32), "bsel": _sb(96, F32), "s24": _sb(24, F32),
-    "o2": _sb(8, U16), "ov": _sb(24, U16), "op": _sb(128, U16),
-    "sm": _sb(8, F32), "x4": _sb(128, F32), "y4": _sb(128, F32),
+    "o2": _sb(8, U16), "ov": _sb(24, U16), "op": _sb(32, U16),
+    "sm": _sb(8, F32), "x4": _sb(32, F32), "y4": _sb(32, F32),
     "ys": _sb(512, F32), "cs": _sb(512, F32),
 }
 for _b in range(8):
     SCRATCH["p%d" % _b] = ("psum", [128, 512], F32)
 
-NC, ND = 60, 20
+NC, ND = 80, 20
 SEMAPHORES = ["arr0", "arr1", "arr2", "left"] + ["c%d" % _i for _i in range(NC)] + ["d%d" % _i for _i in range(ND)]
 
 
@@ -157,12 +162,15 @@ def rank_program(g, core, T, topo):
     def rcp(out, a):
         op("v", lambda: vec.reciprocal(out[0], a[0]), [a], [out])
 
+    def total(out, a):
+        op("v", lambda: vec.tensor_reduce(out[0], a[0], AX.X, ALU.add), [a], [out])
+
     def scan(out, d0, d1, init, o0, o1):
         op("v", lambda: vec.tensor_tensor_scan(out[0], d0[0], d1[0], ap(init), o0, o1),
            [d0, d1] + ([init] if isv(init) else []), [out])
 
-    def quant(q, s, a, b, src):
-        vq, vs = V(q, a, b), V(s, a, b)
+    def quant(q, s, a, b, src, d=0):
+        vq, vs = V(q, a, b), V(s, a + d, b + d)
         op("v", lambda: vec.quantize_mx(vq[0], vs[0], src[0]), [src], [vq, vs])
 
     def A(out, a, func, bias=0.0, scale=1.0, acc=None):
@@ -172,9 +180,9 @@ def rank_program(g, core, T, topo):
         else:
             op("s", lambda: act.activation(out[0], a[0], func, bias=ap(bias), scale=ap(scale), accum_out=acc[0]), r, [out, acc])
 
-    def mm(bank, lq, ls, l0, rq, rs, a, b):
+    def mm(bank, lq, ls, l0, rq, rs, a, b, d=0):
         out = V("p%d" % bank, 0, b - a)
-        w, ws_, x, xs = V(lq, l0, l0 + 128), V(ls, l0, l0 + 128), V(rq, a, b), V(rs, a, b)
+        w, ws_, x, xs = V(lq, l0, l0 + 128), V(ls, l0, l0 + 128), V(rq, a, b), V(rs, a + d, b + d)
         op("t", lambda: pe.matmul_mx(out[0], w[0], ws_[0], x[0], xs[0], True, True), [w, ws_, x, xs], [out])
 
     def iota(out, pat, base, cm, flt=True):
@@ -213,26 +221,27 @@ def rank_program(g, core, T, topo):
     dma("y", T.wq[:].bitcast(dt.uint8), T.wc[:], [somex], [V("wq", 0, 512)])
     dma("y", T.wsc[:], T.ws[:], [somex], [V("wsc", 0, 512)])
 
-    rcol, qcol, tcol = V("rf", 0, 1), V("rf", 1, 2), V("rf", 2, 3)
+    rcol, qcol, tcol, pcol = V("rf", 0, 1), V("rf", 1, 2), V("rf", 2, 3), V("rf", 3, 4)
     cthr, ca4, ct52 = V("col", 0, 1), V("col", 1, 2), V("col", 2, 3)
     tiny = V("tiny", 0, 1)
     iota(V("pi", 0, 1), [[0, 1]], 0, 1, False)
-    iota(V("nq", 0, 128), [[0, 8], [1, 4], [0, 4]], 0, 0)
+    iota(V("nq", 0, 128), [[0, 8], [0, 4], [1, 4]], 0, 0)
     sel(V("nq", 0, 128), V("nq", 0, 128), [[-16, 8], [0, 16]], ALU.is_ge, 99.0, 0, 1)
     sel(V("nq", 0, 128), V("nq", 0, 128), [[16, 8], [0, 16]], ALU.is_ge, 99.0, 15, -1)
     iota(V("iw", 0, 128), [[1, 128]], 0, 0)
     iota(V("jq", 0, 128), [[0, 32], [1, 4]], 0, 0)
     ms(tiny, -2.0 ** -120)
-    ms(V("half", 0, 528), 0.5)
-    ms(V("cmp", 96, 512), 0.0)
+    ms(V("eb", 0, 528), 0.0)
+    ms(V("cmp", 96, 4 * CW), 0.0)
     ms(V("vt", 384, 512), 0.0)
     ms(V("c36", 0, 128), 36.0)
     ts(V("ri", 0, 1), V("pi", 0, 1), 15, None, ALU.bitwise_and)
     ts(V("ri", 1, 2), V("pi", 0, 1), 2, 3, ALU.arith_shift_right, ALU.bitwise_and)
     ts(V("ri", 2, 3), V("pi", 0, 1), 3, None, ALU.bitwise_and)
     cp(V("rf", 0, 3), V("ri", 0, 3))
-    A(cthr, qcol, ACT.Identity, bias=36.0 + 0.5 / M, scale=-9.0)
-    A(ca4, qcol, ACT.Identity, bias=2.0 - 144.0 * M, scale=36.0 * M)
+    cp(pcol, V("pi", 0, 1))
+    A(cthr, tcol, ACT.Identity, bias=36.0 + 0.5 / M, scale=-9.0)
+    A(ca4, tcol, ACT.Identity, bias=2.0 - 144.0 * M, scale=36.0 * M)
     A(ct52, tcol, ACT.Identity, bias=-52.0)
     for s in (3, 2, 1, 0):
         ts(V("gt", 512 + s, 1024, 4), V("nq", 0, 128), float(s), 0.5, ALU.is_le, ALU.mult)
@@ -241,110 +250,124 @@ def rank_program(g, core, T, topo):
         ts(V("gt", 2 + s, 512, 4), V("nq", 0, 128), 3.0, 0.5, ALU.is_le, ALU.mult)
     for s in range(4):
         sel(V("gt", 1024 + s, 1536, 4), V("gt", 515, 1024, 4), [[0, 8], [-1, 4], [0, 4]], ALU.is_equal, 0.0, s, 0)
-    sel(V("eb", 0, 528), V("half", 0, 528), [[-1, 528]], ALU.is_equal, 0.0, 3, 4)
+    ts(V("eb", 3, 515, 4), V("iw", 0, 128), pcol, 0.5, ALU.is_equal, ALU.mult)
     quant("gq", "gsc", 0, 256, V("gt", 0, 1024))
     ts(V("k6", 0, 6), V("iw", 0, 96, 16), rcol, 1.0e-4, ALU.add, ALU.max)
+    for e in range(4):
+        quant("eq", "esc", 128 * e, 128 * e + 128, V("eb", 3 - e, 515 - e))
     quant("uq", "usc", 0, 128, V("ut", 0, 512))
     A(V("k96", 0, 96), V("iw", 0, 96), ACT.Copy, scale=1.0 / M)
 
     def q_state(b, a0, a1):
-        quant("aq", "asc", TC * b + a0, TC * b + a1, V("t%d" % b, 4 * a0, 4 * a1))
+        quant("aq", "asc", TC * b + a0, TC * b + a1, V("t%d" % b, 4 * a0, 4 * a1), 128 * (b + 1))
 
     def z_mm(b, a0, a1, bank):
-        mm(bank, "uq", "usc", 0, "aq", "asc", TC * b + a0, TC * b + a1)
+        mm(bank, "uq", "usc", 0, "aq", "asc", TC * b + a0, TC * b + a1, 128 * (b + 1))
 
     def z_sign(a0, a1, bank, fin=False):
         A(V("sgf", 4 * a0, 4 * a1, 4) if fin else V("sg", a0, a1), V("p%d" % bank, 0, a1 - a0), ACT.Sign, bias=tiny)
 
-    def da_mm(b, e):
-        mm(4 + e, "eq", "esc", 128 * e, "aq", "asc", TC * b, TC * b + TC)
+    def da_mm(b, e, bank, a0, a1):
+        mm(bank, "eq", "esc", 128 * e, "aq", "asc", TC * b + a0, TC * b + a1, 128 * (b + 1))
 
-    def da_cp(eng, e, h, k=1):
-        move(eng, V("da", 1024 * h + e, 1024 * (h + k), 4), V("p%d" % (4 + e), 256 * h, 256 * (h + k)), 1.0)
+    def da_cp(eng, e):
+        move(eng, V("da", DA * e, DA * (e + 1)), V("p%d" % DB[e], 0, DA), 1.0)
+
+    def way(b):
+        peer = T.cores[rank ^ (1 << (b % 2))]
+        rid, pid, _ = topo.addr(peer)
+        return rid, pid, topo.engines(core, peer)
+
+    def send_first():
+        rid, pid, eng = way(0)
+        mask = sum(1 << e for e in eng)
+        sq_, ss_, lq, ls = V("aq", 0, 1), V("asc", 128, 129), V("cq", CW, CW + 1), V("csc", CW, CW + 1)
+        op("g", lambda: g.remote_dma(lq[0].bitcast(dt.uint8), sq_[0].bitcast(dt.uint8), T.sem.arr0, T.sem.left, pid, rid, mask), [sq_], [])
+        op("g", lambda: g.remote_dma(ls[0], ss_[0], T.sem.arr0, T.sem.left, pid, rid, mask), [ss_], [])
+        sent[0] += 2 * len(eng)
 
     def exchange(b):
-        early = b > 0
         S = V("cw", 127, 128)
-        if early:
-            da_mm(b, 0)
         quant("sq", "ssc", 128 * b, 128 * b + 128, V("sg", 0, 512))
         mm(2, "gq", "gsc", 0, "sq", "ssc", 128 * b, 128 * b + 128)
         mm(3, "gq", "gsc", 128, "sq", "ssc", 128 * b, 128 * b + 128)
-        if early:
-            da_mm(b, 1)
-            da_cp("s", 0, 0)
-        else:
-            A(V("w6", 0, 6), V("r6", 0, 6), ACT.Copy, scale=-M * (1.0 - 5.0e-7))
+        if b == 0:
+            A(V("w6", 0, 4), V("r6", 0, 4), ACT.Copy, scale=-M * (1.0 - 5.0e-7))
+            A(V("w6", 4, 6), V("r6", 4, 6), ACT.Copy, scale=M * (1.0 - 5.0e-7))
         scan(V("cw", 0, 128), V("p2", 0, 128), V("c36", 0, 128), 0.0, ALU.add, ALU.add)
-        for m in range(6):
+        for m in range(4):
             A(V("junk", 32 * m, 32 * m + 32), V("cw", 3, 128, 4), ACT.Sign, bias=S, scale=V("w6", m, m + 1), acc=V("acc", m, m + 1))
+        for m in range(4, 6):
+            ts(V("junk", 32 * m, 32 * m + 32), V("cw", 3, 128, 4), V("w6", m, m + 1), S, ALU.mult, ALU.is_lt)
         tt(V("ew", 0, 128), V("cw", 0, 128), V("p3", 0, 128), ALU.subtract)
+        for m in range(4, 6):
+            total(V("acc", m, m + 1), V("junk", 32 * m, 32 * m + 32))
         ts(V("th96", 0, 96), V("k96", 0, 96), S, cthr, ALU.mult, ALU.add)
         scan(V("ed", 0, 128), V("m2", 0, 128), V("ew", 0, 128), 0.0, ALU.max, ALU.min)
-        if not early:
-            quant("gq", "gsc", 256, 384, V("gt", 1024, 1536))
-        ts(V("o2", 0, 6), V("acc", 0, 6), 2.0, 67.0, ALU.mult, ALU.add)
+        ts(V("o2", 4, 6), V("acc", 4, 6), 4.0, 3.0, ALU.mult, ALU.add)
+        ts(V("o2", 0, 4), V("acc", 0, 4), 2.0, 67.0, ALU.mult, ALU.add)
         tt(V("cmp", 0, 96), IND(V("ed", 0, 128), V("o2", 0, 6)), V("th96", 0, 96), ALU.is_le)
         A(V("brep", 0, 96), IND(V("iw", 0, 128), V("o2", 0, 6)), ACT.Copy, scale=2.0)
-        if early:
-            da_cp("s", 1, 0)
-        quant("cq", "csc", 128 * b, 128 * b + 128, V("cmp", 0, 512))
-        mm(0, "gq", "gsc", 256, "cq", "csc", 128 * b, 128 * b + 128)
-        if early:
-            da_mm(b, 2)
-            da_mm(b, 3)
-        scan(V("bsel", 0, 96), V("m3", 0, 96), V("brep", 0, 96), 0.0, ALU.max, ALU.min)
+        da_cp("s", 2)
+        dc = (CS - CQ) * b
+        quant("cq", "csc", CQ * b, CQ * b + CW, V("cmp", 0, 4 * CW), dc)
+        mm(0, "gq", "gsc", 256, "cq", "csc", CQ * b, CQ * b + 128, dc)
+        scan(V("bsel", 0, 96), V("m2", 0, 96), V("brep", 0, 96), 0.0, ALU.max, ALU.min)
         tt(V("s24", 0, 24), V("p0", 0, 24), V("bsel", 3, 96, 4), ALU.add)
         ts(V("ov", 0, 24), V("s24", 0, 24), 8.0, ct52, ALU.mult, ALU.add)
         st = V("t%d" % b, 0, 2048)
         cp(V("vt", 0, 192), IND(st, V("ov", 0, 12)))
         A(V("vt", 192, 384), IND(st, V("ov", 12, 24)), ACT.Copy)
-        own = CV * b + M
-        quant("cvq", "cvs", own, own + 128, V("vt", 0, 512))
-        peer = T.cores[rank ^ (1 << (b % 2))]
-        rid, pid, _ = topo.addr(peer)
-        mask = topo.mask(core, peer)
-        n = len(topo.engines(core, peer))
-        sq_, ss_, lq, ls = V("cvq", own, own + M), V("cvs", own, own + M), V("cvq", CV * b, own), V("cvs", CV * b, own)
+        quant("vq", "asc", 128 * b, 128 * b + 128, V("vt", 0, 512), TC * b)
+        f = 1 if b == 0 else 0
+        rid, pid, eng = way(b)
+        h = len(eng) // 2
+        sq_, ss_ = V("vq", 128 * b + f, 128 * b + M), V("asc", AS * b + f, AS * b + f + 4 * (M - f))
+        lq, ls = V("cq", CQ * b + CW + f, CQ * (b + 1)), V("csc", CS * b + CW + f, CS * b + CW + f + 4 * (M - f))
         arr = T.sem["arr%d" % b]
-        op("g", lambda: g.remote_dma(lq[0].bitcast(dt.uint8), sq_[0].bitcast(dt.uint8), arr, T.sem.left, pid, rid, mask), [sq_], [])
-        op("g", lambda: g.remote_dma(ls[0], ss_[0], arr, T.sem.left, pid, rid, mask), [ss_], [])
-        sent.append(2 * n)
+        to = [DstId(rid=rid, pnc=pid)]
+        pair = [RemoteDMATransfer(dst_ids=to, dma_engine_mask=sum(1 << e for e in eng[:h]), remote_sem=arr,
+                                  src=sq_[0].bitcast(dt.uint8), dst=lq[0].bitcast(dt.uint8)),
+                RemoteDMATransfer(dst_ids=to, dma_engine_mask=sum(1 << e for e in eng[h:]), remote_sem=arr, src=ss_[0], dst=ls[0])]
+        op("g", lambda: g.remote_dma_fused(pair, local_sem=T.sem.left), [sq_, ss_], [])
+        sent[b] += len(eng)
         if b == 0:
             iota(V("c9", 0, 512), [[0, 512]], 9, 0)
             iota(V("sgf", 0, 2048), [[0, 2048]], 0, 0)
-            for e in range(4):
-                quant("eq", "esc", 128 * e, 128 * e + 128, V("eb", 3 - e, 515 - e))
-                da_mm(b, e)
-            da_cp("s", 0, 0)
-            da_cp("s", 1, 0, 2)
-        da_cp("s", 2, 0, 2)
-        da_cp("s", 3, 0, 2)
+        da_cp("s", 3)
+        if b == 0:
+            da_cp("v", 0)
+            da_cp("s", 1)
         big = 1.5 * 2.0 ** 25
         rcp(V("sm", 0, 1), S)
         ts(V("sm", 1, 2), S, -2.0, ca4, ALU.mult, ALU.add)
-        ts(V("x4", 0, 128), V("ew", 0, 128), 4.0 * M, V("sm", 1, 2), ALU.mult, ALU.add)
-        da_cp("v", 0, 1)
-        ts(V("y4", 0, 128), V("x4", 0, 128), V("sm", 0, 1), big, ALU.mult, ALU.add)
-        if early:
-            da_cp("s", 1, 1)
-        ts(V("op", 0, 128), V("y4", 0, 128), big, tcol, ALU.subtract, ALU.add)
-        op("x", None, [], [lq, ls], sem=("arr%d" % b, 2 * n))
-        for e in (0, 2, 1, 3):
-            mm(e, "eq", "esc", 128 * e, "cvq", "cvs", CV * b, CV * b + 128)
-        for e in (0, 2, 1, 3):
-            move("v" if e < 2 else "s", V("dv", e, 384, 4), V("p%d" % e, 0, M), 1.0)
+        ts(V("x4", 0, 32), V("ed", 3, 128, 4), 4.0 * M, V("sm", 1, 2), ALU.mult, ALU.add)
+        ts(V("y4", 0, 32), V("x4", 0, 32), V("sm", 0, 1), big, ALU.mult, ALU.add)
+        ts(V("op", 0, 32), V("y4", 0, 32), big, 0.25, ALU.subtract, ALU.mult)
+        op("x", None, [], [V("cq", CQ * b + CW, CQ * (b + 1)), V("csc", CS * b + CW, CS * (b + 1))], sem=("arr%d" % b, sent[b]))
+        for e in range(4):
+            mm(e, "eq", "esc", 128 * e, "cq", "csc", CQ * (b + 1) - 128, CQ * (b + 1), dc)
+        for e in range(4):
+            move("v" if e == 0 else "s", V("dv", M * e, M * (e + 1)), V("p%d" % e, 128 - M, 128), 1.0)
+            da_mm(b, e, e, DA, TC)
 
     def h_make(b, c):
         a0, a1 = CH[c]
-        tt(V("ht", 4 * a0, 4 * a1), IND(V("dv", 0, 384), V("op", a0 // 4, a1 // 4)), V("da", 4 * a0, 4 * a1), ALU.add)
+        for e in range(4):
+            out, win = V("ht", 4 * a0 + e, 4 * a1, 4), V("dv", M * e, M * (e + 1))
+            dg = V("dg", TC * e + DA, TC * (e + 1))
+            if c == 0:
+                tt(out, IND(win, V("op", 0, DA // 16)), V("da", DA * e, DA * (e + 1)), ALU.add)
+                A(dg, IND(win, V("op", DA // 16, TC // 16)), ACT.Copy)
+            else:
+                tt(out, V("p%d" % e, 0, a1 - a0), dg, ALU.add)
         quant("hq", "hsc", TC * b + a0, TC * b + a1, V("ht", 4 * a0, 4 * a1))
         for i in range(4):
-            mm(4 + i, "wq", "wsc", 128 * i, "hq", "hsc", TC * b + a0, TC * b + a1)
+            mm(4 * (1 - c) + i, "wq", "wsc", 128 * i, "hq", "hsc", TC * b + a0, TC * b + a1)
 
     def r_cp(b, c, i, eng):
         a0, a1 = CH[c]
-        move(eng, V("t%d" % (b + 1), 4 * a0 + i, 4 * a1, 4), V("p%d" % (4 + i), 0, a1 - a0), 0.03125)
+        move(eng, V("t%d" % (b + 1), 4 * a0 + i, 4 * a1, 4), V("p%d" % (4 * (1 - c) + i), 0, a1 - a0), 0.03125)
 
     def y_cp(eng, a0, a1, bank):
         move(eng, V("ys", a0, a1), V("p%d" % bank, 0, a1 - a0), 1.0)
@@ -354,7 +377,8 @@ def rank_program(g, core, T, topo):
         store("y", T.oc[:, 4 * a0:4 * a1], v[0].bitcast(dt.uint8), [v])
 
     def st_scales(e, k):
-        store(e, T.osc[4 * k:4 * k + 4, :], T.asc[32 * k:32 * k + 4, TC * R:TC * R + TC], [V("asc", TC * R, TC * R + TC)])
+        o = AS * R + 128
+        store(e, T.osc[4 * k:4 * k + 4, :], T.asc[32 * k:32 * k + 4, o:o + TC], [V("asc", o, o + TC)])
 
     def st_y(e, a0, a1):
         v = V("ys", a0, a1)
@@ -366,37 +390,49 @@ def rank_program(g, core, T, topo):
         mm(bank, "gq", "gsc", 0, "sq", "ssc", o + a0, o + a1)
         scan(V("cs", a0, a1), V("p%d" % bank, 0, a1 - a0), V("c9", a0, a1), V("cs", a0 - 1, a0) if a0 else 0.0, ALU.add, ALU.add)
 
-    sent = []
-    n = len(CH)
+    sent = [0] * R
     for c, (a0, a1) in enumerate(XC):
         q_state(0, a0, a1)
-        z_mm(0, a0, a1, c % 2)
-        z_sign(a0, a1, c % 2)
+        if c == 0:
+            send_first()
+        z_mm(0, a0, a1, 4 * (1 - c))
+        z_sign(a0, a1, 4 * (1 - c))
     rcp(V("r6", 0, 6), V("k6", 0, 6))
-    ts(V("m2", 0, 128), V("jq", 0, 128), tcol, 1.0e6, ALU.is_equal, ALU.mult)
-    ts(V("m3", 0, 96), V("jq", 0, 96), qcol, 1.0e6, ALU.is_equal, ALU.mult)
-    e1 = CH[-1][0]
+    for e in range(4):
+        da_mm(0, e, DB[e], 0, DA)
+    ts(V("m2", 0, 128), V("jq", 0, 128), qcol, 1.0e6, ALU.is_equal, ALU.mult)
+    quant("gq", "gsc", 256, 384, V("gt", 1024, 1536))
+    e1 = DA
     for b in range(R):
         exchange(b)
         fin = b == R - 1
-        for c in range(n):
-            h_make(b, c)
-            if c < n - 1:
-                for i in range(4):
-                    r_cp(b, c, i, "s")
+        h_make(b, 0)
+        for i in range(3):
+            r_cp(b, 0, i, "s")
+        h_make(b, 1)
+        r_cp(b, 0, 3, "v")
         q_state(b + 1, 0, e1)
-        z_mm(b + 1, 0, e1, 1)
+        z_mm(b + 1, 0, e1, 4)
         if fin:
             st_codes(0, e1)
         for i in range(4):
-            r_cp(b, n - 1, i, "s" if i % 2 == 0 else "v")
-        z_sign(0, e1, 1, fin)
+            r_cp(b, 1, i, "s" if i % 2 == 0 else "v")
+        z_sign(0, e1, 4, fin)
+        if not fin:
+            da_mm(b + 1, 0, DB[0], 0, DA)
+            da_mm(b + 1, 1, DB[1], 0, DA)
         q_state(b + 1, e1, TC)
         z_mm(b + 1, e1, TC, 0)
         if fin:
-            y_cp("s", 0, e1, 1)
-            last_clocks(0, e1, 2)
+            y_cp("s", 0, e1, 4)
+            last_clocks(0, e1, 5)
+        else:
+            da_mm(b + 1, 2, DB[2], 0, DA)
+            da_mm(b + 1, 3, DB[3], 0, DA)
         z_sign(e1, TC, 0, fin)
+        if not fin:
+            da_cp("v", 0)
+            da_cp("s", 1)
     st_codes(e1, TC)
     st_y("y", 0, e1)
     y_cp("s", e1, TC, 0)
@@ -405,7 +441,7 @@ def rank_program(g, core, T, topo):
     st_scales("y", 1)
     st_scales("y", 2)
     st_scales("s", 3)
-    last_clocks(e1, TC, 3)
+    last_clocks(e1, TC, 6)
     store("s", T.cl[:], T.cs[0:128:16, :], [V("cs", 0, 512)])
     op("y", None, outs, [])
     emit(ops, {"g": g, "v": vec, "s": act, "t": pe, "y": syn}, T)

@@ -1,11 +1,22 @@
 from concourse.bass import DstId, RemoteDMATransfer
-from concourse.mybir import dt, AluOpType as ALU, ActivationFunctionType as ACT, AxisListType as AX
+from concourse.mybir import dt, AluOpType as ALU, ActivationFunctionType as ACT
 
 TC, M, R = 512, 96, 3
-CH = [(0, 288), (288, 512)]
-XC = [(0, 320), (320, 512)]
-DA = CH[0][1]
-DB = (5, 6, 7, 1)
+CFG = {
+    "ch": [0, 192, 384, 512],
+    "h": ["vvss", "vvss", "vvss"],
+    "r": ["ssss", "ssss", "svvs"],
+    "fch": [0, 256, 384, 512], "fh": ["vvss", "vvss", "vvss"], "fr": ["ssss", "ssss", "svvs"],
+    "dv": "vsss", "dvo": [0, 2, 1, 3],
+    "da": "vsvv",
+    "xc": [0, 352, 512], "xq": "sy",
+    "nv": 1, "th": "s", "bt": "ssss",
+    "y": "sss", "soc": [1, 2, 3], "sy": [1, 3], "oq": "yyys",
+    "zl": 1,
+    "wake": 0.1, "gat": 1.5, "pe": 0.8, "far": 2.0, "cy": 0.95e-3,
+    "bias": {"nh10.0": 0.8, "nw20.0": -0.1, "sz0.2": -1.6, "xdv0.0": 0.7, "xdv3.1": -1.0, "fh11.0": 0.8, "fw10.0": -0.8,
+             "nh20.0": 0.4, "nh12.0": -0.6, "fl384.0": -0.7, "xdv2.1": -0.8, "fh22.1": 0.4, "fz0.1": -0.8, "fh21.0": -0.2},
+}
 CW = 128
 CQ, CS = CW + M, CW + 4 * M
 AS = 128 + TC
@@ -27,12 +38,13 @@ SCRATCH = {
     "sg": _sb(512, BF), "sgf": _sb(2048, BF), "sq": _sb(R * 128 + TC, F8), "ssc": _sb(R * 128 + TC, U8),
     "cmp": _sb(4 * CW, BF), "cq": _sb(R * CQ, F8), "csc": _sb(R * CS, U8),
     "eb": _sb(528, BF), "eq": _sb(512, F8), "esc": _sb(512, U8),
-    "nq": _sb(128, BF), "gt": _sb(1536, BF), "gq": _sb(384, F8), "gsc": _sb(384, U8),
+    "nq": _sb(128, BF), "nqq": _sb(128, BF), "gt": _sb(2048, BF), "gq": _sb(512, F8), "gsc": _sb(512, U8),
+    "bt": _sb(512, BF), "bq": _sb(R * 128, F8), "bsc": _sb(R * 128, U8), "mq": _sb(4, F32),
     "pi": _sb(4, I32), "ri": _sb(4, I32), "rf": _sb(4, F32), "col": _sb(8, F32), "tiny": _sb(4, F32),
     "jq": _sb(128, F32), "iw": _sb(128, F32), "c36": _sb(128, F32), "c9": _sb(512, F32),
     "k6": _sb(8, F32), "r6": _sb(8, F32), "w6": _sb(8, F32), "k96": _sb(96, F32), "m2": _sb(128, F32),
     "cw": _sb(128, F32), "ew": _sb(128, F32), "ed": _sb(128, F32), "th96": _sb(96, F32),
-    "junk": _sb(192, F32), "acc": _sb(8, F32), "brep": _sb(96, F32), "bsel": _sb(96, F32), "s24": _sb(24, F32),
+    "junk": _sb(192, F32), "acc": _sb(104, F32),
     "o2": _sb(8, U16), "ov": _sb(24, U16), "op": _sb(32, U16),
     "sm": _sb(8, F32), "x4": _sb(32, F32), "y4": _sb(32, F32),
     "ys": _sb(512, F32), "cs": _sb(512, F32),
@@ -40,12 +52,71 @@ SCRATCH = {
 for _b in range(8):
     SCRATCH["p%d" % _b] = ("psum", [128, 512], F32)
 
-NC, ND = 80, 20
+NC, ND = 110, 24
 SEMAPHORES = ["arr0", "arr1", "arr2", "left"] + ["c%d" % _i for _i in range(NC)] + ["d%d" % _i for _i in range(ND)]
+ORDERS = {}
 
 
 def is_bank(k):
     return k[0] == "p" and k[1:].isdigit()
+
+
+def meets(o, p, waits=False):
+    for (k, m) in o["r"]:
+        if p["W"].get(k, 0) & m or (k in p["R"] and p["e"] != o["e"] and is_bank(k)):
+            return True
+    for (k, m) in o["w"]:
+        if waits and o.get("adds") and p["e"] == "t":
+            continue
+        if (p["W"].get(k, 0) | p["R"].get(k, 0)) & m:
+            return True
+    return False
+
+
+def hazards(ops):
+    users, hz = {}, []
+    for i, o in enumerate(ops):
+        near = set()
+        for k in list(o["R"]) + list(o["W"]):
+            near.update(users.get(k, ()))
+        hz.append([j for j in near if meets(o, ops[j])])
+        for k in list(o["R"]) + list(o["W"]):
+            users.setdefault(k, set()).add(i)
+    return hz
+
+
+def layout(ops, hz, bias):
+    n, wake = len(ops), CFG["wake"]
+    deps = [[(j, ops[j]["lat"] + wake) for j in hz[i]] + ops[i]["after"] for i in range(n)]
+    rest = [o["lat"] for o in ops]
+    for i in range(n - 1, -1, -1):
+        for (j, t) in deps[i]:
+            rest[j] = max(rest[j], rest[i] + t)
+    rank = [rest[i] + bias.get(ops[i]["role"], 0.0) for i in range(n)]
+    for i in range(n):
+        for (j, t) in deps[i]:
+            rank[i] = min(rank[i], rank[j])
+    start, busy = [0.0] * n, {}
+    for i in sorted(range(n), key=lambda i: (-rank[i], i)):
+        t = max([start[j] + d for (j, d) in deps[i]] + [0.0])
+        slots, need = busy.setdefault(ops[i]["e"], []), ops[i]["occ"]
+        k = len(slots)
+        for s, (a, b) in enumerate(slots):
+            if b > t:
+                if a >= t + need:
+                    k = s
+                    break
+                t = b
+        slots.insert(k, (t, t + need))
+        start[i] = t
+    return sorted(range(n), key=lambda i: (start[i], i))
+
+
+def arrange(ops):
+    key = repr(CFG)
+    if key not in ORDERS:
+        ORDERS[key] = layout(ops, hazards(ops), CFG["bias"])
+    return [ops[i] for i in ORDERS[key]]
 
 
 def emit(ops, queues, T):
@@ -60,14 +131,7 @@ def emit(ops, queues, T):
             if known[o["e"]] >> j & 1:
                 continue
             p = ops[j]
-            hit = False
-            for (k, m) in o["r"]:
-                if p["W"].get(k, 0) & m or (is_bank(k) and k in p["R"] and p["e"] != o["e"]):
-                    hit = True
-            for (k, m) in o["w"]:
-                if (p["W"].get(k, 0) | p["R"].get(k, 0)) & m:
-                    hit = True
-            if hit:
+            if meets(o, p, True):
                 o["waits"].append(j)
                 p["by"].append(i)
                 known[o["e"]] |= p["done"]
@@ -110,6 +174,11 @@ def rank_program(g, core, T, topo):
         return
     ops = []
     vec, act, pe, syn = g.vector, g.scalar, g.tensor, g.sync
+    CY = CFG["cy"]
+    part = ["s", "", 0]
+
+    def lab(t):
+        part[1:] = [t, 0]
 
     def V(name, a, b, s=1):
         m = 0
@@ -120,22 +189,25 @@ def rank_program(g, core, T, topo):
         else:
             for c in range(a, b, s):
                 m |= 1 << c
-        return (T[name][:, a:b] if s == 1 else T[name][:, a:b:s], [(name, m)])
+        return (T[name][:, a:b] if s == 1 else T[name][:, a:b:s], [(name, m)], len(range(a, b, s)))
 
     def IND(win, off):
-        return (win[0].indirect(off[0]), win[1] + off[1])
+        return (win[0].indirect(off[0]), win[1] + off[1], 16 * off[2], True)
 
-    def op(e, f, r, w, dma=False, sem=None):
+    def op(e, f, r, w, occ, lat=None, dma=False, sem=None, after=(), nb=0):
         rr = [a for v in r for a in v[1]]
         ww = [a for v in w for a in v[1]]
-        o = {"e": e, "f": f, "r": rr, "w": ww, "R": {}, "W": {}, "dma": dma}
+        o = {"e": e, "f": f, "r": rr, "w": ww, "R": {}, "W": {}, "dma": dma, "occ": occ, "lat": occ if lat is None else lat, "after": list(after)}
         for (k, m) in rr:
             o["R"][k] = o["R"].get(k, 0) | m
         for (k, m) in ww:
             o["W"][k] = o["W"].get(k, 0) | m
         if sem:
             o["sem"] = sem
+        o["role"], o["nb"] = part[0] + part[1] + "." + str(part[2]), nb
+        part[2] += 1
         ops.append(o)
+        return len(ops) - 1
 
     def isv(a):
         return isinstance(a, tuple)
@@ -143,67 +215,77 @@ def rank_program(g, core, T, topo):
     def ap(a):
         return a[0] if isv(a) else a
 
+    def cost(a, k=1.0):
+        return 0.06 + a[2] * CFG["gat"] * 1e-3 if len(a) > 3 else max(64, k * a[2]) * CY
+
+    def narrow(*vs):
+        return 0.5 if all(SCRATCH[v[1][0][0]][2] in (BF, U16) for v in vs) else 1.0
+
     def ts(out, in0, s1, s2, o0, o1=None):
         r = [in0] + [a for a in (s1, s2) if isv(a)]
+        c = cost(in0, narrow(out, in0))
         if o1 is None:
-            op("v", lambda: vec.tensor_scalar(out[0], in0[0], ap(s1), None, o0), r, [out])
+            op("v", lambda: vec.tensor_scalar(out[0], in0[0], ap(s1), None, o0), r, [out], c)
         else:
-            op("v", lambda: vec.tensor_scalar(out[0], in0[0], ap(s1), ap(s2), o0, o1), r, [out])
+            op("v", lambda: vec.tensor_scalar(out[0], in0[0], ap(s1), ap(s2), o0, o1), r, [out], c)
 
     def tt(out, a, b, o):
-        op("v", lambda: vec.tensor_tensor(out[0], a[0], b[0], o), [a, b], [out])
+        k = 1.0 if is_bank(a[1][0][0]) or is_bank(b[1][0][0]) else 2.0
+        op("v", lambda: vec.tensor_tensor(out[0], a[0], b[0], o), [a, b], [out], cost(a, k))
 
     def cp(out, a):
-        op("v", lambda: vec.tensor_copy(out[0], a[0]), [a], [out])
+        op("v", lambda: vec.tensor_copy(out[0], a[0]), [a], [out], cost(a, narrow(out, a)))
 
     def ms(out, c):
-        op("v", lambda: vec.memset(out[0], c), [], [out])
+        op("v", lambda: vec.memset(out[0], c), [], [out], cost(out, narrow(out)))
 
     def rcp(out, a):
-        op("v", lambda: vec.reciprocal(out[0], a[0]), [a], [out])
-
-    def total(out, a):
-        op("v", lambda: vec.tensor_reduce(out[0], a[0], AX.X, ALU.add), [a], [out])
+        op("v", lambda: vec.reciprocal(out[0], a[0]), [a], [out], 0.19 + 6 * CY * a[2])
 
     def scan(out, d0, d1, init, o0, o1):
         op("v", lambda: vec.tensor_tensor_scan(out[0], d0[0], d1[0], ap(init), o0, o1),
-           [d0, d1] + ([init] if isv(init) else []), [out])
+           [d0, d1] + ([init] if isv(init) else []), [out], cost(out))
 
     def quant(q, s, a, b, src, d=0):
         vq, vs = V(q, a, b), V(s, a + d, b + d)
-        op("v", lambda: vec.quantize_mx(vq[0], vs[0], src[0]), [src], [vq, vs])
+        op("v", lambda: vec.quantize_mx(vq[0], vs[0], src[0]), [src], [vq, vs], (14.5 + 0.265 * src[2]) * CY)
 
     def A(out, a, func, bias=0.0, scale=1.0, acc=None):
         r = [a] + [c for c in (bias, scale) if isv(c)]
         if acc is None:
-            op("s", lambda: act.activation(out[0], a[0], func, bias=ap(bias), scale=ap(scale)), r, [out])
+            op("s", lambda: act.activation(out[0], a[0], func, bias=ap(bias), scale=ap(scale)), r, [out], cost(a))
         else:
-            op("s", lambda: act.activation(out[0], a[0], func, bias=ap(bias), scale=ap(scale), accum_out=acc[0]), r, [out, acc])
+            op("s", lambda: act.activation(out[0], a[0], func, bias=ap(bias), scale=ap(scale), accum_out=acc[0]), r, [out, acc], cost(a) + 0.02)
 
-    def mm(bank, lq, ls, l0, rq, rs, a, b, d=0):
+    def mm(bank, lq, ls, l0, rq, rs, a, b, d=0, start=True, stop=True):
         out = V("p%d" % bank, 0, b - a)
         w, ws_, x, xs = V(lq, l0, l0 + 128), V(ls, l0, l0 + 128), V(rq, a, b), V(rs, a + d, b + d)
-        op("t", lambda: pe.matmul_mx(out[0], w[0], ws_[0], x[0], xs[0], True, True), [w, ws_, x, xs], [out])
+        op("t", lambda: pe.matmul_mx(out[0], w[0], ws_[0], x[0], xs[0], start, stop), [w, ws_, x, xs], [out], 0.05 + (b - a + 16) * CFG["pe"] * 1e-3)
+        ops[-1]["adds"] = not start
 
-    def iota(out, pat, base, cm, flt=True):
+    def iota(out, pat, base, cm, flt=True, after=()):
+        c = 0.16 + 2 * CY * out[2]
         if flt:
-            op("g", lambda: g.iota(out[0], pat, base, cm, allow_small_or_imprecise_dtypes=True), [], [out])
+            op("g", lambda: g.iota(out[0], pat, base, cm, allow_small_or_imprecise_dtypes=True), [], [out], c, after=after)
         else:
-            op("g", lambda: g.iota(out[0], pat, base, cm), [], [out])
+            op("g", lambda: g.iota(out[0], pat, base, cm), [], [out], c)
 
     def sel(out, a, pat, cmp_, fill, base, cm):
-        op("g", lambda: g.affine_select(out[0], a[0], pat, cmp_, fill, base, cm), [a], [out])
+        op("g", lambda: g.affine_select(out[0], a[0], pat, cmp_, fill, base, cm), [a], [out], 0.21 + 2 * CY * out[2])
 
-    def dma(e, out, a, r, w):
+    last_dma = {}
+
+    def dma(e, out, a, r, w, nbytes):
         q = syn if e == "y" else act
-        op(e, lambda: q.dma_start(out, a), r, w, dma=True)
+        after = [(last_dma[e], 0.05)] if e in last_dma else []
+        last_dma[e] = op(e, lambda: q.dma_start(out, a), r, w, 0.05, 1.5 + nbytes / 2.5e5, dma=True, after=after, nb=nbytes)
 
     outs = []
 
-    def store(e, out, a, r):
+    def store(e, out, a, r, nbytes):
         tag = (None, [("out%d" % len(outs), 1)])
         outs.append(tag)
-        dma(e, out, a, r, [tag])
+        dma(e, out, a, r, [tag], nbytes)
 
     def move(e, out, a, scale):
         if e == "s":
@@ -213,22 +295,37 @@ def rank_program(g, core, T, topo):
         else:
             ts(out, a, scale, None, ALU.mult)
 
-    dma("y", T.ut[:], T.u[:], [], [V("ut", 0, 512)])
+    idle = list(range(8))
+
+    def take():
+        return idle.pop(0)
+
+    def give(*banks):
+        idle.extend(banks)
+
+    def pieces(edges):
+        return list(zip(edges[:-1], edges[1:]))
+
+    XC = pieces(CFG["xc"])
+    dma("y", T.ut[:], T.u[:], [], [V("ut", 0, 512)], 1 << 17)
     for c, (a, b) in enumerate(XC):
         v = V("t0", 4 * a, 4 * b)
-        dma("s" if c % 2 == 0 else "y", v[0], T.x[:, 4 * a:4 * b], [], [v])
-    somex = V("t0", 4 * XC[0][0], 4 * XC[0][1])
-    dma("y", T.wq[:].bitcast(dt.uint8), T.wc[:], [somex], [V("wq", 0, 512)])
-    dma("y", T.wsc[:], T.ws[:], [somex], [V("wsc", 0, 512)])
+        dma(CFG["xq"][c], v[0], T.x[:, 4 * a:4 * b], [], [v], 1024 * (b - a))
+    somex = V("t0", 4 * XC[-2][0], 4 * XC[-2][1])
+    dma("y", T.wq[:].bitcast(dt.uint8), T.wc[:], [somex], [V("wq", 0, 512)], 1 << 18)
+    dma("y", T.wsc[:], T.ws[:], [somex], [V("wsc", 0, 512)], 1 << 18)
 
     rcol, qcol, tcol, pcol = V("rf", 0, 1), V("rf", 1, 2), V("rf", 2, 3), V("rf", 3, 4)
-    cthr, ca4, ct52 = V("col", 0, 1), V("col", 1, 2), V("col", 2, 3)
+    cthr, ca4, cov = V("col", 0, 1), V("col", 1, 2), V("col", 2, 3)
     tiny = V("tiny", 0, 1)
     iota(V("pi", 0, 1), [[0, 1]], 0, 1, False)
     iota(V("nq", 0, 128), [[0, 8], [0, 4], [1, 4]], 0, 0)
     sel(V("nq", 0, 128), V("nq", 0, 128), [[-16, 8], [0, 16]], ALU.is_ge, 99.0, 0, 1)
     sel(V("nq", 0, 128), V("nq", 0, 128), [[16, 8], [0, 16]], ALU.is_ge, 99.0, 15, -1)
     iota(V("iw", 0, 128), [[1, 128]], 0, 0)
+    iota(V("nqq", 0, 128), [[0, 8], [1, 4], [0, 4]], 0, 0)
+    sel(V("nqq", 0, 128), V("nqq", 0, 128), [[-16, 8], [0, 16]], ALU.is_ge, 99.0, 0, 1)
+    sel(V("nqq", 0, 128), V("nqq", 0, 128), [[16, 8], [0, 16]], ALU.is_ge, 99.0, 15, -1)
     iota(V("jq", 0, 128), [[0, 32], [1, 4]], 0, 0)
     ms(tiny, -2.0 ** -120)
     ms(V("eb", 0, 528), 0.0)
@@ -242,14 +339,18 @@ def rank_program(g, core, T, topo):
     cp(pcol, V("pi", 0, 1))
     A(cthr, tcol, ACT.Identity, bias=36.0 + 0.5 / M, scale=-9.0)
     A(ca4, tcol, ACT.Identity, bias=2.0 - 144.0 * M, scale=36.0 * M)
-    A(ct52, tcol, ACT.Identity, bias=-52.0)
+    A(cov, tcol, ACT.Identity, bias=1020.0)
     for s in (3, 2, 1, 0):
         ts(V("gt", 512 + s, 1024, 4), V("nq", 0, 128), float(s), 0.5, ALU.is_le, ALU.mult)
     for s in range(2):
         A(V("gt", s, 512, 4), V("gt", 515, 1024, 4), ACT.Copy)
         ts(V("gt", 2 + s, 512, 4), V("nq", 0, 128), 3.0, 0.5, ALU.is_le, ALU.mult)
     for s in range(4):
-        sel(V("gt", 1024 + s, 1536, 4), V("gt", 515, 1024, 4), [[0, 8], [-1, 4], [0, 4]], ALU.is_equal, 0.0, s, 0)
+        ts(V("gt", 1024 + s, 1536, 4), V("nqq", 0, 128), float(s), 0.5, ALU.is_equal, ALU.mult)
+    ms(V("gt", 1536, 2048), 0.0)
+    ms(V("bt", 0, 512), 0.0)
+    ts(V("gt", 1536, 2048, 4), V("nqq", 0, 128), tcol, 4.0, ALU.is_equal, ALU.mult)
+    ts(V("mq", 0, 4), V("jq", 0, 4), qcol, None, ALU.is_equal)
     ts(V("eb", 3, 515, 4), V("iw", 0, 128), pcol, 0.5, ALU.is_equal, ALU.mult)
     quant("gq", "gsc", 0, 256, V("gt", 0, 1024))
     ts(V("k6", 0, 6), V("iw", 0, 96, 16), rcol, 1.0e-4, ALU.add, ALU.max)
@@ -257,21 +358,30 @@ def rank_program(g, core, T, topo):
         quant("eq", "esc", 128 * e, 128 * e + 128, V("eb", 3 - e, 515 - e))
     quant("uq", "usc", 0, 128, V("ut", 0, 512))
     A(V("k96", 0, 96), V("iw", 0, 96), ACT.Copy, scale=1.0 / M)
+    rcp(V("r6", 0, 6), V("k6", 0, 6))
+    ts(V("m2", 0, 128), V("jq", 0, 128), qcol, 1.0e6, ALU.is_equal, ALU.mult)
+    quant("gq", "gsc", 256, 512, V("gt", 1024, 2048))
+    NV = CFG["nv"]
+    AC = 32 * NV - NV
+    if NV:
+        A(V("w6", 0, NV), V("r6", 0, NV), ACT.Copy, scale=M * (1.0 - 5.0e-7))
+    A(V("w6", NV, 6), V("r6", NV, 6), ACT.Copy, scale=-M * (1.0 - 5.0e-7))
 
     def q_state(b, a0, a1):
         quant("aq", "asc", TC * b + a0, TC * b + a1, V("t%d" % b, 4 * a0, 4 * a1), 128 * (b + 1))
 
-    def z_mm(b, a0, a1, bank):
-        mm(bank, "uq", "usc", 0, "aq", "asc", TC * b + a0, TC * b + a1, 128 * (b + 1))
+    def a_mm(b, bank, lq, ls, l0, a0, a1):
+        mm(bank, lq, ls, l0, "aq", "asc", TC * b + a0, TC * b + a1, 128 * (b + 1))
 
-    def z_sign(a0, a1, bank, fin=False):
-        A(V("sgf", 4 * a0, 4 * a1, 4) if fin else V("sg", a0, a1), V("p%d" % bank, 0, a1 - a0), ACT.Sign, bias=tiny)
-
-    def da_mm(b, e, bank, a0, a1):
-        mm(bank, "eq", "esc", 128 * e, "aq", "asc", TC * b + a0, TC * b + a1, 128 * (b + 1))
-
-    def da_cp(eng, e):
-        move(eng, V("da", DA * e, DA * (e + 1)), V("p%d" % DB[e], 0, DA), 1.0)
+    def signs(b, a0, a1, c):
+        lab("z%d" % c)
+        bank = take()
+        a_mm(b, bank, "uq", "usc", 0, a0, a1)
+        z = V("p%d" % bank, 0, a1 - a0)
+        A(V("sgf", 4 * a0, 4 * a1, 4) if b == R else V("sg", a0, a1), z, ACT.Sign, bias=tiny)
+        if b == R:
+            move(CFG["y"][c], V("ys", a0, a1), z, 1.0)
+        give(bank)
 
     def way(b):
         peer = T.cores[rank ^ (1 << (b % 2))]
@@ -282,39 +392,58 @@ def rank_program(g, core, T, topo):
         rid, pid, eng = way(0)
         mask = sum(1 << e for e in eng)
         sq_, ss_, lq, ls = V("aq", 0, 1), V("asc", 128, 129), V("cq", CW, CW + 1), V("csc", CW, CW + 1)
-        op("g", lambda: g.remote_dma(lq[0].bitcast(dt.uint8), sq_[0].bitcast(dt.uint8), T.sem.arr0, T.sem.left, pid, rid, mask), [sq_], [])
-        op("g", lambda: g.remote_dma(ls[0], ss_[0], T.sem.arr0, T.sem.left, pid, rid, mask), [ss_], [])
+        first.append(op("g", lambda: g.remote_dma(lq[0].bitcast(dt.uint8), sq_[0].bitcast(dt.uint8), T.sem.arr0, T.sem.left, pid, rid, mask), [sq_], [], 1.3))
+        first.append(op("g", lambda: g.remote_dma(ls[0], ss_[0], T.sem.arr0, T.sem.left, pid, rid, mask), [ss_], [], 0.3))
         sent[0] += 2 * len(eng)
+
+    def plan(b):
+        fin = b == R - 1 and CFG["fch"]
+        return pieces(CFG["fch" if fin else "ch"]), CFG["fh" if fin else "h"], CFG["fr" if fin else "r"]
+
+    def span(b, e, who):
+        CH, H, _ = plan(b)
+        mine = [CH[c] for c in range(len(CH)) if H[c][e] == who]
+        return (mine[0][0], mine[-1][1]) if mine else None
 
     def exchange(b):
         S = V("cw", 127, 128)
         quant("sq", "ssc", 128 * b, 128 * b + 128, V("sg", 0, 512))
-        mm(2, "gq", "gsc", 0, "sq", "ssc", 128 * b, 128 * b + 128)
-        mm(3, "gq", "gsc", 128, "sq", "ssc", 128 * b, 128 * b + 128)
-        if b == 0:
-            A(V("w6", 0, 4), V("r6", 0, 4), ACT.Copy, scale=-M * (1.0 - 5.0e-7))
-            A(V("w6", 4, 6), V("r6", 4, 6), ACT.Copy, scale=M * (1.0 - 5.0e-7))
-        scan(V("cw", 0, 128), V("p2", 0, 128), V("c36", 0, 128), 0.0, ALU.add, ALU.add)
-        for m in range(4):
-            A(V("junk", 32 * m, 32 * m + 32), V("cw", 3, 128, 4), ACT.Sign, bias=S, scale=V("w6", m, m + 1), acc=V("acc", m, m + 1))
-        for m in range(4, 6):
-            ts(V("junk", 32 * m, 32 * m + 32), V("cw", 3, 128, 4), V("w6", m, m + 1), S, ALU.mult, ALU.is_lt)
-        tt(V("ew", 0, 128), V("cw", 0, 128), V("p3", 0, 128), ALU.subtract)
-        for m in range(4, 6):
-            total(V("acc", m, m + 1), V("junk", 32 * m, 32 * m + 32))
-        ts(V("th96", 0, 96), V("k96", 0, 96), S, cthr, ALU.mult, ALU.add)
+        b2, b3 = take(), take()
+        mm(b2, "gq", "gsc", 0, "sq", "ssc", 128 * b, 128 * b + 128)
+        mm(b3, "gq", "gsc", 128, "sq", "ssc", 128 * b, 128 * b + 128)
+        scan(V("cw", 0, 128), V("p%d" % b2, 0, 128), V("c36", 0, 128), 0.0, ALU.add, ALU.add)
+        for m in range(NV):
+            lab("c%d" % m)
+            j = V("junk", 32 * m, 32 * m + 32)
+            ts(j, V("cw", 3, 128, 4), V("w6", m, m + 1), S, ALU.mult, ALU.is_lt)
+            scan(V("acc", m, AC + m + 1, NV), j, j, -32.0, ALU.add, ALU.add)
+        for m in range(NV, 6):
+            lab("c%d" % m)
+            A(V("junk", 32 * m, 32 * m + 32), V("cw", 3, 128, 4), ACT.Sign, bias=S, scale=V("w6", m, m + 1), acc=V("acc", AC + m, AC + m + 1))
+        lab("F")
+        tt(V("ew", 0, 128), V("cw", 0, 128), V("p%d" % b3, 0, 128), ALU.subtract)
+        give(b2, b3)
+        if CFG["th"] == "v":
+            ts(V("th96", 0, 96), V("k96", 0, 96), S, cthr, ALU.mult, ALU.add)
+        else:
+            A(V("th96", 0, 96), V("k96", 0, 96), ACT.Identity, bias=cthr, scale=S)
         scan(V("ed", 0, 128), V("m2", 0, 128), V("ew", 0, 128), 0.0, ALU.max, ALU.min)
-        ts(V("o2", 4, 6), V("acc", 4, 6), 4.0, 3.0, ALU.mult, ALU.add)
-        ts(V("o2", 0, 4), V("acc", 0, 4), 2.0, 67.0, ALU.mult, ALU.add)
+        ts(V("o2", 0, 6), V("acc", AC, AC + 6), 2.0, 67.0, ALU.mult, ALU.add)
         tt(V("cmp", 0, 96), IND(V("ed", 0, 128), V("o2", 0, 6)), V("th96", 0, 96), ALU.is_le)
-        A(V("brep", 0, 96), IND(V("iw", 0, 128), V("o2", 0, 6)), ACT.Copy, scale=2.0)
-        da_cp("s", 2)
+        for j in range(4):
+            bo, bi = V("bt", 4 * j, 96, 16), V("acc", AC, AC + 6)
+            if CFG["bt"][j] == "s":
+                A(bo, bi, ACT.Copy, scale=V("mq", j, j + 1))
+            else:
+                ts(bo, bi, V("mq", j, j + 1), None, ALU.mult)
+        quant("bq", "bsc", 128 * b, 128 * b + 128, V("bt", 0, 512))
         dc = (CS - CQ) * b
         quant("cq", "csc", CQ * b, CQ * b + CW, V("cmp", 0, 4 * CW), dc)
-        mm(0, "gq", "gsc", 256, "cq", "csc", CQ * b, CQ * b + 128, dc)
-        scan(V("bsel", 0, 96), V("m2", 0, 96), V("brep", 0, 96), 0.0, ALU.max, ALU.min)
-        tt(V("s24", 0, 24), V("p0", 0, 24), V("bsel", 3, 96, 4), ALU.add)
-        ts(V("ov", 0, 24), V("s24", 0, 24), 8.0, ct52, ALU.mult, ALU.add)
+        b0 = take()
+        mm(b0, "gq", "gsc", 384, "bq", "bsc", 128 * b, 128 * b + 128, 0, True, False)
+        mm(b0, "gq", "gsc", 256, "cq", "csc", CQ * b, CQ * b + 128, dc, False, True)
+        ts(V("ov", 0, 24), V("p%d" % b0, 0, 24), 8.0, cov, ALU.mult, ALU.add)
+        give(b0)
         st = V("t%d" % b, 0, 2048)
         cp(V("vt", 0, 192), IND(st, V("ov", 0, 12)))
         A(V("vt", 192, 384), IND(st, V("ov", 12, 24)), ACT.Copy)
@@ -329,120 +458,126 @@ def rank_program(g, core, T, topo):
         pair = [RemoteDMATransfer(dst_ids=to, dma_engine_mask=sum(1 << e for e in eng[:h]), remote_sem=arr,
                                   src=sq_[0].bitcast(dt.uint8), dst=lq[0].bitcast(dt.uint8)),
                 RemoteDMATransfer(dst_ids=to, dma_engine_mask=sum(1 << e for e in eng[h:]), remote_sem=arr, src=ss_[0], dst=ls[0])]
-        op("g", lambda: g.remote_dma_fused(pair, local_sem=T.sem.left), [sq_, ss_], [])
+        gone = op("g", lambda: g.remote_dma_fused(pair, local_sem=T.sem.left), [sq_, ss_], [], 0.3, after=[(j, 0.3) for j in first])
         sent[b] += len(eng)
         if b == 0:
-            iota(V("c9", 0, 512), [[0, 512]], 9, 0)
-            iota(V("sgf", 0, 2048), [[0, 2048]], 0, 0)
-        da_cp("s", 3)
-        if b == 0:
-            da_cp("v", 0)
-            da_cp("s", 1)
+            iota(V("c9", 0, 512), [[0, 512]], 9, 0, after=[(gone, 0.3)])
+            iota(V("sgf", 0, 2048), [[0, 2048]], 0, 0, after=[(gone, 0.3)])
+        for e in range(4):
+            lab("da%d" % e)
+            sp = span(b, e, "v")
+            if sp:
+                bank = take()
+                a_mm(b, bank, "eq", "esc", 128 * e, sp[0], sp[1])
+                move(CFG["da"][e], V("da", TC * e + sp[0], TC * e + sp[1]), V("p%d" % bank, 0, sp[1] - sp[0]), 1.0)
+                give(bank)
+        held = {}
+        for e in range(4):
+            lab("hd%d" % e)
+            sp = span(b, e, "s")
+            if sp:
+                held[e] = (take(), sp[0], sp[1])
+                a_mm(b, held[e][0], "eq", "esc", 128 * e, sp[0], sp[1])
+        lab("P")
         big = 1.5 * 2.0 ** 25
         rcp(V("sm", 0, 1), S)
         ts(V("sm", 1, 2), S, -2.0, ca4, ALU.mult, ALU.add)
         ts(V("x4", 0, 32), V("ed", 3, 128, 4), 4.0 * M, V("sm", 1, 2), ALU.mult, ALU.add)
         ts(V("y4", 0, 32), V("x4", 0, 32), V("sm", 0, 1), big, ALU.mult, ALU.add)
         ts(V("op", 0, 32), V("y4", 0, 32), big, 0.25, ALU.subtract, ALU.mult)
-        op("x", None, [], [V("cq", CQ * b + CW, CQ * (b + 1)), V("csc", CS * b + CW, CS * (b + 1))], sem=("arr%d" % b, sent[b]))
-        for e in range(4):
-            mm(e, "eq", "esc", 128 * e, "cq", "csc", CQ * (b + 1) - 128, CQ * (b + 1), dc)
-        for e in range(4):
-            move("v" if e == 0 else "s", V("dv", M * e, M * (e + 1)), V("p%d" % e, 128 - M, 128), 1.0)
-            da_mm(b, e, e, DA, TC)
+        op("x", None, [], [V("cq", CQ * b + CW, CQ * (b + 1)), V("csc", CS * b + CW, CS * (b + 1))], 0.0, sem=("arr%d" % b, sent[b]),
+           after=[(gone, CFG["far"])])
+        for e in CFG["dvo"]:
+            lab("dv%d" % e)
+            bank = take()
+            mm(bank, "eq", "esc", 128 * e, "cq", "csc", CQ * (b + 1) - 128, CQ * (b + 1), dc)
+            move(CFG["dv"][e], V("dv", M * e, M * (e + 1)), V("p%d" % bank, 128 - M, 128), 1.0)
+            give(bank)
+        return held
 
-    def h_make(b, c):
+    def next_state(b, c, held):
+        CH, H, RC = plan(b)
         a0, a1 = CH[c]
+        off = V("op", a0 // 16, a1 // 16)
         for e in range(4):
+            lab("h%d%d" % (c, e))
             out, win = V("ht", 4 * a0 + e, 4 * a1, 4), V("dv", M * e, M * (e + 1))
-            dg = V("dg", TC * e + DA, TC * (e + 1))
-            if c == 0:
-                tt(out, IND(win, V("op", 0, DA // 16)), V("da", DA * e, DA * (e + 1)), ALU.add)
-                A(dg, IND(win, V("op", DA // 16, TC // 16)), ACT.Copy)
+            if H[c][e] == "v":
+                tt(out, IND(win, off), V("da", TC * e + a0, TC * e + a1), ALU.add)
             else:
-                tt(out, V("p%d" % e, 0, a1 - a0), dg, ALU.add)
+                bank, s0, s1 = held[e]
+                dg = V("dg", TC * e + a0, TC * e + a1)
+                A(dg, IND(win, off), ACT.Copy)
+                tt(out, V("p%d" % bank, a0 - s0, a1 - s0), dg, ALU.add)
+                if a1 == s1:
+                    give(bank)
+        lab("qh%d" % c)
         quant("hq", "hsc", TC * b + a0, TC * b + a1, V("ht", 4 * a0, 4 * a1))
         for i in range(4):
-            mm(4 * (1 - c) + i, "wq", "wsc", 128 * i, "hq", "hsc", TC * b + a0, TC * b + a1)
-
-    def r_cp(b, c, i, eng):
-        a0, a1 = CH[c]
-        move(eng, V("t%d" % (b + 1), 4 * a0 + i, 4 * a1, 4), V("p%d" % (4 * (1 - c) + i), 0, a1 - a0), 0.03125)
-
-    def y_cp(eng, a0, a1, bank):
-        move(eng, V("ys", a0, a1), V("p%d" % bank, 0, a1 - a0), 1.0)
+            lab("w%d%d" % (c, i))
+            bank = take()
+            mm(bank, "wq", "wsc", 128 * i, "hq", "hsc", TC * b + a0, TC * b + a1)
+            move(RC[c][i], V("t%d" % (b + 1), 4 * a0 + i, 4 * a1, 4), V("p%d" % bank, 0, a1 - a0), 0.03125)
+            give(bank)
+        lab("qa%d" % c)
+        q_state(b + 1, a0, a1)
 
     def st_codes(a0, a1):
         v = V("aq", TC * R + a0, TC * R + a1)
-        store("y", T.oc[:, 4 * a0:4 * a1], v[0].bitcast(dt.uint8), [v])
+        store("y", T.oc[:, 4 * a0:4 * a1], v[0].bitcast(dt.uint8), [v], 512 * (a1 - a0))
 
     def st_scales(e, k):
         o = AS * R + 128
-        store(e, T.osc[4 * k:4 * k + 4, :], T.asc[32 * k:32 * k + 4, o:o + TC], [V("asc", o, o + TC)])
+        store(e, T.osc[4 * k:4 * k + 4, :], T.asc[32 * k:32 * k + 4, o:o + TC], [V("asc", o, o + TC)], 2048)
 
     def st_y(e, a0, a1):
         v = V("ys", a0, a1)
-        store(e, T.y[:, a0:a1], v[0], [v])
+        store(e, T.y[:, a0:a1], v[0], [v], 512 * (a1 - a0))
 
-    def last_clocks(a0, a1, bank):
+    def last_clocks(a0, a1):
+        lab("l%d" % a0)
         o = 128 * R
         quant("sq", "ssc", o + a0, o + a1, V("sgf", 4 * a0, 4 * a1))
+        bank = take()
         mm(bank, "gq", "gsc", 0, "sq", "ssc", o + a0, o + a1)
         scan(V("cs", a0, a1), V("p%d" % bank, 0, a1 - a0), V("c9", a0, a1), V("cs", a0 - 1, a0) if a0 else 0.0, ALU.add, ALU.add)
+        give(bank)
 
-    sent = [0] * R
+    sent, first = [0] * R, []
     for c, (a0, a1) in enumerate(XC):
         q_state(0, a0, a1)
         if c == 0:
             send_first()
-        z_mm(0, a0, a1, 4 * (1 - c))
-        z_sign(a0, a1, 4 * (1 - c))
-    rcp(V("r6", 0, 6), V("k6", 0, 6))
-    for e in range(4):
-        da_mm(0, e, DB[e], 0, DA)
-    ts(V("m2", 0, 128), V("jq", 0, 128), qcol, 1.0e6, ALU.is_equal, ALU.mult)
-    quant("gq", "gsc", 256, 384, V("gt", 1024, 1536))
-    e1 = DA
+        signs(0, a0, a1, c)
     for b in range(R):
-        exchange(b)
-        fin = b == R - 1
-        h_make(b, 0)
-        for i in range(3):
-            r_cp(b, 0, i, "s")
-        h_make(b, 1)
-        r_cp(b, 0, 3, "v")
-        q_state(b + 1, 0, e1)
-        z_mm(b + 1, 0, e1, 4)
-        if fin:
-            st_codes(0, e1)
-        for i in range(4):
-            r_cp(b, 1, i, "s" if i % 2 == 0 else "v")
-        z_sign(0, e1, 4, fin)
-        if not fin:
-            da_mm(b + 1, 0, DB[0], 0, DA)
-            da_mm(b + 1, 1, DB[1], 0, DA)
-        q_state(b + 1, e1, TC)
-        z_mm(b + 1, e1, TC, 0)
-        if fin:
-            y_cp("s", 0, e1, 4)
-            last_clocks(0, e1, 5)
+        part[:] = ["x", "", 0]
+        held = exchange(b)
+        part[0] = "f" if b == R - 1 else "n"
+        CH = plan(b)[0]
+        n, lag = len(CH), CFG["zl"]
+        for c in range(n + lag):
+            if c < n:
+                next_state(b, c, held)
+            if c >= lag:
+                signs(b + 1, CH[c - lag][0], CH[c - lag][1], c - lag)
+                if b == R - 1:
+                    last_clocks(CH[c - lag][0], CH[c - lag][1])
+    part[:] = ["o", "", 0]
+    edge = [a for (a, _) in CH] + [TC]
+    todo = []
+    for kind, ends in (("oc", CFG["soc"]), ("y", CFG["sy"])):
+        for (c0, c1) in pieces([0] + ends):
+            todo.append((c1 + (0.6 if kind == "y" else 0.0), kind, edge[c0], edge[c1]))
+    todo.append((len(CH) + 0.3, "osc", 0, 0))
+    for (_, kind, a0, a1) in sorted(todo):
+        if kind == "oc":
+            st_codes(a0, a1)
+        elif kind == "y":
+            st_y("y", a0, a1)
         else:
-            da_mm(b + 1, 2, DB[2], 0, DA)
-            da_mm(b + 1, 3, DB[3], 0, DA)
-        z_sign(e1, TC, 0, fin)
-        if not fin:
-            da_cp("v", 0)
-            da_cp("s", 1)
-    st_codes(e1, TC)
-    st_y("y", 0, e1)
-    y_cp("s", e1, TC, 0)
-    st_scales("y", 0)
-    st_y("y", e1, TC)
-    st_scales("y", 1)
-    st_scales("y", 2)
-    st_scales("s", 3)
-    last_clocks(e1, TC, 6)
-    store("s", T.cl[:], T.cs[0:128:16, :], [V("cs", 0, 512)])
-    op("y", None, outs, [])
-    emit(ops, {"g": g, "v": vec, "s": act, "t": pe, "y": syn}, T)
+            for k in range(4):
+                st_scales(CFG["oq"][k], k)
+    store("s", T.cl[:], T.cs[0:128:16, :], [V("cs", 0, 512)], 16384)
+    op("y", None, outs, [], 0.01)
+    emit(arrange(ops), {"g": g, "v": vec, "s": act, "t": pe, "y": syn}, T)
     g.wait_ge(T.sem.left, sum(sent))

@@ -1,4 +1,3 @@
-from concourse.bass import DstId, RemoteDMATransfer
 from concourse.mybir import dt, AluOpType as ALU, ActivationFunctionType as ACT
 
 TC, M, R = 512, 96, 3
@@ -6,17 +5,15 @@ CFG = {
     "ch": [0, 192, 384, 512],
     "h": ["vvss", "vvss", "vvss"],
     "r": ["ssss", "ssss", "svvs"],
-    "fch": [0, 256, 384, 512], "fh": ["vvss", "vvss", "vvss"], "fr": ["ssss", "ssss", "svvs"],
-    "dv": "vsss", "dvo": [0, 2, 1, 3],
+    "dv": "ssss", "dvo": [0, 2, 1, 3],
     "da": "vsvv",
-    "xc": [0, 352, 512], "xq": "sy",
-    "nv": 1, "th": "s", "bt": "ssss",
-    "y": "sss", "soc": [1, 2, 3], "sy": [1, 3], "oq": "yyys",
-    "zl": 1,
-    "wake": 0.1, "gat": 1.5, "pe": 0.8, "far": 2.0, "cy": 0.95e-3,
-    "bias": {"nh10.0": 0.8, "nw20.0": -0.1, "sz0.2": -1.6, "xdv0.0": 0.7, "xdv3.1": -1.0, "fh11.0": 0.8, "fw10.0": -0.8,
-             "nh20.0": 0.4, "nh12.0": -0.6, "fl384.0": -0.7, "xdv2.1": -0.8, "fh22.1": 0.4, "fz0.1": -0.8, "fh21.0": -0.2},
+    "y": "vsv",
+    "xc": [0, 320, 512], "xq": "sy",
+    "nv": 2,
+    "oq": "yyss",
 }
+ORDER = [0, 1, 2, 3, 4, 5, 6, 7, 8, 37, 11, 13, 10, 14, 15, 12, 9, 16, 17, 19, 48, 43, 25, 24, 50, 58, 36, 20, 18, 39, 26, 38, 28, 49, 31, 61, 59, 60, 29, 30, 62, 63, 32, 27, 34, 33, 35, 42, 64, 65, 40, 54, 23, 57, 21, 51, 22, 56, 53, 52, 66, 55, 67, 68, 69, 41, 72, 70, 78, 73, 71, 76, 77, 75, 74, 79, 83, 84, 86, 85, 80, 81, 82, 87, 88, 89, 90, 44, 91, 92, 93, 94, 98, 46, 105, 102, 106, 45, 47, 100, 99, 104, 107, 108, 103, 101, 95, 109, 110, 116, 112, 114,
+         111, 117, 113, 122, 115, 120, 136, 156, 138, 154, 134, 118, 123, 119, 121, 137, 124, 135, 139, 157, 140, 155, 152, 153, 125, 127, 129, 131, 126, 128, 130, 132, 158, 143, 141, 145, 147, 144, 142, 146, 148, 133, 163, 159, 165, 161, 164, 149, 162, 150, 160, 166, 151, 167, 168, 170, 169, 171, 172, 173, 174, 175, 176, 178, 184, 177, 179, 180, 182, 183, 181, 185, 191, 192, 189, 190, 186, 187, 209, 188, 193, 194, 195, 196, 197, 199, 198, 210, 200, 208, 211, 212, 204, 207, 202, 203, 206, 205, 97, 96, 201, 213, 214, 220, 216, 215, 218, 221, 217, 226, 219, 224, 238, 222, 227, 223, 225, 240, 242, 260, 258, 241, 228, 239, 243, 229, 231, 233, 235, 261, 244, 256, 259, 257, 247, 245, 230, 249, 234, 232, 236, 248, 246, 251, 250, 252, 262, 237, 267, 263, 265, 269, 264, 270, 268, 253, 266, 254, 255, 271, 272, 274, 273, 275, 276, 277, 278, 279, 280, 282, 288, 281, 283, 284, 286, 285, 287, 289, 295, 296, 293, 294, 290, 291, 313, 292, 297, 298, 306, 310, 299, 300, 308, 311, 301, 303, 302, 314, 304, 305, 312, 317, 315, 316, 307, 309, 318, 324, 320, 322, 319, 325, 321, 330, 323, 328, 342, 326, 331, 327, 329, 344, 366, 346, 368, 345, 332, 339, 333, 340, 334, 343, 347, 335, 337, 336, 338, 367, 348, 369, 365, 364, 341, 351, 349, 353, 355, 352, 350, 354, 356, 370, 358, 360, 371, 373, 375, 377, 357, 359, 372, 374, 376, 361, 378, 380, 381, 382, 362, 379, 386, 387, 392, 393, 394, 383, 363, 384, 389, 388, 396, 398, 395, 397, 401, 385, 390, 391, 400, 399, 402, 403]
 CW = 128
 CQ, CS = CW + M, CW + 4 * M
 AS = 128 + TC
@@ -38,10 +35,11 @@ SCRATCH = {
     "sg": _sb(512, BF), "sgf": _sb(2048, BF), "sq": _sb(R * 128 + TC, F8), "ssc": _sb(R * 128 + TC, U8),
     "cmp": _sb(4 * CW, BF), "cq": _sb(R * CQ, F8), "csc": _sb(R * CS, U8),
     "eb": _sb(528, BF), "eq": _sb(512, F8), "esc": _sb(512, U8),
-    "nq": _sb(128, BF), "nqq": _sb(128, BF), "gt": _sb(2048, BF), "gq": _sb(512, F8), "gsc": _sb(512, U8),
-    "bt": _sb(512, BF), "bq": _sb(R * 128, F8), "bsc": _sb(R * 128, U8), "mq": _sb(4, F32),
-    "pi": _sb(4, I32), "ri": _sb(4, I32), "rf": _sb(4, F32), "col": _sb(8, F32), "tiny": _sb(4, F32),
-    "jq": _sb(128, F32), "iw": _sb(128, F32), "c36": _sb(128, F32), "c9": _sb(512, F32),
+    "nv": _sb(128, BF), "nvq": _sb(128, BF), "nq": _sb(128, BF), "nqq": _sb(128, BF),
+    "gt": _sb(2048, BF), "gq": _sb(512, F8), "gsc": _sb(512, U8),
+    "bt": _sb(512, BF), "bq": _sb(R * 128, F8), "bsc": _sb(R * 128, U8), "mq": _sb(4, F32), "mb": _sb(4, F32),
+    "pi": _sb(4, I32), "rf": _sb(8, F32), "col": _sb(8, F32), "tiny": _sb(4, F32),
+    "iw": _sb(128, F32), "c36": _sb(128, F32), "c9": _sb(512, F32),
     "k6": _sb(8, F32), "r6": _sb(8, F32), "w6": _sb(8, F32), "k96": _sb(96, F32), "m2": _sb(128, F32),
     "cw": _sb(128, F32), "ew": _sb(128, F32), "ed": _sb(128, F32), "th96": _sb(96, F32),
     "junk": _sb(192, F32), "acc": _sb(104, F32),
@@ -54,69 +52,22 @@ for _b in range(8):
 
 NC, ND = 110, 24
 SEMAPHORES = ["arr0", "arr1", "arr2", "left"] + ["c%d" % _i for _i in range(NC)] + ["d%d" % _i for _i in range(ND)]
-ORDERS = {}
 
 
 def is_bank(k):
     return k[0] == "p" and k[1:].isdigit()
 
 
-def meets(o, p, waits=False):
+def meets(o, p):
     for (k, m) in o["r"]:
         if p["W"].get(k, 0) & m or (k in p["R"] and p["e"] != o["e"] and is_bank(k)):
             return True
     for (k, m) in o["w"]:
-        if waits and o.get("adds") and p["e"] == "t":
+        if o.get("adds") and p["e"] == "t":
             continue
         if (p["W"].get(k, 0) | p["R"].get(k, 0)) & m:
             return True
     return False
-
-
-def hazards(ops):
-    users, hz = {}, []
-    for i, o in enumerate(ops):
-        near = set()
-        for k in list(o["R"]) + list(o["W"]):
-            near.update(users.get(k, ()))
-        hz.append([j for j in near if meets(o, ops[j])])
-        for k in list(o["R"]) + list(o["W"]):
-            users.setdefault(k, set()).add(i)
-    return hz
-
-
-def layout(ops, hz, bias):
-    n, wake = len(ops), CFG["wake"]
-    deps = [[(j, ops[j]["lat"] + wake) for j in hz[i]] + ops[i]["after"] for i in range(n)]
-    rest = [o["lat"] for o in ops]
-    for i in range(n - 1, -1, -1):
-        for (j, t) in deps[i]:
-            rest[j] = max(rest[j], rest[i] + t)
-    rank = [rest[i] + bias.get(ops[i]["role"], 0.0) for i in range(n)]
-    for i in range(n):
-        for (j, t) in deps[i]:
-            rank[i] = min(rank[i], rank[j])
-    start, busy = [0.0] * n, {}
-    for i in sorted(range(n), key=lambda i: (-rank[i], i)):
-        t = max([start[j] + d for (j, d) in deps[i]] + [0.0])
-        slots, need = busy.setdefault(ops[i]["e"], []), ops[i]["occ"]
-        k = len(slots)
-        for s, (a, b) in enumerate(slots):
-            if b > t:
-                if a >= t + need:
-                    k = s
-                    break
-                t = b
-        slots.insert(k, (t, t + need))
-        start[i] = t
-    return sorted(range(n), key=lambda i: (start[i], i))
-
-
-def arrange(ops):
-    key = repr(CFG)
-    if key not in ORDERS:
-        ORDERS[key] = layout(ops, hazards(ops), CFG["bias"])
-    return [ops[i] for i in ORDERS[key]]
 
 
 def emit(ops, queues, T):
@@ -131,7 +82,7 @@ def emit(ops, queues, T):
             if known[o["e"]] >> j & 1:
                 continue
             p = ops[j]
-            if meets(o, p, True):
+            if meets(o, p):
                 o["waits"].append(j)
                 p["by"].append(i)
                 known[o["e"]] |= p["done"]
@@ -174,11 +125,6 @@ def rank_program(g, core, T, topo):
         return
     ops = []
     vec, act, pe, syn = g.vector, g.scalar, g.tensor, g.sync
-    CY = CFG["cy"]
-    part = ["s", "", 0]
-
-    def lab(t):
-        part[1:] = [t, 0]
 
     def V(name, a, b, s=1):
         m = 0
@@ -189,25 +135,22 @@ def rank_program(g, core, T, topo):
         else:
             for c in range(a, b, s):
                 m |= 1 << c
-        return (T[name][:, a:b] if s == 1 else T[name][:, a:b:s], [(name, m)], len(range(a, b, s)))
+        return (T[name][:, a:b] if s == 1 else T[name][:, a:b:s], [(name, m)])
 
     def IND(win, off):
-        return (win[0].indirect(off[0]), win[1] + off[1], 16 * off[2], True)
+        return (win[0].indirect(off[0]), win[1] + off[1])
 
-    def op(e, f, r, w, occ, lat=None, dma=False, sem=None, after=(), nb=0):
+    def op(e, f, r, w, dma=False, sem=None):
         rr = [a for v in r for a in v[1]]
         ww = [a for v in w for a in v[1]]
-        o = {"e": e, "f": f, "r": rr, "w": ww, "R": {}, "W": {}, "dma": dma, "occ": occ, "lat": occ if lat is None else lat, "after": list(after)}
+        o = {"e": e, "f": f, "r": rr, "w": ww, "R": {}, "W": {}, "dma": dma}
         for (k, m) in rr:
             o["R"][k] = o["R"].get(k, 0) | m
         for (k, m) in ww:
             o["W"][k] = o["W"].get(k, 0) | m
         if sem:
             o["sem"] = sem
-        o["role"], o["nb"] = part[0] + part[1] + "." + str(part[2]), nb
-        part[2] += 1
         ops.append(o)
-        return len(ops) - 1
 
     def isv(a):
         return isinstance(a, tuple)
@@ -215,77 +158,62 @@ def rank_program(g, core, T, topo):
     def ap(a):
         return a[0] if isv(a) else a
 
-    def cost(a, k=1.0):
-        return 0.06 + a[2] * CFG["gat"] * 1e-3 if len(a) > 3 else max(64, k * a[2]) * CY
-
-    def narrow(*vs):
-        return 0.5 if all(SCRATCH[v[1][0][0]][2] in (BF, U16) for v in vs) else 1.0
-
     def ts(out, in0, s1, s2, o0, o1=None):
         r = [in0] + [a for a in (s1, s2) if isv(a)]
-        c = cost(in0, narrow(out, in0))
         if o1 is None:
-            op("v", lambda: vec.tensor_scalar(out[0], in0[0], ap(s1), None, o0), r, [out], c)
+            op("v", lambda: vec.tensor_scalar(out[0], in0[0], ap(s1), None, o0), r, [out])
         else:
-            op("v", lambda: vec.tensor_scalar(out[0], in0[0], ap(s1), ap(s2), o0, o1), r, [out], c)
+            op("v", lambda: vec.tensor_scalar(out[0], in0[0], ap(s1), ap(s2), o0, o1), r, [out])
 
     def tt(out, a, b, o):
-        k = 1.0 if is_bank(a[1][0][0]) or is_bank(b[1][0][0]) else 2.0
-        op("v", lambda: vec.tensor_tensor(out[0], a[0], b[0], o), [a, b], [out], cost(a, k))
+        op("v", lambda: vec.tensor_tensor(out[0], a[0], b[0], o), [a, b], [out])
 
     def cp(out, a):
-        op("v", lambda: vec.tensor_copy(out[0], a[0]), [a], [out], cost(a, narrow(out, a)))
+        op("v", lambda: vec.tensor_copy(out[0], a[0]), [a], [out])
 
     def ms(out, c):
-        op("v", lambda: vec.memset(out[0], c), [], [out], cost(out, narrow(out)))
+        op("v", lambda: vec.memset(out[0], c), [], [out])
 
     def rcp(out, a):
-        op("v", lambda: vec.reciprocal(out[0], a[0]), [a], [out], 0.19 + 6 * CY * a[2])
+        op("v", lambda: vec.reciprocal(out[0], a[0]), [a], [out])
 
     def scan(out, d0, d1, init, o0, o1):
         op("v", lambda: vec.tensor_tensor_scan(out[0], d0[0], d1[0], ap(init), o0, o1),
-           [d0, d1] + ([init] if isv(init) else []), [out], cost(out))
+           [d0, d1] + ([init] if isv(init) else []), [out])
 
     def quant(q, s, a, b, src, d=0):
         vq, vs = V(q, a, b), V(s, a + d, b + d)
-        op("v", lambda: vec.quantize_mx(vq[0], vs[0], src[0]), [src], [vq, vs], (14.5 + 0.265 * src[2]) * CY)
+        op("v", lambda: vec.quantize_mx(vq[0], vs[0], src[0]), [src], [vq, vs])
 
     def A(out, a, func, bias=0.0, scale=1.0, acc=None):
         r = [a] + [c for c in (bias, scale) if isv(c)]
         if acc is None:
-            op("s", lambda: act.activation(out[0], a[0], func, bias=ap(bias), scale=ap(scale)), r, [out], cost(a))
+            op("s", lambda: act.activation(out[0], a[0], func, bias=ap(bias), scale=ap(scale)), r, [out])
         else:
-            op("s", lambda: act.activation(out[0], a[0], func, bias=ap(bias), scale=ap(scale), accum_out=acc[0]), r, [out, acc], cost(a) + 0.02)
+            op("s", lambda: act.activation(out[0], a[0], func, bias=ap(bias), scale=ap(scale), accum_out=acc[0]), r, [out, acc])
 
     def mm(bank, lq, ls, l0, rq, rs, a, b, d=0, start=True, stop=True):
         out = V("p%d" % bank, 0, b - a)
         w, ws_, x, xs = V(lq, l0, l0 + 128), V(ls, l0, l0 + 128), V(rq, a, b), V(rs, a + d, b + d)
-        op("t", lambda: pe.matmul_mx(out[0], w[0], ws_[0], x[0], xs[0], start, stop), [w, ws_, x, xs], [out], 0.05 + (b - a + 16) * CFG["pe"] * 1e-3)
+        op("t", lambda: pe.matmul_mx(out[0], w[0], ws_[0], x[0], xs[0], start, stop), [w, ws_, x, xs], [out])
         ops[-1]["adds"] = not start
 
-    def iota(out, pat, base, cm, flt=True, after=()):
-        c = 0.16 + 2 * CY * out[2]
+    def iota(out, pat, base, cm, flt=True):
         if flt:
-            op("g", lambda: g.iota(out[0], pat, base, cm, allow_small_or_imprecise_dtypes=True), [], [out], c, after=after)
+            op("g", lambda: g.iota(out[0], pat, base, cm, allow_small_or_imprecise_dtypes=True), [], [out])
         else:
-            op("g", lambda: g.iota(out[0], pat, base, cm), [], [out], c)
+            op("g", lambda: g.iota(out[0], pat, base, cm), [], [out])
 
-    def sel(out, a, pat, cmp_, fill, base, cm):
-        op("g", lambda: g.affine_select(out[0], a[0], pat, cmp_, fill, base, cm), [a], [out], 0.21 + 2 * CY * out[2])
-
-    last_dma = {}
-
-    def dma(e, out, a, r, w, nbytes):
+    def dma(e, out, a, r, w):
         q = syn if e == "y" else act
-        after = [(last_dma[e], 0.05)] if e in last_dma else []
-        last_dma[e] = op(e, lambda: q.dma_start(out, a), r, w, 0.05, 1.5 + nbytes / 2.5e5, dma=True, after=after, nb=nbytes)
+        op(e, lambda: q.dma_start(out, a), r, w, dma=True)
 
     outs = []
 
-    def store(e, out, a, r, nbytes):
+    def store(e, out, a, r):
         tag = (None, [("out%d" % len(outs), 1)])
         outs.append(tag)
-        dma(e, out, a, r, [tag], nbytes)
+        dma(e, out, a, r, [tag])
 
     def move(e, out, a, scale):
         if e == "s":
@@ -306,51 +234,48 @@ def rank_program(g, core, T, topo):
     def pieces(edges):
         return list(zip(edges[:-1], edges[1:]))
 
-    XC = pieces(CFG["xc"])
-    dma("y", T.ut[:], T.u[:], [], [V("ut", 0, 512)], 1 << 17)
+    XC, CH, H, RC = pieces(CFG["xc"]), pieces(CFG["ch"]), CFG["h"], CFG["r"]
+    dma("y", T.ut[:], T.u[:], [], [V("ut", 0, 512)])
     for c, (a, b) in enumerate(XC):
         v = V("t0", 4 * a, 4 * b)
-        dma(CFG["xq"][c], v[0], T.x[:, 4 * a:4 * b], [], [v], 1024 * (b - a))
-    somex = V("t0", 4 * XC[-2][0], 4 * XC[-2][1])
-    dma("y", T.wq[:].bitcast(dt.uint8), T.wc[:], [somex], [V("wq", 0, 512)], 1 << 18)
-    dma("y", T.wsc[:], T.ws[:], [somex], [V("wsc", 0, 512)], 1 << 18)
+        dma(CFG["xq"][c], v[0], T.x[:, 4 * a:4 * b], [], [v])
+    somex = V("t0", 4 * XC[0][0], 4 * XC[0][1])
+    dma("y", T.wq[:].bitcast(dt.uint8), T.wc[:], [somex], [V("wq", 0, 512)])
+    dma("y", T.wsc[:], T.ws[:], [somex], [V("wsc", 0, 512)])
 
-    rcol, qcol, tcol, pcol = V("rf", 0, 1), V("rf", 1, 2), V("rf", 2, 3), V("rf", 3, 4)
+    pcol, gcol, tcol, rcol, q4col = V("rf", 0, 1), V("rf", 1, 2), V("rf", 2, 3), V("rf", 3, 4), V("rf", 5, 6)
     cthr, ca4, cov = V("col", 0, 1), V("col", 1, 2), V("col", 2, 3)
     tiny = V("tiny", 0, 1)
     iota(V("pi", 0, 1), [[0, 1]], 0, 1, False)
-    iota(V("nq", 0, 128), [[0, 8], [0, 4], [1, 4]], 0, 0)
-    sel(V("nq", 0, 128), V("nq", 0, 128), [[-16, 8], [0, 16]], ALU.is_ge, 99.0, 0, 1)
-    sel(V("nq", 0, 128), V("nq", 0, 128), [[16, 8], [0, 16]], ALU.is_ge, 99.0, 15, -1)
+    iota(V("nv", 0, 128), [[16, 8], [0, 4], [1, 4]], 0, 0)
     iota(V("iw", 0, 128), [[1, 128]], 0, 0)
-    iota(V("nqq", 0, 128), [[0, 8], [1, 4], [0, 4]], 0, 0)
-    sel(V("nqq", 0, 128), V("nqq", 0, 128), [[-16, 8], [0, 16]], ALU.is_ge, 99.0, 0, 1)
-    sel(V("nqq", 0, 128), V("nqq", 0, 128), [[16, 8], [0, 16]], ALU.is_ge, 99.0, 15, -1)
-    iota(V("jq", 0, 128), [[0, 32], [1, 4]], 0, 0)
+    iota(V("nvq", 0, 128), [[16, 8], [1, 4], [0, 4]], 0, 0)
     ms(tiny, -2.0 ** -120)
     ms(V("eb", 0, 528), 0.0)
-    ms(V("cmp", 96, 4 * CW), 0.0)
+    iota(V("cmp", 96, 4 * CW), [[0, 4 * CW - 96]], 0, 0)
     ms(V("vt", 384, 512), 0.0)
     ms(V("c36", 0, 128), 36.0)
-    ts(V("ri", 0, 1), V("pi", 0, 1), 15, None, ALU.bitwise_and)
-    ts(V("ri", 1, 2), V("pi", 0, 1), 2, 3, ALU.arith_shift_right, ALU.bitwise_and)
-    ts(V("ri", 2, 3), V("pi", 0, 1), 3, None, ALU.bitwise_and)
-    cp(V("rf", 0, 3), V("ri", 0, 3))
-    cp(pcol, V("pi", 0, 1))
+    ts(V("pi", 1, 2), V("pi", 0, 1), 112, None, ALU.bitwise_and)
+    ts(V("pi", 2, 3), V("pi", 0, 1), 3, None, ALU.bitwise_and)
+    cp(V("rf", 0, 3), V("pi", 0, 3))
+    A(rcol, gcol, ACT.Identity, bias=pcol, scale=-1.0)
+    A(q4col, tcol, ACT.Identity, bias=rcol, scale=-1.0)
+    A(V("nq", 0, 128), V("nv", 0, 128), ACT.Abs, bias=gcol, scale=-1.0)
+    A(V("nqq", 0, 128), V("nvq", 0, 128), ACT.Abs, bias=gcol, scale=-1.0)
     A(cthr, tcol, ACT.Identity, bias=36.0 + 0.5 / M, scale=-9.0)
     A(ca4, tcol, ACT.Identity, bias=2.0 - 144.0 * M, scale=36.0 * M)
     A(cov, tcol, ACT.Identity, bias=1020.0)
     for s in (3, 2, 1, 0):
         ts(V("gt", 512 + s, 1024, 4), V("nq", 0, 128), float(s), 0.5, ALU.is_le, ALU.mult)
-    for s in range(2):
+    for s in range(4):
         A(V("gt", s, 512, 4), V("gt", 515, 1024, 4), ACT.Copy)
-        ts(V("gt", 2 + s, 512, 4), V("nq", 0, 128), 3.0, 0.5, ALU.is_le, ALU.mult)
     for s in range(4):
         ts(V("gt", 1024 + s, 1536, 4), V("nqq", 0, 128), float(s), 0.5, ALU.is_equal, ALU.mult)
-    ms(V("gt", 1536, 2048), 0.0)
-    ms(V("bt", 0, 512), 0.0)
+    A(V("gt", 1536, 2048), V("eb", 0, 512), ACT.Copy)
+    iota(V("bt", 0, 512), [[0, 512]], 0, 0)
     ts(V("gt", 1536, 2048, 4), V("nqq", 0, 128), tcol, 4.0, ALU.is_equal, ALU.mult)
-    ts(V("mq", 0, 4), V("jq", 0, 4), qcol, None, ALU.is_equal)
+    ts(V("mq", 0, 4), V("iw", 0, 16, 4), q4col, None, ALU.is_equal)
+    A(V("mb", 0, 4), V("mq", 0, 4), ACT.Copy, scale=1.0e4)
     ts(V("eb", 3, 515, 4), V("iw", 0, 128), pcol, 0.5, ALU.is_equal, ALU.mult)
     quant("gq", "gsc", 0, 256, V("gt", 0, 1024))
     ts(V("k6", 0, 6), V("iw", 0, 96, 16), rcol, 1.0e-4, ALU.add, ALU.max)
@@ -359,12 +284,12 @@ def rank_program(g, core, T, topo):
     quant("uq", "usc", 0, 128, V("ut", 0, 512))
     A(V("k96", 0, 96), V("iw", 0, 96), ACT.Copy, scale=1.0 / M)
     rcp(V("r6", 0, 6), V("k6", 0, 6))
-    ts(V("m2", 0, 128), V("jq", 0, 128), qcol, 1.0e6, ALU.is_equal, ALU.mult)
+    for j in range(4):
+        A(V("m2", j, 128, 4), V("c36", 0, 32), ACT.Copy, scale=V("mb", j, j + 1))
     quant("gq", "gsc", 256, 512, V("gt", 1024, 2048))
     NV = CFG["nv"]
     AC = 32 * NV - NV
-    if NV:
-        A(V("w6", 0, NV), V("r6", 0, NV), ACT.Copy, scale=M * (1.0 - 5.0e-7))
+    A(V("w6", 0, NV), V("r6", 0, NV), ACT.Copy, scale=M * (1.0 - 5.0e-7))
     A(V("w6", NV, 6), V("r6", NV, 6), ACT.Copy, scale=-M * (1.0 - 5.0e-7))
 
     def q_state(b, a0, a1):
@@ -373,8 +298,7 @@ def rank_program(g, core, T, topo):
     def a_mm(b, bank, lq, ls, l0, a0, a1):
         mm(bank, lq, ls, l0, "aq", "asc", TC * b + a0, TC * b + a1, 128 * (b + 1))
 
-    def signs(b, a0, a1, c):
-        lab("z%d" % c)
+    def signs(b, c, a0, a1):
         bank = take()
         a_mm(b, bank, "uq", "usc", 0, a0, a1)
         z = V("p%d" % bank, 0, a1 - a0)
@@ -383,25 +307,21 @@ def rank_program(g, core, T, topo):
             move(CFG["y"][c], V("ys", a0, a1), z, 1.0)
         give(bank)
 
-    def way(b):
+    def write(b, land, src):
         peer = T.cores[rank ^ (1 << (b % 2))]
         rid, pid, _ = topo.addr(peer)
-        return rid, pid, topo.engines(core, peer)
+        return g.remote_dma(land, src, T.sem["arr%d" % b], T.sem.left, pid, rid, topo.mask(core, peer))
+
+    def count(b):
+        sent[b] += 2 * len(topo.engines(core, T.cores[rank ^ (1 << (b % 2))]))
 
     def send_first():
-        rid, pid, eng = way(0)
-        mask = sum(1 << e for e in eng)
         sq_, ss_, lq, ls = V("aq", 0, 1), V("asc", 128, 129), V("cq", CW, CW + 1), V("csc", CW, CW + 1)
-        first.append(op("g", lambda: g.remote_dma(lq[0].bitcast(dt.uint8), sq_[0].bitcast(dt.uint8), T.sem.arr0, T.sem.left, pid, rid, mask), [sq_], [], 1.3))
-        first.append(op("g", lambda: g.remote_dma(ls[0], ss_[0], T.sem.arr0, T.sem.left, pid, rid, mask), [ss_], [], 0.3))
-        sent[0] += 2 * len(eng)
+        op("g", lambda: write(0, lq[0].bitcast(dt.uint8), sq_[0].bitcast(dt.uint8)), [sq_], [])
+        op("g", lambda: write(0, ls[0], ss_[0]), [ss_], [])
+        count(0)
 
-    def plan(b):
-        fin = b == R - 1 and CFG["fch"]
-        return pieces(CFG["fch" if fin else "ch"]), CFG["fh" if fin else "h"], CFG["fr" if fin else "r"]
-
-    def span(b, e, who):
-        CH, H, _ = plan(b)
+    def span(e, who):
         mine = [CH[c] for c in range(len(CH)) if H[c][e] == who]
         return (mine[0][0], mine[-1][1]) if mine else None
 
@@ -413,29 +333,19 @@ def rank_program(g, core, T, topo):
         mm(b3, "gq", "gsc", 128, "sq", "ssc", 128 * b, 128 * b + 128)
         scan(V("cw", 0, 128), V("p%d" % b2, 0, 128), V("c36", 0, 128), 0.0, ALU.add, ALU.add)
         for m in range(NV):
-            lab("c%d" % m)
             j = V("junk", 32 * m, 32 * m + 32)
             ts(j, V("cw", 3, 128, 4), V("w6", m, m + 1), S, ALU.mult, ALU.is_lt)
             scan(V("acc", m, AC + m + 1, NV), j, j, -32.0, ALU.add, ALU.add)
         for m in range(NV, 6):
-            lab("c%d" % m)
             A(V("junk", 32 * m, 32 * m + 32), V("cw", 3, 128, 4), ACT.Sign, bias=S, scale=V("w6", m, m + 1), acc=V("acc", AC + m, AC + m + 1))
-        lab("F")
         tt(V("ew", 0, 128), V("cw", 0, 128), V("p%d" % b3, 0, 128), ALU.subtract)
         give(b2, b3)
-        if CFG["th"] == "v":
-            ts(V("th96", 0, 96), V("k96", 0, 96), S, cthr, ALU.mult, ALU.add)
-        else:
-            A(V("th96", 0, 96), V("k96", 0, 96), ACT.Identity, bias=cthr, scale=S)
+        A(V("th96", 0, 96), V("k96", 0, 96), ACT.Identity, bias=cthr, scale=S)
         scan(V("ed", 0, 128), V("m2", 0, 128), V("ew", 0, 128), 0.0, ALU.max, ALU.min)
         ts(V("o2", 0, 6), V("acc", AC, AC + 6), 2.0, 67.0, ALU.mult, ALU.add)
         tt(V("cmp", 0, 96), IND(V("ed", 0, 128), V("o2", 0, 6)), V("th96", 0, 96), ALU.is_le)
         for j in range(4):
-            bo, bi = V("bt", 4 * j, 96, 16), V("acc", AC, AC + 6)
-            if CFG["bt"][j] == "s":
-                A(bo, bi, ACT.Copy, scale=V("mq", j, j + 1))
-            else:
-                ts(bo, bi, V("mq", j, j + 1), None, ALU.mult)
+            A(V("bt", 4 * j, 96, 16), V("acc", AC, AC + 6), ACT.Copy, scale=V("mq", j, j + 1))
         quant("bq", "bsc", 128 * b, 128 * b + 128, V("bt", 0, 512))
         dc = (CS - CQ) * b
         quant("cq", "csc", CQ * b, CQ * b + CW, V("cmp", 0, 4 * CW), dc)
@@ -449,23 +359,15 @@ def rank_program(g, core, T, topo):
         A(V("vt", 192, 384), IND(st, V("ov", 12, 24)), ACT.Copy)
         quant("vq", "asc", 128 * b, 128 * b + 128, V("vt", 0, 512), TC * b)
         f = 1 if b == 0 else 0
-        rid, pid, eng = way(b)
-        h = len(eng) // 2
-        sq_, ss_ = V("vq", 128 * b + f, 128 * b + M), V("asc", AS * b + f, AS * b + f + 4 * (M - f))
-        lq, ls = V("cq", CQ * b + CW + f, CQ * (b + 1)), V("csc", CS * b + CW + f, CS * b + CW + f + 4 * (M - f))
-        arr = T.sem["arr%d" % b]
-        to = [DstId(rid=rid, pnc=pid)]
-        pair = [RemoteDMATransfer(dst_ids=to, dma_engine_mask=sum(1 << e for e in eng[:h]), remote_sem=arr,
-                                  src=sq_[0].bitcast(dt.uint8), dst=lq[0].bitcast(dt.uint8)),
-                RemoteDMATransfer(dst_ids=to, dma_engine_mask=sum(1 << e for e in eng[h:]), remote_sem=arr, src=ss_[0], dst=ls[0])]
-        gone = op("g", lambda: g.remote_dma_fused(pair, local_sem=T.sem.left), [sq_, ss_], [], 0.3, after=[(j, 0.3) for j in first])
-        sent[b] += len(eng)
+        sq_, ss_ = V("vq", 128 * b + f, 128 * b + M), V("asc", AS * b + f, AS * b + M)
+        lq, ls = V("cq", CQ * b + CW + f, CQ * (b + 1)), V("csc", CS * b + CW + f, CS * b + CW + M)
+        op("g", lambda: [write(b, lq[0].bitcast(dt.uint8), sq_[0].bitcast(dt.uint8)), write(b, ls[0], ss_[0])], [sq_, ss_], [])
+        count(b)
         if b == 0:
-            iota(V("c9", 0, 512), [[0, 512]], 9, 0, after=[(gone, 0.3)])
-            iota(V("sgf", 0, 2048), [[0, 2048]], 0, 0, after=[(gone, 0.3)])
+            iota(V("c9", 0, 512), [[0, 512]], 9, 0)
+            iota(V("sgf", 0, 2048), [[0, 2048]], 0, 0)
         for e in range(4):
-            lab("da%d" % e)
-            sp = span(b, e, "v")
+            sp = span(e, "v")
             if sp:
                 bank = take()
                 a_mm(b, bank, "eq", "esc", 128 * e, sp[0], sp[1])
@@ -473,22 +375,18 @@ def rank_program(g, core, T, topo):
                 give(bank)
         held = {}
         for e in range(4):
-            lab("hd%d" % e)
-            sp = span(b, e, "s")
+            sp = span(e, "s")
             if sp:
                 held[e] = (take(), sp[0], sp[1])
                 a_mm(b, held[e][0], "eq", "esc", 128 * e, sp[0], sp[1])
-        lab("P")
         big = 1.5 * 2.0 ** 25
         rcp(V("sm", 0, 1), S)
         ts(V("sm", 1, 2), S, -2.0, ca4, ALU.mult, ALU.add)
         ts(V("x4", 0, 32), V("ed", 3, 128, 4), 4.0 * M, V("sm", 1, 2), ALU.mult, ALU.add)
         ts(V("y4", 0, 32), V("x4", 0, 32), V("sm", 0, 1), big, ALU.mult, ALU.add)
         ts(V("op", 0, 32), V("y4", 0, 32), big, 0.25, ALU.subtract, ALU.mult)
-        op("x", None, [], [V("cq", CQ * b + CW, CQ * (b + 1)), V("csc", CS * b + CW, CS * (b + 1))], 0.0, sem=("arr%d" % b, sent[b]),
-           after=[(gone, CFG["far"])])
+        op("x", None, [], [V("cq", CQ * b + CW, CQ * (b + 1)), V("csc", CS * b + CW, CS * (b + 1))], sem=("arr%d" % b, sent[b]))
         for e in CFG["dvo"]:
-            lab("dv%d" % e)
             bank = take()
             mm(bank, "eq", "esc", 128 * e, "cq", "csc", CQ * (b + 1) - 128, CQ * (b + 1), dc)
             move(CFG["dv"][e], V("dv", M * e, M * (e + 1)), V("p%d" % bank, 128 - M, 128), 1.0)
@@ -496,11 +394,9 @@ def rank_program(g, core, T, topo):
         return held
 
     def next_state(b, c, held):
-        CH, H, RC = plan(b)
         a0, a1 = CH[c]
         off = V("op", a0 // 16, a1 // 16)
         for e in range(4):
-            lab("h%d%d" % (c, e))
             out, win = V("ht", 4 * a0 + e, 4 * a1, 4), V("dv", M * e, M * (e + 1))
             if H[c][e] == "v":
                 tt(out, IND(win, off), V("da", TC * e + a0, TC * e + a1), ALU.add)
@@ -511,31 +407,15 @@ def rank_program(g, core, T, topo):
                 tt(out, V("p%d" % bank, a0 - s0, a1 - s0), dg, ALU.add)
                 if a1 == s1:
                     give(bank)
-        lab("qh%d" % c)
         quant("hq", "hsc", TC * b + a0, TC * b + a1, V("ht", 4 * a0, 4 * a1))
         for i in range(4):
-            lab("w%d%d" % (c, i))
             bank = take()
             mm(bank, "wq", "wsc", 128 * i, "hq", "hsc", TC * b + a0, TC * b + a1)
             move(RC[c][i], V("t%d" % (b + 1), 4 * a0 + i, 4 * a1, 4), V("p%d" % bank, 0, a1 - a0), 0.03125)
             give(bank)
-        lab("qa%d" % c)
         q_state(b + 1, a0, a1)
 
-    def st_codes(a0, a1):
-        v = V("aq", TC * R + a0, TC * R + a1)
-        store("y", T.oc[:, 4 * a0:4 * a1], v[0].bitcast(dt.uint8), [v], 512 * (a1 - a0))
-
-    def st_scales(e, k):
-        o = AS * R + 128
-        store(e, T.osc[4 * k:4 * k + 4, :], T.asc[32 * k:32 * k + 4, o:o + TC], [V("asc", o, o + TC)], 2048)
-
-    def st_y(e, a0, a1):
-        v = V("ys", a0, a1)
-        store(e, T.y[:, a0:a1], v[0], [v], 512 * (a1 - a0))
-
     def last_clocks(a0, a1):
-        lab("l%d" % a0)
         o = 128 * R
         quant("sq", "ssc", o + a0, o + a1, V("sgf", 4 * a0, 4 * a1))
         bank = take()
@@ -543,41 +423,32 @@ def rank_program(g, core, T, topo):
         scan(V("cs", a0, a1), V("p%d" % bank, 0, a1 - a0), V("c9", a0, a1), V("cs", a0 - 1, a0) if a0 else 0.0, ALU.add, ALU.add)
         give(bank)
 
-    sent, first = [0] * R, []
+    sent = [0] * R
     for c, (a0, a1) in enumerate(XC):
         q_state(0, a0, a1)
         if c == 0:
             send_first()
-        signs(0, a0, a1, c)
+        signs(0, c, a0, a1)
     for b in range(R):
-        part[:] = ["x", "", 0]
         held = exchange(b)
-        part[0] = "f" if b == R - 1 else "n"
-        CH = plan(b)[0]
-        n, lag = len(CH), CFG["zl"]
-        for c in range(n + lag):
-            if c < n:
+        for c in range(len(CH) + 1):
+            if c < len(CH):
                 next_state(b, c, held)
-            if c >= lag:
-                signs(b + 1, CH[c - lag][0], CH[c - lag][1], c - lag)
+            if c:
+                signs(b + 1, c - 1, *CH[c - 1])
                 if b == R - 1:
-                    last_clocks(CH[c - lag][0], CH[c - lag][1])
-    part[:] = ["o", "", 0]
-    edge = [a for (a, _) in CH] + [TC]
-    todo = []
-    for kind, ends in (("oc", CFG["soc"]), ("y", CFG["sy"])):
-        for (c0, c1) in pieces([0] + ends):
-            todo.append((c1 + (0.6 if kind == "y" else 0.0), kind, edge[c0], edge[c1]))
-    todo.append((len(CH) + 0.3, "osc", 0, 0))
-    for (_, kind, a0, a1) in sorted(todo):
-        if kind == "oc":
-            st_codes(a0, a1)
-        elif kind == "y":
-            st_y("y", a0, a1)
-        else:
+                    last_clocks(*CH[c - 1])
+    for c, (a0, a1) in enumerate(CH):
+        v = V("aq", TC * R + a0, TC * R + a1)
+        store("y", T.oc[:, 4 * a0:4 * a1], v[0].bitcast(dt.uint8), [v])
+        if c == len(CH) - 1:
+            o = AS * R + 128
             for k in range(4):
-                st_scales(CFG["oq"][k], k)
-    store("s", T.cl[:], T.cs[0:128:16, :], [V("cs", 0, 512)], 16384)
-    op("y", None, outs, [], 0.01)
-    emit(arrange(ops), {"g": g, "v": vec, "s": act, "t": pe, "y": syn}, T)
+                store(CFG["oq"][k], T.osc[4 * k:4 * k + 4, :], T.asc[32 * k:32 * k + 4, o:o + TC], [V("asc", o, o + TC)])
+        v = V("ys", a0, a1)
+        store("y", T.y[:, a0:a1], v[0], [v])
+    store("s", T.cl[:], T.cs[0:128:16, :], [V("cs", 0, 512)])
+    op("y", None, outs, [])
+    assert sorted(ORDER) == list(range(len(ops)))
+    emit([ops[i] for i in ORDER], {"g": g, "v": vec, "s": act, "t": pe, "y": syn}, T)
     g.wait_ge(T.sem.left, sum(sent))

@@ -2,18 +2,20 @@ from concourse.mybir import dt, AluOpType as ALU, ActivationFunctionType as ACT
 
 TC, M, R = 512, 96, 3
 CFG = {
-    "ch": [0, 192, 384, 512],
-    "h": ["vvss", "vvss", "vvss"],
-    "r": ["ssss", "ssss", "svvs"],
-    "dv": "ssss", "dvo": [0, 2, 1, 3],
-    "da": "vsvv",
-    "y": "vsv",
-    "xc": [0, 320, 512], "xq": "sy",
+    "ch": [0, 224, 384, 512],
+    "hv": [[(0, 224), (224, 384)], [(0, 224)], [(0, 224)], []],
+    "hs": [[], [(224, 384)], [(224, 384)], [(0, 224), (224, 384)]],
+    "X": (384, 512),
+    "dvo": [0, 2, 1, 3],
+    "xc": [0, 256, 384, 512], "xq": "syy",
     "nv": 2,
+    "vs": 12,
+    "w1": [96, 56, 56],
     "oq": "yyss",
+    "eng": "ssssssssvvsvsvvssvssssssvssssvsvvssssvvvssvsssvsssssvssssssvvvssvsvsvvssvsssssvsvssvssssvvvsss",
 }
-ORDER = [0, 1, 2, 3, 4, 5, 6, 7, 8, 37, 11, 13, 10, 14, 15, 12, 9, 16, 17, 19, 48, 43, 25, 24, 50, 58, 36, 20, 18, 39, 26, 38, 28, 49, 31, 61, 59, 60, 29, 30, 62, 63, 32, 27, 34, 33, 35, 42, 64, 65, 40, 54, 23, 57, 21, 51, 22, 56, 53, 52, 66, 55, 67, 68, 69, 41, 72, 70, 78, 73, 71, 76, 77, 75, 74, 79, 83, 84, 86, 85, 80, 81, 82, 87, 88, 89, 90, 44, 91, 92, 93, 94, 98, 46, 105, 102, 106, 45, 47, 100, 99, 104, 107, 108, 103, 101, 95, 109, 110, 116, 112, 114,
-         111, 117, 113, 122, 115, 120, 136, 156, 138, 154, 134, 118, 123, 119, 121, 137, 124, 135, 139, 157, 140, 155, 152, 153, 125, 127, 129, 131, 126, 128, 130, 132, 158, 143, 141, 145, 147, 144, 142, 146, 148, 133, 163, 159, 165, 161, 164, 149, 162, 150, 160, 166, 151, 167, 168, 170, 169, 171, 172, 173, 174, 175, 176, 178, 184, 177, 179, 180, 182, 183, 181, 185, 191, 192, 189, 190, 186, 187, 209, 188, 193, 194, 195, 196, 197, 199, 198, 210, 200, 208, 211, 212, 204, 207, 202, 203, 206, 205, 97, 96, 201, 213, 214, 220, 216, 215, 218, 221, 217, 226, 219, 224, 238, 222, 227, 223, 225, 240, 242, 260, 258, 241, 228, 239, 243, 229, 231, 233, 235, 261, 244, 256, 259, 257, 247, 245, 230, 249, 234, 232, 236, 248, 246, 251, 250, 252, 262, 237, 267, 263, 265, 269, 264, 270, 268, 253, 266, 254, 255, 271, 272, 274, 273, 275, 276, 277, 278, 279, 280, 282, 288, 281, 283, 284, 286, 285, 287, 289, 295, 296, 293, 294, 290, 291, 313, 292, 297, 298, 306, 310, 299, 300, 308, 311, 301, 303, 302, 314, 304, 305, 312, 317, 315, 316, 307, 309, 318, 324, 320, 322, 319, 325, 321, 330, 323, 328, 342, 326, 331, 327, 329, 344, 366, 346, 368, 345, 332, 339, 333, 340, 334, 343, 347, 335, 337, 336, 338, 367, 348, 369, 365, 364, 341, 351, 349, 353, 355, 352, 350, 354, 356, 370, 358, 360, 371, 373, 375, 377, 357, 359, 372, 374, 376, 361, 378, 380, 381, 382, 362, 379, 386, 387, 392, 393, 394, 383, 363, 384, 389, 388, 396, 398, 395, 397, 401, 385, 390, 391, 400, 399, 402, 403]
+ORDER = [13,6,1,7,11,15,14,16,8,12,0,19,23,10,17,2,26,24,44,25,28,20,3,38,32,27,52,30,4,18,31,43,29,45,54,55,21,57,5,9,51,33,56,58,66,53,59,34,67,22,60,68,35,50,48,61,46,62,96,69,63,70,47,36,71,72,49,64,79,75,73,78,81,80,76,37,74,77,83,82,65,108,84,86,85,87,88,89,107,90,109,91,110,92,93,111,94,41,95,40,102,39,100,42,103,98,112,119,179,113,115,117,120,114,116,118,101,123,121,126,99,124,130,122,127,128,106,125,131,134,105,104,129,173,182,152,176,132,135,133,150,172,136,174,183,148,180,153,177,137,175,184,151,140,181,149,144,178,138,147,142,145,185,141,154,190,139,186,143,155,157,191,161,156,159,187,192,188,158,146,160,162,164,189,193,163,165,194,195,166,197,226,196,167,198,168,199,169,200,228,170,201,202,171,208,205,203,209,211,210,206,204,207,213,212,214,236,216,215,217,218,219,235,220,304,237,230,221,310,238,223,222,239,229,224,227,225,240,245,241,243,247,246,242,248,244,231,251,249,252,258,256,250,253,254,259,301,233,257,260,307,234,255,97,263,232,261,276,262,278,300,264,308,311,280,302,277,305,265,309,312,281,270,303,279,272,306,268,275,266,273,313,269,282,320,267,318,271,283,289,321,285,284,287,319,316,314,290,274,286,288,292,315,317,356,291,293,322,323,294,325,358,324,296,326,295,327,297,328,329,298,427,330,299,333,338,331,337,339,335,334,332,336,341,340,342,364,344,357,343,345,346,347,363,348,430,365,436,349,354,366,350,351,362,367,355,352,359,353,368,369,373,375,371,370,374,376,372,379,377,382,386,384,378,383,380,387,385,390,361,360,381,391,389,404,388,408,426,392,428,437,406,431,405,433,434,393,429,438,403,396,432,398,409,435,400,407,394,397,439,399,410,444,401,446,395,415,411,445,413,416,417,402,440,442,412,414,418,420,441,447,443,421,419,448,449,463,423,455,468,465,450,422,461,424,456,452,466,451,462,425,453,457,464,458,454,467,470,459,469,460,471,472]
+BANKS = [0,1,3,4,2,5,6,7,2,1,0,5,1,0,4,5,7,6,2,7,4,0,5,6,7,0,1,7,0,2,6,3,4,3,4,1,2,5,3,2,1,5,6,4,7,5,7,1,2,4,5,1,0,2,4,5,7,5,2,3,1,0,2,6,3,2,0,4,0,6,1,6,3,4,1,3,4,7,5,3,7,1,5,7,4,3,2,5,3,6,7,5,4,3,0,5,6,0,4,2,6,2,0,1,4,3,7,6]
 CW = 128
 CQ, CS = CW + M, CW + 4 * M
 AS = 128 + TC
@@ -29,29 +31,32 @@ SCRATCH = {
     "aq": _sb(4 * TC, F8), "asc": _sb(4 * AS, U8),
     "ut": _sb(512, BF), "uq": _sb(128, F8), "usc": _sb(128, U8),
     "wq": _sb(512, F8), "wsc": _sb(512, U8),
-    "ht": _sb(2048, BF), "hq": _sb(R * TC, F8), "hsc": _sb(R * TC, U8),
-    "da": _sb(2048, BF), "dg": _sb(2048, BF), "dv": _sb(384, BF), "vt": _sb(512, BF),
+    "ht": _sb(2048, BF), "hq": _sb(R * (TC + 128), F8), "hsc": _sb(R * (TC + 128), U8),
+    "da": _sb(2048, BF), "dg": _sb(2048, BF), "dv": _sb(384, BF), "vt": _sb(1648, BF),
     "vq": _sb(R * 128, F8),
-    "sg": _sb(512, BF), "sgf": _sb(2048, BF), "sq": _sb(R * 128 + TC, F8), "ssc": _sb(R * 128 + TC, U8),
-    "cmp": _sb(4 * CW, BF), "cq": _sb(R * CQ, F8), "csc": _sb(R * CS, U8),
+    "sgf": _sb(2048, BF), "sq": _sb(R * 256 + TC, F8), "ssc": _sb(R * 256 + TC, U8),
+    "cq": _sb(R * CQ, F8), "csc": _sb(R * CS, U8),
     "eb": _sb(528, BF), "eq": _sb(512, F8), "esc": _sb(512, U8),
-    "nv": _sb(128, BF), "nvq": _sb(128, BF), "nq": _sb(128, BF), "nqq": _sb(128, BF),
-    "gt": _sb(2048, BF), "gq": _sb(512, F8), "gsc": _sb(512, U8),
-    "bt": _sb(512, BF), "bq": _sb(R * 128, F8), "bsc": _sb(R * 128, U8), "mq": _sb(4, F32), "mb": _sb(4, F32),
+    "nv": _sb(128, BF), "nq": _sb(128, BF), "w4": _sb(128, F32), "dq": _sb(512, BF),
+    "gt": _sb(1536, BF), "gq": _sb(512, F8), "gsc": _sb(512, U8),
+    "bq": _sb(R * 128, F8), "bsc": _sb(R * 128, U8),
     "pi": _sb(4, I32), "rf": _sb(8, F32), "col": _sb(8, F32), "tiny": _sb(4, F32),
-    "iw": _sb(128, F32), "c36": _sb(128, F32), "c9": _sb(512, F32),
+    "iw": _sb(128, F32), "c9": _sb(512, F32),
     "k6": _sb(8, F32), "r6": _sb(8, F32), "w6": _sb(8, F32), "k96": _sb(96, F32), "m2": _sb(128, F32),
     "cw": _sb(128, F32), "ew": _sb(128, F32), "ed": _sb(128, F32), "th96": _sb(96, F32),
-    "junk": _sb(192, F32), "acc": _sb(104, F32),
-    "o2": _sb(8, U16), "ov": _sb(24, U16), "op": _sb(32, U16),
-    "sm": _sb(8, F32), "x4": _sb(32, F32), "y4": _sb(32, F32),
+    "junk": _sb(192, F32), "acc": _sb(200, F32), "ob": _sb(2, U16), "mq32": _sb(32, F32),
+    "lp": _sb(8 * R, U16), "lo": _sb(32, U16), "xt": _sb(512, BF), "xq": _sb(R * 128, F8), "xs": _sb(R * 128, U8),
+    "xl": _sb(R * 128, F8), "xls": _sb(R * 128, U8),
+    "o2": _sb(8, U16), "ov": _sb(24, U16), "op": _sb(32 * R, U16),
+    "sm": _sb(8, F32), "x4": _sb(32, F32),
     "ys": _sb(512, F32), "cs": _sb(512, F32),
 }
 for _b in range(8):
     SCRATCH["p%d" % _b] = ("psum", [128, 512], F32)
 
 NC, ND = 110, 24
-SEMAPHORES = ["arr0", "arr1", "arr2", "left"] + ["c%d" % _i for _i in range(NC)] + ["d%d" % _i for _i in range(ND)]
+SEMAPHORES = (["arr0", "arr1", "arr2", "lst0", "lst1", "lst2", "xar0", "xar1", "xar2", "left"]
+              + ["c%d" % _i for _i in range(NC)] + ["d%d" % _i for _i in range(ND)])
 
 
 def is_bank(k):
@@ -209,32 +214,41 @@ def rank_program(g, core, T, topo):
         op(e, lambda: q.dma_start(out, a), r, w, dma=True)
 
     outs = []
+    marks = []
 
     def store(e, out, a, r):
         tag = (None, [("out%d" % len(outs), 1)])
         outs.append(tag)
         dma(e, out, a, r, [tag])
 
-    def move(e, out, a, scale):
-        if e == "s":
+    def who():
+        marks.append((len(ops), CFG["eng"][len(marks)]))
+        return marks[-1][1]
+
+    def move(out, a, scale):
+        if who() == "s":
             A(out, a, ACT.Copy, scale=scale)
         elif scale == 1.0:
             cp(out, a)
         else:
             ts(out, a, scale, None, ALU.mult)
 
-    idle = list(range(8))
+    def affine(out, a, scale, bias):
+        if who() == "s":
+            A(out, a, ACT.Identity, bias=bias, scale=scale)
+        else:
+            ts(out, a, scale, bias, ALU.mult, ALU.add)
+
+    taken = [0]
 
     def take():
-        return idle.pop(0)
-
-    def give(*banks):
-        idle.extend(banks)
+        taken[0] += 1
+        return taken[0] - 1 if CFG.get("virt") else BANKS[taken[0] - 1]
 
     def pieces(edges):
         return list(zip(edges[:-1], edges[1:]))
 
-    XC, CH, H, RC = pieces(CFG["xc"]), pieces(CFG["ch"]), CFG["h"], CFG["r"]
+    XC, CH, X = pieces(CFG["xc"]), pieces(CFG["ch"]), CFG["X"]
     dma("y", T.ut[:], T.u[:], [], [V("ut", 0, 512)])
     for c, (a, b) in enumerate(XC):
         v = V("t0", 4 * a, 4 * b)
@@ -243,52 +257,51 @@ def rank_program(g, core, T, topo):
     dma("y", T.wq[:].bitcast(dt.uint8), T.wc[:], [somex], [V("wq", 0, 512)])
     dma("y", T.wsc[:], T.ws[:], [somex], [V("wsc", 0, 512)])
 
+    NV = CFG["nv"]
+    AC, C36 = 64, 70
+    CM, BT, ZR, SG = 384, 480, 608, 1136
     pcol, gcol, tcol, rcol, q4col = V("rf", 0, 1), V("rf", 1, 2), V("rf", 2, 3), V("rf", 3, 4), V("rf", 5, 6)
-    cthr, ca4, cov = V("col", 0, 1), V("col", 1, 2), V("col", 2, 3)
+    cthr, ca4, cov, g4col, g4t = V("col", 0, 1), V("col", 1, 2), V("col", 2, 3), V("col", 3, 4), V("col", 4, 5)
     tiny = V("tiny", 0, 1)
     iota(V("pi", 0, 1), [[0, 1]], 0, 1, False)
     iota(V("nv", 0, 128), [[16, 8], [0, 4], [1, 4]], 0, 0)
     iota(V("iw", 0, 128), [[1, 128]], 0, 0)
-    iota(V("nvq", 0, 128), [[16, 8], [1, 4], [0, 4]], 0, 0)
+    iota(V("w4", 0, 128), [[0, 32], [4, 4]], 0, 0)
+    iota(V("dq", 0, 512), [[1, 32], [0, 4], [-1, 4]], 0, 0)
     ms(tiny, -2.0 ** -120)
-    ms(V("eb", 0, 528), 0.0)
-    iota(V("cmp", 96, 4 * CW), [[0, 4 * CW - 96]], 0, 0)
-    ms(V("vt", 384, 512), 0.0)
-    ms(V("c36", 0, 128), 36.0)
+    ms(V("vt", BT, SG), 0.0)
+    ms(V("acc", C36, C36 + 128), 36.0)
     ts(V("pi", 1, 2), V("pi", 0, 1), 112, None, ALU.bitwise_and)
     ts(V("pi", 2, 3), V("pi", 0, 1), 3, None, ALU.bitwise_and)
     cp(V("rf", 0, 3), V("pi", 0, 3))
     A(rcol, gcol, ACT.Identity, bias=pcol, scale=-1.0)
     A(q4col, tcol, ACT.Identity, bias=rcol, scale=-1.0)
     A(V("nq", 0, 128), V("nv", 0, 128), ACT.Abs, bias=gcol, scale=-1.0)
-    A(V("nqq", 0, 128), V("nvq", 0, 128), ACT.Abs, bias=gcol, scale=-1.0)
     A(cthr, tcol, ACT.Identity, bias=36.0 + 0.5 / M, scale=-9.0)
     A(ca4, tcol, ACT.Identity, bias=2.0 - 144.0 * M, scale=36.0 * M)
     A(cov, tcol, ACT.Identity, bias=1020.0)
+    A(g4col, gcol, ACT.Copy, scale=0.25)
+    A(g4t, gcol, ACT.Identity, bias=tcol, scale=0.25)
     for s in (3, 2, 1, 0):
         ts(V("gt", 512 + s, 1024, 4), V("nq", 0, 128), float(s), 0.5, ALU.is_le, ALU.mult)
     for s in range(4):
-        A(V("gt", s, 512, 4), V("gt", 515, 1024, 4), ACT.Copy)
-    for s in range(4):
-        ts(V("gt", 1024 + s, 1536, 4), V("nqq", 0, 128), float(s), 0.5, ALU.is_equal, ALU.mult)
-    A(V("gt", 1536, 2048), V("eb", 0, 512), ACT.Copy)
-    iota(V("bt", 0, 512), [[0, 512]], 0, 0)
-    ts(V("gt", 1536, 2048, 4), V("nqq", 0, 128), tcol, 4.0, ALU.is_equal, ALU.mult)
-    ts(V("mq", 0, 4), V("iw", 0, 16, 4), q4col, None, ALU.is_equal)
-    A(V("mb", 0, 4), V("mq", 0, 4), ACT.Copy, scale=1.0e4)
-    ts(V("eb", 3, 515, 4), V("iw", 0, 128), pcol, 0.5, ALU.is_equal, ALU.mult)
+        move(V("gt", s, 512, 4), V("gt", 515, 1024, 4), 1.0)
     quant("gq", "gsc", 0, 256, V("gt", 0, 1024))
+    ts(V("gt", 1024, 1536), V("dq", 0, 512), g4col, 0.5, ALU.is_equal, ALU.mult)
+    ts(V("gt", 512, 1024, 4), V("dq", 0, 512, 4), g4t, 4.0, ALU.is_equal, ALU.mult)
+    quant("gq", "gsc", 256, 512, V("gt", 512, 1536))
+    eb, zr = V("eb", 0, 528), V("vt", ZR, SG)
+    op("g", lambda: g.affine_select(eb[0], zr[0], [[-1, 528]], ALU.not_equal, 0.5, 3, 4), [zr], [eb])
     ts(V("k6", 0, 6), V("iw", 0, 96, 16), rcol, 1.0e-4, ALU.add, ALU.max)
     for e in range(4):
         quant("eq", "esc", 128 * e, 128 * e + 128, V("eb", 3 - e, 515 - e))
     quant("uq", "usc", 0, 128, V("ut", 0, 512))
     A(V("k96", 0, 96), V("iw", 0, 96), ACT.Copy, scale=1.0 / M)
     rcp(V("r6", 0, 6), V("k6", 0, 6))
-    for j in range(4):
-        A(V("m2", j, 128, 4), V("c36", 0, 32), ACT.Copy, scale=V("mb", j, j + 1))
-    quant("gq", "gsc", 256, 512, V("gt", 1024, 2048))
-    NV = CFG["nv"]
-    AC = 32 * NV - NV
+    A(V("junk", 0, 128), V("w4", 0, 128), ACT.Abs, bias=q4col, scale=-1.0)
+    A(V("m2", 0, 128), V("junk", 0, 128), ACT.Relu, bias=2.0 ** 18, scale=-2.0 ** 18)
+    ts(V("ob", 0, 2), V("iw", 0, 32, 16), q4col, 0.25, ALU.add, ALU.mult)
+    A(V("mq32", 0, 32), V("m2", 0, 32), ACT.Copy, scale=2.0 ** -18)
     A(V("w6", 0, NV), V("r6", 0, NV), ACT.Copy, scale=M * (1.0 - 5.0e-7))
     A(V("w6", NV, 6), V("r6", NV, 6), ACT.Copy, scale=-M * (1.0 - 5.0e-7))
 
@@ -302,67 +315,83 @@ def rank_program(g, core, T, topo):
         bank = take()
         a_mm(b, bank, "uq", "usc", 0, a0, a1)
         z = V("p%d" % bank, 0, a1 - a0)
-        A(V("sgf", 4 * a0, 4 * a1, 4) if b == R else V("sg", a0, a1), z, ACT.Sign, bias=tiny)
+        A(V("sgf", 4 * a0, 4 * a1, 4) if b == R else V("vt", SG + a0, SG + a1), z, ACT.Sign, bias=tiny)
         if b == R:
-            move(CFG["y"][c], V("ys", a0, a1), z, 1.0)
-        give(bank)
+            move(V("ys", a0, a1), z, 1.0)
 
-    def write(b, land, src):
-        peer = T.cores[rank ^ (1 << (b % 2))]
-        rid, pid, _ = topo.addr(peer)
-        return g.remote_dma(land, src, T.sem["arr%d" % b], T.sem.left, pid, rid, topo.mask(core, peer))
+    def partner(b):
+        return T.cores[rank ^ (1 << (b % 2))]
 
-    def count(b):
-        sent[b] += 2 * len(topo.engines(core, T.cores[rank ^ (1 << (b % 2))]))
+    def write(b, land, src, sem="arr"):
+        rid, pid, _ = topo.addr(partner(b))
+        return g.remote_dma(land, src, T.sem[sem + str(b)], T.sem.left, pid, rid, topo.mask(core, partner(b)))
+
+    NE = [len(topo.engines(core, partner(b))) for b in range(R)]
 
     def send_first():
         sq_, ss_, lq, ls = V("aq", 0, 1), V("asc", 128, 129), V("cq", CW, CW + 1), V("csc", CW, CW + 1)
         op("g", lambda: write(0, lq[0].bitcast(dt.uint8), sq_[0].bitcast(dt.uint8)), [sq_], [])
         op("g", lambda: write(0, ls[0], ss_[0]), [ss_], [])
-        count(0)
 
-    def span(e, who):
-        mine = [CH[c] for c in range(len(CH)) if H[c][e] == who]
+    def x_chunk(b):
+        op("x", None, [], [V("xl", 128 * b, 128 * b + 128), V("xls", 128 * b, 128 * b + 128)], sem=("xar%d" % b, 2 * NE[b]))
+        for e in range(4):
+            bank = take()
+            mm(bank, "eq", "esc", 128 * e, "aq", "asc", TC * b + X[0], TC * b + X[1], 128 * (b + 1), True, False)
+            mm(bank, "eq", "esc", 128 * e, "xl", "xls", 128 * b, 128 * b + 128, 0, False, True)
+            move(V("ht", 4 * X[0] + e, 4 * X[1], 4), V("p%d" % bank, 0, 128), 1.0)
+
+    def span(e, k):
+        mine = CFG["h" + k][e]
         return (mine[0][0], mine[-1][1]) if mine else None
+
+    def clock_part(b, w0, w1):
+        o = 256 * b + (128 if w0 else 0)
+        quant("sq", "ssc", o, o + 128, V("vt", SG + 4 * w1 - 512, SG + 4 * w1))
+        b2, b3 = take(), take()
+        mm(b2, "gq", "gsc", 0, "sq", "ssc", o, o + 128)
+        mm(b3, "gq", "gsc", 128, "sq", "ssc", o, o + 128)
+        n = w1 - w0
+        scan(V("cw", w0, w1), V("p%d" % b2, 128 - n, 128), V("acc", C36, C36 + n), V("cw", w0 - 1, w0) if w0 else 0.0, ALU.add, ALU.add)
+        return b3
+
+    def early_clocks(b):
+        w1 = CFG["w1"][b]
+        b3 = clock_part(b, 0, w1)
+        tt(V("ew", 0, w1), V("cw", 0, w1), V("p%d" % b3, 128 - w1, 128), ALU.subtract)
+        scan(V("ed", 0, w1), V("m2", 0, w1), V("ew", 0, w1), 0.0, ALU.max, ALU.min)
 
     def exchange(b):
         S = V("cw", 127, 128)
-        quant("sq", "ssc", 128 * b, 128 * b + 128, V("sg", 0, 512))
-        b2, b3 = take(), take()
-        mm(b2, "gq", "gsc", 0, "sq", "ssc", 128 * b, 128 * b + 128)
-        mm(b3, "gq", "gsc", 128, "sq", "ssc", 128 * b, 128 * b + 128)
-        scan(V("cw", 0, 128), V("p%d" % b2, 0, 128), V("c36", 0, 128), 0.0, ALU.add, ALU.add)
+        w1 = CFG["w1"][b]
+        b3 = clock_part(b, w1, 128)
         for m in range(NV):
             j = V("junk", 32 * m, 32 * m + 32)
             ts(j, V("cw", 3, 128, 4), V("w6", m, m + 1), S, ALU.mult, ALU.is_lt)
-            scan(V("acc", m, AC + m + 1, NV), j, j, -32.0, ALU.add, ALU.add)
+            scan(V("acc", AC + m - 31 * NV, AC + m + 1, NV), j, j, -32.0, ALU.add, ALU.add)
         for m in range(NV, 6):
             A(V("junk", 32 * m, 32 * m + 32), V("cw", 3, 128, 4), ACT.Sign, bias=S, scale=V("w6", m, m + 1), acc=V("acc", AC + m, AC + m + 1))
-        tt(V("ew", 0, 128), V("cw", 0, 128), V("p%d" % b3, 0, 128), ALU.subtract)
-        give(b2, b3)
+        tt(V("ew", w1, 128), V("cw", w1, 128), V("p%d" % b3, w1, 128), ALU.subtract)
         A(V("th96", 0, 96), V("k96", 0, 96), ACT.Identity, bias=cthr, scale=S)
-        scan(V("ed", 0, 128), V("m2", 0, 128), V("ew", 0, 128), 0.0, ALU.max, ALU.min)
+        scan(V("ed", w1, 128), V("m2", w1, 128), V("ew", w1, 128), 0.0, ALU.max, ALU.min)
         ts(V("o2", 0, 6), V("acc", AC, AC + 6), 2.0, 67.0, ALU.mult, ALU.add)
-        tt(V("cmp", 0, 96), IND(V("ed", 0, 128), V("o2", 0, 6)), V("th96", 0, 96), ALU.is_le)
-        for j in range(4):
-            A(V("bt", 4 * j, 96, 16), V("acc", AC, AC + 6), ACT.Copy, scale=V("mq", j, j + 1))
-        quant("bq", "bsc", 128 * b, 128 * b + 128, V("bt", 0, 512))
+        tt(V("vt", CM, CM + M), IND(V("ed", 0, 128), V("o2", 0, 6)), V("th96", 0, 96), ALU.is_le)
+        tt(V("vt", BT, BT + 128, 4), IND(V("acc", AC, AC + 8), V("ob", 0, 2)), V("mq32", 0, 32), ALU.mult)
+        quant("bq", "bsc", 128 * b, 128 * b + 128, V("vt", BT, BT + 512))
         dc = (CS - CQ) * b
-        quant("cq", "csc", CQ * b, CQ * b + CW, V("cmp", 0, 4 * CW), dc)
+        quant("cq", "csc", CQ * b, CQ * b + CW, V("vt", CM, CM + 512), dc)
         b0 = take()
-        mm(b0, "gq", "gsc", 384, "bq", "bsc", 128 * b, 128 * b + 128, 0, True, False)
-        mm(b0, "gq", "gsc", 256, "cq", "csc", CQ * b, CQ * b + 128, dc, False, True)
+        mm(b0, "gq", "gsc", 256, "bq", "bsc", 128 * b, 128 * b + 128, 0, True, False)
+        mm(b0, "gq", "gsc", 384, "cq", "csc", CQ * b, CQ * b + 128, dc, False, True)
         ts(V("ov", 0, 24), V("p%d" % b0, 0, 24), 8.0, cov, ALU.mult, ALU.add)
-        give(b0)
-        st = V("t%d" % b, 0, 2048)
-        cp(V("vt", 0, 192), IND(st, V("ov", 0, 12)))
-        A(V("vt", 192, 384), IND(st, V("ov", 12, 24)), ACT.Copy)
+        st, vs = V("t%d" % b, 0, 2048), CFG["vs"]
+        cp(V("vt", 0, 16 * vs), IND(st, V("ov", 0, vs)))
+        A(V("vt", 16 * vs, 384), IND(st, V("ov", vs, 24)), ACT.Copy)
         quant("vq", "asc", 128 * b, 128 * b + 128, V("vt", 0, 512), TC * b)
         f = 1 if b == 0 else 0
         sq_, ss_ = V("vq", 128 * b + f, 128 * b + M), V("asc", AS * b + f, AS * b + M)
         lq, ls = V("cq", CQ * b + CW + f, CQ * (b + 1)), V("csc", CS * b + CW + f, CS * b + CW + M)
         op("g", lambda: [write(b, lq[0].bitcast(dt.uint8), sq_[0].bitcast(dt.uint8)), write(b, ls[0], ss_[0])], [sq_, ss_], [])
-        count(b)
         if b == 0:
             iota(V("c9", 0, 512), [[0, 512]], 9, 0)
             iota(V("sgf", 0, 2048), [[0, 2048]], 0, 0)
@@ -371,73 +400,83 @@ def rank_program(g, core, T, topo):
             if sp:
                 bank = take()
                 a_mm(b, bank, "eq", "esc", 128 * e, sp[0], sp[1])
-                move(CFG["da"][e], V("da", TC * e + sp[0], TC * e + sp[1]), V("p%d" % bank, 0, sp[1] - sp[0]), 1.0)
-                give(bank)
+                move(V("da", TC * e + sp[0], TC * e + sp[1]), V("p%d" % bank, 0, sp[1] - sp[0]), 1.0)
         held = {}
         for e in range(4):
             sp = span(e, "s")
             if sp:
                 held[e] = (take(), sp[0], sp[1])
                 a_mm(b, held[e][0], "eq", "esc", 128 * e, sp[0], sp[1])
-        big = 1.5 * 2.0 ** 25
         rcp(V("sm", 0, 1), S)
-        ts(V("sm", 1, 2), S, -2.0, ca4, ALU.mult, ALU.add)
-        ts(V("x4", 0, 32), V("ed", 3, 128, 4), 4.0 * M, V("sm", 1, 2), ALU.mult, ALU.add)
-        ts(V("y4", 0, 32), V("x4", 0, 32), V("sm", 0, 1), big, ALU.mult, ALU.add)
-        ts(V("op", 0, 32), V("y4", 0, 32), big, 0.25, ALU.subtract, ALU.mult)
-        op("x", None, [], [V("cq", CQ * b + CW, CQ * (b + 1)), V("csc", CS * b + CW, CS * (b + 1))], sem=("arr%d" % b, sent[b]))
+        affine(V("sm", 1, 2), S, -2.0, ca4)
+        affine(V("x4", 0, 32), V("ed", 3, 128, 4), 4.0 * M, V("sm", 1, 2))
+        ts(V("op", 32 * b, 32 * b + 32), V("x4", 0, 32), V("sm", 0, 1), 0.25, ALU.mult, ALU.mult)
+        mine, lp = V("op", 32 * b + X[0] // 16, 32 * b + X[1] // 16), V("lp", 8 * b, 8 * b + 8)
+        op("g", lambda: write(b, lp[0], mine[0], "lst"), [mine], [])
+        op("x", None, [], [lp], sem=("lst%d" % b, NE[b]))
+        for e in range(4):
+            ts(V("lo", 8 * e, 8 * e + 8), lp, 4.0, float(e), ALU.mult, ALU.add)
+            move(V("xt", e, 512, 4), IND(V("vt", 0, 384), V("lo", 8 * e, 8 * e + 8)), 1.0)
+        quant("xq", "xs", 128 * b, 128 * b + 128, V("xt", 0, 512))
+        xq, xs, xl, xls = [V(k, 128 * b, 128 * b + 128) for k in ("xq", "xs", "xl", "xls")]
+        op("g", lambda: [write(b, xl[0].bitcast(dt.uint8), xq[0].bitcast(dt.uint8), "xar"), write(b, xls[0], xs[0], "xar")], [xq, xs], [])
+        op("x", None, [], [V("cq", CQ * b + CW, CQ * (b + 1)), V("csc", CS * b + CW, CS * (b + 1))], sem=("arr%d" % b, (2 + 2 * f) * NE[b]))
         for e in CFG["dvo"]:
             bank = take()
             mm(bank, "eq", "esc", 128 * e, "cq", "csc", CQ * (b + 1) - 128, CQ * (b + 1), dc)
-            move(CFG["dv"][e], V("dv", M * e, M * (e + 1)), V("p%d" % bank, 128 - M, 128), 1.0)
-            give(bank)
+            move(V("dv", M * e, M * (e + 1)), V("p%d" % bank, 128 - M, 128), 1.0)
         return held
 
     def next_state(b, c, held):
         a0, a1 = CH[c]
-        off = V("op", a0 // 16, a1 // 16)
         for e in range(4):
-            out, win = V("ht", 4 * a0 + e, 4 * a1, 4), V("dv", M * e, M * (e + 1))
-            if H[c][e] == "v":
-                tt(out, IND(win, off), V("da", TC * e + a0, TC * e + a1), ALU.add)
-            else:
+            win = V("dv", M * e, M * (e + 1))
+            for (x0, x1) in CFG["hv"][e]:
+                if a0 <= x0 < a1:
+                    tt(V("ht", 4 * x0 + e, 4 * x1, 4), IND(win, V("op", 32 * b + x0 // 16, 32 * b + x1 // 16)), V("da", TC * e + x0, TC * e + x1), ALU.add)
+            for (x0, x1) in CFG["hs"][e]:
+                if a0 <= x0 < a1:
+                    A(V("dg", TC * e + x0, TC * e + x1), IND(win, V("op", 32 * b + x0 // 16, 32 * b + x1 // 16)), ACT.Copy)
+            sp = span(e, "s")
+            if sp and max(a0, sp[0]) < min(a1, sp[1]):
                 bank, s0, s1 = held[e]
-                dg = V("dg", TC * e + a0, TC * e + a1)
-                A(dg, IND(win, off), ACT.Copy)
-                tt(out, V("p%d" % bank, a0 - s0, a1 - s0), dg, ALU.add)
-                if a1 == s1:
-                    give(bank)
-        quant("hq", "hsc", TC * b + a0, TC * b + a1, V("ht", 4 * a0, 4 * a1))
+                x0, x1 = max(a0, s0), min(a1, s1)
+                tt(V("ht", 4 * x0 + e, 4 * x1, 4), V("p%d" % bank, x0 - s0, x1 - s0), V("dg", TC * e + x0, TC * e + x1), ALU.add)
+        o = (TC + 128) * b + a0
+        quant("hq", "hsc", o, o + a1 - a0, V("ht", 4 * a0, 4 * a1))
         for i in range(4):
             bank = take()
-            mm(bank, "wq", "wsc", 128 * i, "hq", "hsc", TC * b + a0, TC * b + a1)
-            move(RC[c][i], V("t%d" % (b + 1), 4 * a0 + i, 4 * a1, 4), V("p%d" % bank, 0, a1 - a0), 0.03125)
-            give(bank)
+            mm(bank, "wq", "wsc", 128 * i, "hq", "hsc", o, o + a1 - a0)
+            move(V("t%d" % (b + 1), 4 * a0 + i, 4 * a1, 4), V("p%d" % bank, 0, a1 - a0), 0.03125)
         q_state(b + 1, a0, a1)
 
     def last_clocks(a0, a1):
-        o = 128 * R
+        o = 256 * R
         quant("sq", "ssc", o + a0, o + a1, V("sgf", 4 * a0, 4 * a1))
         bank = take()
         mm(bank, "gq", "gsc", 0, "sq", "ssc", o + a0, o + a1)
         scan(V("cs", a0, a1), V("p%d" % bank, 0, a1 - a0), V("c9", a0, a1), V("cs", a0 - 1, a0) if a0 else 0.0, ALU.add, ALU.add)
-        give(bank)
 
-    sent = [0] * R
     for c, (a0, a1) in enumerate(XC):
         q_state(0, a0, a1)
         if c == 0:
             send_first()
         signs(0, c, a0, a1)
+        if a0 < 4 * CFG["w1"][0] <= a1:
+            early_clocks(0)
     for b in range(R):
         held = exchange(b)
         for c in range(len(CH) + 1):
+            if c == len(CH) - 1:
+                x_chunk(b)
             if c < len(CH):
                 next_state(b, c, held)
             if c:
                 signs(b + 1, c - 1, *CH[c - 1])
                 if b == R - 1:
                     last_clocks(*CH[c - 1])
+                elif CH[c - 1][0] < 4 * CFG["w1"][b + 1] <= CH[c - 1][1]:
+                    early_clocks(b + 1)
     for c, (a0, a1) in enumerate(CH):
         v = V("aq", TC * R + a0, TC * R + a1)
         store("y", T.oc[:, 4 * a0:4 * a1], v[0].bitcast(dt.uint8), [v])
@@ -449,6 +488,7 @@ def rank_program(g, core, T, topo):
         store("y", T.y[:, a0:a1], v[0], [v])
     store("s", T.cl[:], T.cs[0:128:16, :], [V("cs", 0, 512)])
     op("y", None, outs, [])
+    ops[0]["marks"] = marks
     assert sorted(ORDER) == list(range(len(ops)))
     emit([ops[i] for i in ORDER], {"g": g, "v": vec, "s": act, "t": pe, "y": syn}, T)
-    g.wait_ge(T.sem.left, sum(sent))
+    g.wait_ge(T.sem.left, 5 * sum(NE) + 2 * NE[0])

from concourse.mybir import dt, AluOpType as ALU, ActivationFunctionType as ACT

TC, M, R = 512, 96, 3
CFG = {
    "ch": [0, 224, 384, 512],
    "hv": [[(0, 224), (224, 384)], [(0, 224)], [(0, 224)], []],
    "hs": [[], [(224, 384)], [(224, 384)], [(0, 224), (224, 384)]],
    "X": (384, 512),
    "dvo": [0, 2, 1, 3],
    "xc": [0, 256, 384, 512], "xq": "syy",
    "nv": 2,
    "vs": 12,
    "w1": [96, 56, 56],
    "oq": "yyss",
    "eng": "ssssssssvvsvsvvssvssssssvssssvsvvssssvvvssvsssvsssssvssssssvvvssvsvsvvssvsssssvsvssvssssvvvsss",
}
ORDER = [13,6,1,7,11,15,14,16,8,12,0,19,23,10,17,2,26,24,44,25,28,20,3,38,32,27,52,30,4,18,31,43,29,45,54,55,21,57,5,9,51,33,56,58,66,53,59,34,67,22,60,68,35,50,48,61,46,62,96,69,63,70,47,36,71,72,49,64,79,75,73,78,81,80,76,37,74,77,83,82,65,108,84,86,85,87,88,89,107,90,109,91,110,92,93,111,94,41,95,40,102,39,100,42,103,98,112,119,179,113,115,117,120,114,116,118,101,123,121,126,99,124,130,122,127,128,106,125,131,134,105,104,129,173,182,152,176,132,135,133,150,172,136,174,183,148,180,153,177,137,175,184,151,140,181,149,144,178,138,147,142,145,185,141,154,190,139,186,143,155,157,191,161,156,159,187,192,188,158,146,160,162,164,189,193,163,165,194,195,166,197,226,196,167,198,168,199,169,200,228,170,201,202,171,208,205,203,209,211,210,206,204,207,213,212,214,236,216,215,217,218,219,235,220,304,237,230,221,310,238,223,222,239,229,224,227,225,240,245,241,243,247,246,242,248,244,231,251,249,252,258,256,250,253,254,259,301,233,257,260,307,234,255,97,263,232,261,276,262,278,300,264,308,311,280,302,277,305,265,309,312,281,270,303,279,272,306,268,275,266,273,313,269,282,320,267,318,271,283,289,321,285,284,287,319,316,314,290,274,286,288,292,315,317,356,291,293,322,323,294,325,358,324,296,326,295,327,297,328,329,298,427,330,299,333,338,331,337,339,335,334,332,336,341,340,342,364,344,357,343,345,346,347,363,348,430,365,436,349,354,366,350,351,362,367,355,352,359,353,368,369,373,375,371,370,374,376,372,379,377,382,386,384,378,383,380,387,385,390,361,360,381,391,389,404,388,408,426,392,428,437,406,431,405,433,434,393,429,438,403,396,432,398,409,435,400,407,394,397,439,399,410,444,401,446,395,415,411,445,413,416,417,402,440,442,412,414,418,420,441,447,443,421,419,448,449,463,423,455,468,465,450,422,461,424,456,452,466,451,462,425,453,457,464,458,454,467,470,459,469,460,471,472]
BANKS = [0,1,3,4,2,5,6,7,2,1,0,5,1,0,4,5,7,6,2,7,4,0,5,6,7,0,1,7,0,2,6,3,4,3,4,1,2,5,3,2,1,5,6,4,7,5,7,1,2,4,5,1,0,2,4,5,7,5,2,3,1,0,2,6,3,2,0,4,0,6,1,6,3,4,1,3,4,7,5,3,7,1,5,7,4,3,2,5,3,6,7,5,4,3,0,5,6,0,4,2,6,2,0,1,4,3,7,6]
CW = 128
CQ, CS = CW + M, CW + 4 * M
AS = 128 + TC
F8, U8, BF, F32, I32, U16 = "float8_e4m3fn_x4", "uint8", "bfloat16", "float32", "int32", "uint16"


def _sb(n, d):
    return ("sbuf", [128, n], d)


SCRATCH = {
    "t0": _sb(2048, BF), "t1": _sb(2048, BF), "t2": _sb(2048, BF), "t3": _sb(2048, BF),
    "aq": _sb(4 * TC, F8), "asc": _sb(4 * AS, U8),
    "ut": _sb(512, BF), "uq": _sb(128, F8), "usc": _sb(128, U8),
    "wq": _sb(512, F8), "wsc": _sb(512, U8),
    "ht": _sb(2048, BF), "hq": _sb(R * (TC + 128), F8), "hsc": _sb(R * (TC + 128), U8),
    "da": _sb(2048, BF), "dg": _sb(2048, BF), "dv": _sb(384, BF), "vt": _sb(1648, BF),
    "vq": _sb(R * 128, F8),
    "sgf": _sb(2048, BF), "sq": _sb(R * 256 + TC, F8), "ssc": _sb(R * 256 + TC, U8),
    "cq": _sb(R * CQ, F8), "csc": _sb(R * CS, U8),
    "eb": _sb(528, BF), "eq": _sb(512, F8), "esc": _sb(512, U8),
    "nv": _sb(128, BF), "nq": _sb(128, BF), "w4": _sb(128, F32), "dq": _sb(512, BF),
    "gt": _sb(1536, BF), "gq": _sb(512, F8), "gsc": _sb(512, U8),
    "bq": _sb(R * 128, F8), "bsc": _sb(R * 128, U8),
    "pi": _sb(4, I32), "rf": _sb(8, F32), "col": _sb(8, F32), "tiny": _sb(4, F32),
    "iw": _sb(128, F32), "c9": _sb(512, F32),
    "k6": _sb(8, F32), "r6": _sb(8, F32), "w6": _sb(8, F32), "k96": _sb(96, F32), "m2": _sb(128, F32),
    "cw": _sb(128, F32), "ew": _sb(128, F32), "ed": _sb(128, F32), "th96": _sb(96, F32),
    "junk": _sb(192, F32), "acc": _sb(200, F32), "ob": _sb(2, U16), "mq32": _sb(32, F32),
    "lp": _sb(8 * R, U16), "lo": _sb(32, U16), "xt": _sb(512, BF), "xq": _sb(R * 128, F8), "xs": _sb(R * 128, U8),
    "xl": _sb(R * 128, F8), "xls": _sb(R * 128, U8),
    "o2": _sb(8, U16), "ov": _sb(24, U16), "op": _sb(32 * R, U16),
    "sm": _sb(8, F32), "x4": _sb(32, F32),
    "ys": _sb(512, F32), "cs": _sb(512, F32),
}
for _b in range(8):
    SCRATCH["p%d" % _b] = ("psum", [128, 512], F32)

NC, ND = 110, 24
SEMAPHORES = (["arr0", "arr1", "arr2", "lst0", "lst1", "lst2", "xar0", "xar1", "xar2", "left"]
              + ["c%d" % _i for _i in range(NC)] + ["d%d" % _i for _i in range(ND)])


def is_bank(k):
    return k[0] == "p" and k[1:].isdigit()


def meets(o, p):
    for (k, m) in o["r"]:
        if p["W"].get(k, 0) & m or (k in p["R"] and p["e"] != o["e"] and is_bank(k)):
            return True
    for (k, m) in o["w"]:
        if o.get("adds") and p["e"] == "t":
            continue
        if (p["W"].get(k, 0) | p["R"].get(k, 0)) & m:
            return True
    return False


def emit(ops, queues, T):
    known = {e: 0 for e in queues}
    for i, o in enumerate(ops):
        o["by"] = []
        if o["e"] == "x":
            o["done"] = 1 << i
            continue
        o["waits"] = []
        for j in range(i - 1, -1, -1):
            if known[o["e"]] >> j & 1:
                continue
            p = ops[j]
            if meets(o, p):
                o["waits"].append(j)
                p["by"].append(i)
                known[o["e"]] |= p["done"]
        o["seen"] = known[o["e"]]
        o["done"] = known[o["e"]] | 1 << i
    groups = {}
    for i, o in enumerate(ops):
        if o["by"] and o["e"] != "x":
            groups.setdefault((o["dma"], tuple(o["by"])), []).append(i)
    pools = {"c": [], "d": []}
    for i, o in enumerate(ops):
        if o["e"] == "x":
            continue
        q = queues[o["e"]]
        for sem in sorted(set(ops[j]["sem"] for j in o["waits"])):
            q.wait_ge(T.sem[sem[0]], sem[1])
        if o["f"] is None:
            continue
        ins = o["f"]()
        if o["by"]:
            kind = "d" if o["dma"] else "c"
            step = 16 if o["dma"] else 1
            if "sem" not in o:
                members = groups[(o["dma"], tuple(o["by"]))]
                mask = sum(1 << j for j in members)
                pool = pools[kind]
                free = [s for s in range(len(pool)) if all(ops[j]["seen"] & pool[s][0] == pool[s][0] for j in members)]
                s = free[0] if free else len(pool)
                if not free:
                    pool.append((0, 0))
                pool[s] = (mask, pool[s][1] + step * len(members))
                for j in members:
                    ops[j]["sem"] = ("%s%d" % (kind, s), pool[s][1])
            ins.then_inc(T.sem[o["sem"][0]], step)


def rank_program(g, core, T, topo):
    rank = T.rank_of(core)
    if rank is None:
        return
    ops = []
    vec, act, pe, syn = g.vector, g.scalar, g.tensor, g.sync

    def V(name, a, b, s=1):
        m = 0
        if is_bank(name):
            m = 1
        elif s == 1:
            m = ((1 << (b - a)) - 1) << a
        else:
            for c in range(a, b, s):
                m |= 1 << c
        return (T[name][:, a:b] if s == 1 else T[name][:, a:b:s], [(name, m)])

    def IND(win, off):
        return (win[0].indirect(off[0]), win[1] + off[1])

    def op(e, f, r, w, dma=False, sem=None):
        rr = [a for v in r for a in v[1]]
        ww = [a for v in w for a in v[1]]
        o = {"e": e, "f": f, "r": rr, "w": ww, "R": {}, "W": {}, "dma": dma}
        for (k, m) in rr:
            o["R"][k] = o["R"].get(k, 0) | m
        for (k, m) in ww:
            o["W"][k] = o["W"].get(k, 0) | m
        if sem:
            o["sem"] = sem
        ops.append(o)

    def isv(a):
        return isinstance(a, tuple)

    def ap(a):
        return a[0] if isv(a) else a

    def ts(out, in0, s1, s2, o0, o1=None):
        r = [in0] + [a for a in (s1, s2) if isv(a)]
        if o1 is None:
            op("v", lambda: vec.tensor_scalar(out[0], in0[0], ap(s1), None, o0), r, [out])
        else:
            op("v", lambda: vec.tensor_scalar(out[0], in0[0], ap(s1), ap(s2), o0, o1), r, [out])

    def tt(out, a, b, o):
        op("v", lambda: vec.tensor_tensor(out[0], a[0], b[0], o), [a, b], [out])

    def cp(out, a):
        op("v", lambda: vec.tensor_copy(out[0], a[0]), [a], [out])

    def ms(out, c):
        op("v", lambda: vec.memset(out[0], c), [], [out])

    def rcp(out, a):
        op("v", lambda: vec.reciprocal(out[0], a[0]), [a], [out])

    def scan(out, d0, d1, init, o0, o1):
        op("v", lambda: vec.tensor_tensor_scan(out[0], d0[0], d1[0], ap(init), o0, o1),
           [d0, d1] + ([init] if isv(init) else []), [out])

    def quant(q, s, a, b, src, d=0):
        vq, vs = V(q, a, b), V(s, a + d, b + d)
        op("v", lambda: vec.quantize_mx(vq[0], vs[0], src[0]), [src], [vq, vs])

    def A(out, a, func, bias=0.0, scale=1.0, acc=None):
        r = [a] + [c for c in (bias, scale) if isv(c)]
        if acc is None:
            op("s", lambda: act.activation(out[0], a[0], func, bias=ap(bias), scale=ap(scale)), r, [out])
        else:
            op("s", lambda: act.activation(out[0], a[0], func, bias=ap(bias), scale=ap(scale), accum_out=acc[0]), r, [out, acc])

    def mm(bank, lq, ls, l0, rq, rs, a, b, d=0, start=True, stop=True):
        out = V("p%d" % bank, 0, b - a)
        w, ws_, x, xs = V(lq, l0, l0 + 128), V(ls, l0, l0 + 128), V(rq, a, b), V(rs, a + d, b + d)
        op("t", lambda: pe.matmul_mx(out[0], w[0], ws_[0], x[0], xs[0], start, stop), [w, ws_, x, xs], [out])
        ops[-1]["adds"] = not start

    def iota(out, pat, base, cm, flt=True):
        if flt:
            op("g", lambda: g.iota(out[0], pat, base, cm, allow_small_or_imprecise_dtypes=True), [], [out])
        else:
            op("g", lambda: g.iota(out[0], pat, base, cm), [], [out])

    def dma(e, out, a, r, w):
        q = syn if e == "y" else act
        op(e, lambda: q.dma_start(out, a), r, w, dma=True)

    outs = []
    marks = []

    def store(e, out, a, r):
        tag = (None, [("out%d" % len(outs), 1)])
        outs.append(tag)
        dma(e, out, a, r, [tag])

    def who():
        marks.append((len(ops), CFG["eng"][len(marks)]))
        return marks[-1][1]

    def move(out, a, scale):
        if who() == "s":
            A(out, a, ACT.Copy, scale=scale)
        elif scale == 1.0:
            cp(out, a)
        else:
            ts(out, a, scale, None, ALU.mult)

    def affine(out, a, scale, bias):
        if who() == "s":
            A(out, a, ACT.Identity, bias=bias, scale=scale)
        else:
            ts(out, a, scale, bias, ALU.mult, ALU.add)

    taken = [0]

    def take():
        taken[0] += 1
        return taken[0] - 1 if CFG.get("virt") else BANKS[taken[0] - 1]

    def pieces(edges):
        return list(zip(edges[:-1], edges[1:]))

    XC, CH, X = pieces(CFG["xc"]), pieces(CFG["ch"]), CFG["X"]
    dma("y", T.ut[:], T.u[:], [], [V("ut", 0, 512)])
    for c, (a, b) in enumerate(XC):
        v = V("t0", 4 * a, 4 * b)
        dma(CFG["xq"][c], v[0], T.x[:, 4 * a:4 * b], [], [v])
    somex = V("t0", 4 * XC[0][0], 4 * XC[0][1])
    dma("y", T.wq[:].bitcast(dt.uint8), T.wc[:], [somex], [V("wq", 0, 512)])
    dma("y", T.wsc[:], T.ws[:], [somex], [V("wsc", 0, 512)])

    NV = CFG["nv"]
    AC, C36 = 64, 70
    CM, BT, ZR, SG = 384, 480, 608, 1136
    pcol, gcol, tcol, rcol, q4col = V("rf", 0, 1), V("rf", 1, 2), V("rf", 2, 3), V("rf", 3, 4), V("rf", 5, 6)
    cthr, ca4, cov, g4col, g4t = V("col", 0, 1), V("col", 1, 2), V("col", 2, 3), V("col", 3, 4), V("col", 4, 5)
    tiny = V("tiny", 0, 1)
    iota(V("pi", 0, 1), [[0, 1]], 0, 1, False)
    iota(V("nv", 0, 128), [[16, 8], [0, 4], [1, 4]], 0, 0)
    iota(V("iw", 0, 128), [[1, 128]], 0, 0)
    iota(V("w4", 0, 128), [[0, 32], [4, 4]], 0, 0)
    iota(V("dq", 0, 512), [[1, 32], [0, 4], [-1, 4]], 0, 0)
    ms(tiny, -2.0 ** -120)
    ms(V("vt", BT, SG), 0.0)
    ms(V("acc", C36, C36 + 128), 36.0)
    ts(V("pi", 1, 2), V("pi", 0, 1), 112, None, ALU.bitwise_and)
    ts(V("pi", 2, 3), V("pi", 0, 1), 3, None, ALU.bitwise_and)
    cp(V("rf", 0, 3), V("pi", 0, 3))
    A(rcol, gcol, ACT.Identity, bias=pcol, scale=-1.0)
    A(q4col, tcol, ACT.Identity, bias=rcol, scale=-1.0)
    A(V("nq", 0, 128), V("nv", 0, 128), ACT.Abs, bias=gcol, scale=-1.0)
    A(cthr, tcol, ACT.Identity, bias=36.0 + 0.5 / M, scale=-9.0)
    A(ca4, tcol, ACT.Identity, bias=2.0 - 144.0 * M, scale=36.0 * M)
    A(cov, tcol, ACT.Identity, bias=1020.0)
    A(g4col, gcol, ACT.Copy, scale=0.25)
    A(g4t, gcol, ACT.Identity, bias=tcol, scale=0.25)
    for s in (3, 2, 1, 0):
        ts(V("gt", 512 + s, 1024, 4), V("nq", 0, 128), float(s), 0.5, ALU.is_le, ALU.mult)
    for s in range(4):
        move(V("gt", s, 512, 4), V("gt", 515, 1024, 4), 1.0)
    quant("gq", "gsc", 0, 256, V("gt", 0, 1024))
    ts(V("gt", 1024, 1536), V("dq", 0, 512), g4col, 0.5, ALU.is_equal, ALU.mult)
    ts(V("gt", 512, 1024, 4), V("dq", 0, 512, 4), g4t, 4.0, ALU.is_equal, ALU.mult)
    quant("gq", "gsc", 256, 512, V("gt", 512, 1536))
    eb, zr = V("eb", 0, 528), V("vt", ZR, SG)
    op("g", lambda: g.affine_select(eb[0], zr[0], [[-1, 528]], ALU.not_equal, 0.5, 3, 4), [zr], [eb])
    ts(V("k6", 0, 6), V("iw", 0, 96, 16), rcol, 1.0e-4, ALU.add, ALU.max)
    for e in range(4):
        quant("eq", "esc", 128 * e, 128 * e + 128, V("eb", 3 - e, 515 - e))
    quant("uq", "usc", 0, 128, V("ut", 0, 512))
    A(V("k96", 0, 96), V("iw", 0, 96), ACT.Copy, scale=1.0 / M)
    rcp(V("r6", 0, 6), V("k6", 0, 6))
    A(V("junk", 0, 128), V("w4", 0, 128), ACT.Abs, bias=q4col, scale=-1.0)
    A(V("m2", 0, 128), V("junk", 0, 128), ACT.Relu, bias=2.0 ** 18, scale=-2.0 ** 18)
    ts(V("ob", 0, 2), V("iw", 0, 32, 16), q4col, 0.25, ALU.add, ALU.mult)
    A(V("mq32", 0, 32), V("m2", 0, 32), ACT.Copy, scale=2.0 ** -18)
    A(V("w6", 0, NV), V("r6", 0, NV), ACT.Copy, scale=M * (1.0 - 5.0e-7))
    A(V("w6", NV, 6), V("r6", NV, 6), ACT.Copy, scale=-M * (1.0 - 5.0e-7))

    def q_state(b, a0, a1):
        quant("aq", "asc", TC * b + a0, TC * b + a1, V("t%d" % b, 4 * a0, 4 * a1), 128 * (b + 1))

    def a_mm(b, bank, lq, ls, l0, a0, a1):
        mm(bank, lq, ls, l0, "aq", "asc", TC * b + a0, TC * b + a1, 128 * (b + 1))

    def signs(b, c, a0, a1):
        bank = take()
        a_mm(b, bank, "uq", "usc", 0, a0, a1)
        z = V("p%d" % bank, 0, a1 - a0)
        A(V("sgf", 4 * a0, 4 * a1, 4) if b == R else V("vt", SG + a0, SG + a1), z, ACT.Sign, bias=tiny)
        if b == R:
            move(V("ys", a0, a1), z, 1.0)

    def partner(b):
        return T.cores[rank ^ (1 << (b % 2))]

    def write(b, land, src, sem="arr"):
        rid, pid, _ = topo.addr(partner(b))
        return g.remote_dma(land, src, T.sem[sem + str(b)], T.sem.left, pid, rid, topo.mask(core, partner(b)))

    NE = [len(topo.engines(core, partner(b))) for b in range(R)]

    def send_first():
        sq_, ss_, lq, ls = V("aq", 0, 1), V("asc", 128, 129), V("cq", CW, CW + 1), V("csc", CW, CW + 1)
        op("g", lambda: write(0, lq[0].bitcast(dt.uint8), sq_[0].bitcast(dt.uint8)), [sq_], [])
        op("g", lambda: write(0, ls[0], ss_[0]), [ss_], [])

    def x_chunk(b):
        op("x", None, [], [V("xl", 128 * b, 128 * b + 128), V("xls", 128 * b, 128 * b + 128)], sem=("xar%d" % b, 2 * NE[b]))
        for e in range(4):
            bank = take()
            mm(bank, "eq", "esc", 128 * e, "aq", "asc", TC * b + X[0], TC * b + X[1], 128 * (b + 1), True, False)
            mm(bank, "eq", "esc", 128 * e, "xl", "xls", 128 * b, 128 * b + 128, 0, False, True)
            move(V("ht", 4 * X[0] + e, 4 * X[1], 4), V("p%d" % bank, 0, 128), 1.0)

    def span(e, k):
        mine = CFG["h" + k][e]
        return (mine[0][0], mine[-1][1]) if mine else None

    def clock_part(b, w0, w1):
        o = 256 * b + (128 if w0 else 0)
        quant("sq", "ssc", o, o + 128, V("vt", SG + 4 * w1 - 512, SG + 4 * w1))
        b2, b3 = take(), take()
        mm(b2, "gq", "gsc", 0, "sq", "ssc", o, o + 128)
        mm(b3, "gq", "gsc", 128, "sq", "ssc", o, o + 128)
        n = w1 - w0
        scan(V("cw", w0, w1), V("p%d" % b2, 128 - n, 128), V("acc", C36, C36 + n), V("cw", w0 - 1, w0) if w0 else 0.0, ALU.add, ALU.add)
        return b3

    def early_clocks(b):
        w1 = CFG["w1"][b]
        b3 = clock_part(b, 0, w1)
        tt(V("ew", 0, w1), V("cw", 0, w1), V("p%d" % b3, 128 - w1, 128), ALU.subtract)
        scan(V("ed", 0, w1), V("m2", 0, w1), V("ew", 0, w1), 0.0, ALU.max, ALU.min)

    def exchange(b):
        S = V("cw", 127, 128)
        w1 = CFG["w1"][b]
        b3 = clock_part(b, w1, 128)
        for m in range(NV):
            j = V("junk", 32 * m, 32 * m + 32)
            ts(j, V("cw", 3, 128, 4), V("w6", m, m + 1), S, ALU.mult, ALU.is_lt)
            scan(V("acc", AC + m - 31 * NV, AC + m + 1, NV), j, j, -32.0, ALU.add, ALU.add)
        for m in range(NV, 6):
            A(V("junk", 32 * m, 32 * m + 32), V("cw", 3, 128, 4), ACT.Sign, bias=S, scale=V("w6", m, m + 1), acc=V("acc", AC + m, AC + m + 1))
        tt(V("ew", w1, 128), V("cw", w1, 128), V("p%d" % b3, w1, 128), ALU.subtract)
        A(V("th96", 0, 96), V("k96", 0, 96), ACT.Identity, bias=cthr, scale=S)
        scan(V("ed", w1, 128), V("m2", w1, 128), V("ew", w1, 128), 0.0, ALU.max, ALU.min)
        ts(V("o2", 0, 6), V("acc", AC, AC + 6), 2.0, 67.0, ALU.mult, ALU.add)
        tt(V("vt", CM, CM + M), IND(V("ed", 0, 128), V("o2", 0, 6)), V("th96", 0, 96), ALU.is_le)
        tt(V("vt", BT, BT + 128, 4), IND(V("acc", AC, AC + 8), V("ob", 0, 2)), V("mq32", 0, 32), ALU.mult)
        quant("bq", "bsc", 128 * b, 128 * b + 128, V("vt", BT, BT + 512))
        dc = (CS - CQ) * b
        quant("cq", "csc", CQ * b, CQ * b + CW, V("vt", CM, CM + 512), dc)
        b0 = take()
        mm(b0, "gq", "gsc", 256, "bq", "bsc", 128 * b, 128 * b + 128, 0, True, False)
        mm(b0, "gq", "gsc", 384, "cq", "csc", CQ * b, CQ * b + 128, dc, False, True)
        ts(V("ov", 0, 24), V("p%d" % b0, 0, 24), 8.0, cov, ALU.mult, ALU.add)
        st, vs = V("t%d" % b, 0, 2048), CFG["vs"]
        cp(V("vt", 0, 16 * vs), IND(st, V("ov", 0, vs)))
        A(V("vt", 16 * vs, 384), IND(st, V("ov", vs, 24)), ACT.Copy)
        quant("vq", "asc", 128 * b, 128 * b + 128, V("vt", 0, 512), TC * b)
        f = 1 if b == 0 else 0
        sq_, ss_ = V("vq", 128 * b + f, 128 * b + M), V("asc", AS * b + f, AS * b + M)
        lq, ls = V("cq", CQ * b + CW + f, CQ * (b + 1)), V("csc", CS * b + CW + f, CS * b + CW + M)
        op("g", lambda: [write(b, lq[0].bitcast(dt.uint8), sq_[0].bitcast(dt.uint8)), write(b, ls[0], ss_[0])], [sq_, ss_], [])
        if b == 0:
            iota(V("c9", 0, 512), [[0, 512]], 9, 0)
            iota(V("sgf", 0, 2048), [[0, 2048]], 0, 0)
        for e in range(4):
            sp = span(e, "v")
            if sp:
                bank = take()
                a_mm(b, bank, "eq", "esc", 128 * e, sp[0], sp[1])
                move(V("da", TC * e + sp[0], TC * e + sp[1]), V("p%d" % bank, 0, sp[1] - sp[0]), 1.0)
        held = {}
        for e in range(4):
            sp = span(e, "s")
            if sp:
                held[e] = (take(), sp[0], sp[1])
                a_mm(b, held[e][0], "eq", "esc", 128 * e, sp[0], sp[1])
        rcp(V("sm", 0, 1), S)
        affine(V("sm", 1, 2), S, -2.0, ca4)
        affine(V("x4", 0, 32), V("ed", 3, 128, 4), 4.0 * M, V("sm", 1, 2))
        ts(V("op", 32 * b, 32 * b + 32), V("x4", 0, 32), V("sm", 0, 1), 0.25, ALU.mult, ALU.mult)
        mine, lp = V("op", 32 * b + X[0] // 16, 32 * b + X[1] // 16), V("lp", 8 * b, 8 * b + 8)
        op("g", lambda: write(b, lp[0], mine[0], "lst"), [mine], [])
        op("x", None, [], [lp], sem=("lst%d" % b, NE[b]))
        for e in range(4):
            ts(V("lo", 8 * e, 8 * e + 8), lp, 4.0, float(e), ALU.mult, ALU.add)
            move(V("xt", e, 512, 4), IND(V("vt", 0, 384), V("lo", 8 * e, 8 * e + 8)), 1.0)
        quant("xq", "xs", 128 * b, 128 * b + 128, V("xt", 0, 512))
        xq, xs, xl, xls = [V(k, 128 * b, 128 * b + 128) for k in ("xq", "xs", "xl", "xls")]
        op("g", lambda: [write(b, xl[0].bitcast(dt.uint8), xq[0].bitcast(dt.uint8), "xar"), write(b, xls[0], xs[0], "xar")], [xq, xs], [])
        op("x", None, [], [V("cq", CQ * b + CW, CQ * (b + 1)), V("csc", CS * b + CW, CS * (b + 1))], sem=("arr%d" % b, (2 + 2 * f) * NE[b]))
        for e in CFG["dvo"]:
            bank = take()
            mm(bank, "eq", "esc", 128 * e, "cq", "csc", CQ * (b + 1) - 128, CQ * (b + 1), dc)
            move(V("dv", M * e, M * (e + 1)), V("p%d" % bank, 128 - M, 128), 1.0)
        return held

    def next_state(b, c, held):
        a0, a1 = CH[c]
        for e in range(4):
            win = V("dv", M * e, M * (e + 1))
            for (x0, x1) in CFG["hv"][e]:
                if a0 <= x0 < a1:
                    tt(V("ht", 4 * x0 + e, 4 * x1, 4), IND(win, V("op", 32 * b + x0 // 16, 32 * b + x1 // 16)), V("da", TC * e + x0, TC * e + x1), ALU.add)
            for (x0, x1) in CFG["hs"][e]:
                if a0 <= x0 < a1:
                    A(V("dg", TC * e + x0, TC * e + x1), IND(win, V("op", 32 * b + x0 // 16, 32 * b + x1 // 16)), ACT.Copy)
            sp = span(e, "s")
            if sp and max(a0, sp[0]) < min(a1, sp[1]):
                bank, s0, s1 = held[e]
                x0, x1 = max(a0, s0), min(a1, s1)
                tt(V("ht", 4 * x0 + e, 4 * x1, 4), V("p%d" % bank, x0 - s0, x1 - s0), V("dg", TC * e + x0, TC * e + x1), ALU.add)
        o = (TC + 128) * b + a0
        quant("hq", "hsc", o, o + a1 - a0, V("ht", 4 * a0, 4 * a1))
        for i in range(4):
            bank = take()
            mm(bank, "wq", "wsc", 128 * i, "hq", "hsc", o, o + a1 - a0)
            move(V("t%d" % (b + 1), 4 * a0 + i, 4 * a1, 4), V("p%d" % bank, 0, a1 - a0), 0.03125)
        q_state(b + 1, a0, a1)

    def last_clocks(a0, a1):
        o = 256 * R
        quant("sq", "ssc", o + a0, o + a1, V("sgf", 4 * a0, 4 * a1))
        bank = take()
        mm(bank, "gq", "gsc", 0, "sq", "ssc", o + a0, o + a1)
        scan(V("cs", a0, a1), V("p%d" % bank, 0, a1 - a0), V("c9", a0, a1), V("cs", a0 - 1, a0) if a0 else 0.0, ALU.add, ALU.add)

    for c, (a0, a1) in enumerate(XC):
        q_state(0, a0, a1)
        if c == 0:
            send_first()
        signs(0, c, a0, a1)
        if a0 < 4 * CFG["w1"][0] <= a1:
            early_clocks(0)
    for b in range(R):
        held = exchange(b)
        for c in range(len(CH) + 1):
            if c == len(CH) - 1:
                x_chunk(b)
            if c < len(CH):
                next_state(b, c, held)
            if c:
                signs(b + 1, c - 1, *CH[c - 1])
                if b == R - 1:
                    last_clocks(*CH[c - 1])
                elif CH[c - 1][0] < 4 * CFG["w1"][b + 1] <= CH[c - 1][1]:
                    early_clocks(b + 1)
    for c, (a0, a1) in enumerate(CH):
        v = V("aq", TC * R + a0, TC * R + a1)
        store("y", T.oc[:, 4 * a0:4 * a1], v[0].bitcast(dt.uint8), [v])
        if c == len(CH) - 1:
            o = AS * R + 128
            for k in range(4):
                store(CFG["oq"][k], T.osc[4 * k:4 * k + 4, :], T.asc[32 * k:32 * k + 4, o:o + TC], [V("asc", o, o + TC)])
        v = V("ys", a0, a1)
        store("y", T.y[:, a0:a1], v[0], [v])
    store("s", T.cl[:], T.cs[0:128:16, :], [V("cs", 0, 512)])
    op("y", None, outs, [])
    ops[0]["marks"] = marks
    assert sorted(ORDER) == list(range(len(ops)))
    emit([ops[i] for i in ORDER], {"g": g, "v": vec, "s": act, "t": pe, "y": syn}, T)
    g.wait_ge(T.sem.left, 5 * sum(NE) + 2 * NE[0])
